import numpy as np, ml_dtypes
CORES = [10,34,74,98]
N = 4
BF = ml_dtypes.bfloat16
def f(rng, *shape):
    return (rng.standard_normal(shape, dtype=np.float32) * np.exp2(rng.integers(-2, 3, shape[:-1] + (1,)))).astype(BF)
def wide(rng, *shape):
    v = f(rng, *shape).astype(np.float32); k = shape[:-2] + (1, shape[-1])
    return (v * np.exp2(rng.integers(-6, 7, k)) * (rng.random(k) > 0.0625)).astype(BF)
W, V, L, DM, ST = 4096, 1024, 256, 3, 6
def hotty(rng, hot, n, share):
    h = hot[np.arange(8)[None, :, None, None], rng.integers(0, hot.shape[1], (N, 8, 16, n))]
    return np.where(rng.random((N, 8, 16, n)) < share, h, rng.integers(0, W, (N, 8, 16, n)))
def parts(rng):
    hot = rng.integers(0, W, (8, W // 16)); share = rng.choice(np.array([0.25, 0.5, 0.75]), (N, 8, 1, 1))
    refs = hotty(rng, hot, V, share); gloss = hotty(rng, hot, W, share)
    u = rng.random((N, ST, L))
    need = np.where(u < 0.4, rng.integers(1, 45, u.shape), np.where(u < 0.9, rng.integers(58, 71, u.shape), rng.integers(90, 129, u.shape)))
    v = rng.integers(0, V, (N, 8, L)); p = rng.integers(0, V, (N, DM, 8, L)); a = rng.integers(0, 16, (N, DM, 8, L)); d = rng.integers(0, DM + 1, (N, L))
    return refs, gloss, f(rng, N, 128, W), f(rng, N, 128, L), need, v, p, a, d
def pack(refs, gloss, facts, cases, need, v, p, a, d):
    i = lambda x: np.ascontiguousarray(x).astype(np.int32)
    return {"refs": i(refs.reshape(N, 128, V)), "gloss": i(gloss.reshape(N, 128, W)), "facts": np.ascontiguousarray(facts).astype(BF), "cases": np.ascontiguousarray(cases).astype(BF), "need": i(need),
            "vp0": i(np.concatenate([v, p.reshape(N, 8 * DM, L)], axis=1)), "act0": i(a.reshape(N, 8 * DM, L)), "dep0": i(d.reshape(N, 1, L))}
def setup_inputs(rng):
    return pack(*parts(rng))
def skew(rng, n):
    e = rng.choice(np.array([1.0, 2.0, 4.0]), (N, 8, 16, 1)); x = np.minimum((W * rng.random((N, 8, 16, n)) ** e).astype(np.int64), W - 1)
    return np.where(rng.random((N, 8, 1, 1)) < 0.5, W - 1 - x, x)
def setup_inputs_spread(rng):
    refs, gloss, facts, cases, need, v, p, a, d = parts(rng)
    need = np.where(rng.random(need.shape) < 0.3, rng.integers(1, 129, need.shape), need)
    far = np.exp2(40.0 * (rng.permutation(128)[None, :, None] % 3 - 1)).astype(np.float32)
    return pack(skew(rng, V), skew(rng, W), wide(rng, N, 128, W).astype(np.float32) * far, wide(rng, N, 128, L).astype(np.float32) * far, need, v, p, a, d)
def tips(rng, x, top, share):
    return np.where(rng.random(x.shape) < share, top * rng.integers(0, 2, x.shape), x)
def setup_inputs_ends(rng):
    refs, gloss, facts, cases, need, v, p, a, d = parts(rng)
    al = rng.random((N, 1, L)) < 0.5; al[:, :, 0] = True; al[:, :, L - 1] = True
    bit = np.where(rng.random((N, 1, 16, V)) < 0.7, rng.integers(0, 2, (N, 1, 16, V)), rng.integers(0, 2, (N, 8, 16, V)))
    refs = np.where(rng.random(refs.shape) < 0.9, (W - 1) * bit, refs)
    refs[..., 0] = (W - 1) * (np.arange(16) & 1); refs[..., V - 1] = (W - 1) * (np.arange(16) == 15)
    gloss = tips(rng, gloss, W - 1, 0.85)
    for c in (0, W - 1): gloss[..., c] = (W - 1) * rng.integers(0, 2, (N, 8, 16))
    gloss[:, :, 0, 0] = 0; gloss[:, :, 0, W - 1] = W - 1; gloss[:, :, 15, 0] = W - 1; gloss[:, :, 15, W - 1] = 0
    v = (V - 1) * np.where(al, rng.integers(0, 2, (N, 1, L)), rng.integers(0, 2, (N, 8, L)))
    p = tips(rng, p, V - 1, 0.9); a = np.where(al[:, None], 15 * rng.integers(0, 2, (N, DM, 1, L)), tips(rng, a, 15, 0.9))
    d = tips(rng, d, DM, 0.8); d[:, 0] = DM; d[:, L - 1] = DM
    need = np.where(rng.random(need.shape) < 0.8, np.where(rng.random(need.shape) < 0.5, 1, 128), rng.integers(40, 90, need.shape))
    need[:, 0, 0] = 128; need[:, 0, L - 1] = 128
    facts[:, :, 0] = -64; facts[:, :, W - 1] = 64
    u = rng.random((N, 1, L)); u[:, :, 0] = 0.1; u[:, :, L - 1] = 0.1
    z = np.where(u < 0.25, np.float32(-64), cases.astype(np.float32)); one = rng.integers(0, 128, (N, 1, L)) == np.arange(128)[None, :, None]
    z = np.where(one & (u > 0.6) & (u < 0.8), np.float32(-128), np.where(one & (u >= 0.8), np.float32(128), z))
    return pack(refs, gloss, facts, z, need, v, p, a, d)
def setup_inputs_corners(rng):
    refs, gloss, facts, cases, need, v, p, a, d = parts(rng)
    facts = rng.integers(-3, 4, (N, 128, W)).astype(np.float32); z = rng.integers(-3, 4, (N, 128, L)).astype(np.float32)
    k = rng.integers(0, 6, (N, L)); k[:, :6] = np.arange(6); k[:, L - 6:] = np.arange(6)[::-1]
    cnt = np.where(k == 0, 128, np.where(k == 1, 0, np.where(k == 2, 64, rng.choice(np.array([1, 127]), (N, L)))))
    order = np.argsort(rng.random((N, 128, L)), axis=1)
    z = np.where((k < 4)[:, None, :], np.where(order < cnt[:, None, :], 1024.0, -1024.0), z)
    other = (np.arange(128)[None, :, None] >> 4) != rng.integers(0, 8, (N, 1, L))
    z = np.where((k == 5)[:, None, :] & other, 1024.0, z)
    kk = k[:, None, :]; s = need.shape
    need = np.where(kk < 2, np.where(rng.random(s) < 0.5, 1, 128), np.where(kk < 4, cnt[:, None, :] + rng.integers(0, 2, s), np.where(kk == 4, rng.integers(62, 84, s), rng.integers(118, 125, s))))
    ve = np.array([0, 1, V - 2, V - 1])
    v = np.where(rng.random(v.shape) < 0.7, rng.choice(ve, v.shape), v); p = np.where(rng.random(p.shape) < 0.7, rng.choice(ve, p.shape), p)
    a = np.where(rng.random(a.shape) < 0.7, rng.choice(np.array([0, 1, 14, 15]), a.shape), a)
    return pack(refs, gloss, facts, z, need, v, p, a, d)
def setup_inputs_crowd(rng):
    refs, gloss, facts, cases, need, v, p, a, d = parts(rng)
    a = rng.integers(8, 16, a.shape); a[:, 0] = rng.integers(1, 8, (N, 8, L))
    cases[:, :48] = 2048; cases[:, 48:96] = -2048; cases[:, 96:100] = 512
    for g in range(8):
        s = 1 + rng.permutation(W - 2)[:4]
        if g < 4:
            if g < 2: s[1] = (W - 1) * (1 - g)
            gloss[:, g, 8:, s[0]] = s[1]; gloss[:, g, 8:, s[1]] = s[1]; refs[:, g, 0] = s[0]
            if g >= 2:
                gloss[:, g, 8:, s[2]] = s[3]; gloss[:, g, 8:, s[3]] = s[3]
                w = int(rng.integers(0, V)); refs[:, g, 0, w] = s[2]
                v[:, g] = np.where(v[:, g] == w, (w + 1) % V, v[:, g]); v[np.arange(N), g, rng.integers(0, L, N)] = w
        elif g == 4:
            for c in s: gloss[:, g, 8:, c] = c
            refs[:, g] = s[rng.integers(0, 4, (N, 16, V))]
        elif g == 5:
            o = rng.permutation(W); own = o[:N * L]; rest = o[N * L:]; gg = gloss[:, g]
            gg[:, 8:, own] = own; gg[:, 8:, rest] = rest[rng.integers(0, W - N * L, (N, 8, W - N * L))]
            gg[:, 1:8, own] = 2 * (gg[:, 1:8, own] // 2); gg[:, 1:8, rest] = 2 * (gg[:, 1:8, rest] // 2) + 1
            refs[:, g, 0] = own.reshape(N, L)[:, np.arange(V) % L]; refs[:, g, 1:] = rest[rng.integers(0, W - N * L, (N, 15, V))]
            v[:, g] = np.argsort(rng.random((N, L)), axis=1) + L * rng.integers(0, V // L, (N, L))
            a[:, 0, g] = np.minimum(a[:, 0, g], 6); a[:, 0, g, L - 1] = 7
        else:
            gloss[:, g, 1:, s[0]] = s[0]; refs[:, g, 0] = s[0]; facts[:, 16 * g:16 * g + 16, s[0]] = 1024
    need = rng.integers(50, 58, need.shape); need[:, 0] = rng.integers(49, 53, (N, L)); need[::2, 2] = 128
    need[:, ST - 1] = np.where(rng.random((N, L)) < 0.5, 1, need[:, ST - 1])
    d[:] = DM; d[1::2] = np.where(rng.random(d[1::2].shape) < 0.1, rng.integers(0, DM, d[1::2].shape), DM)
    return pack(refs, gloss, facts, cases, need, v, p, a, d)
def setup_inputs_calm(rng):
    refs, gloss, facts, cases, need, v, p, a, d = parts(rng)
    hi = np.arange(8)[:, None] >= 4; few = np.where(hi, W - 4 + np.arange(4), np.arange(4))
    refs[:, :7] = hotty(rng, few, V, 1.0)[:, :7]; gloss[:, :7] = hotty(rng, few, W, 1.0)[:, :7]
    v = rng.integers(0, 4, v.shape) + (V - 4) * hi; p = rng.integers(0, 4, p.shape) + (V - 4) * hi; a = rng.integers(0, 4, a.shape) + 12 * hi
    return pack(refs, gloss, facts, cases, need, v, p, a, d)
def check_inputs(d):
    bad = []
    for k, lo, hi in (("refs", 0, W - 1), ("gloss", 0, W - 1), ("need", 1, 128), ("vp0", 0, V - 1), ("act0", 0, 15), ("dep0", 0, DM)):
        if np.min(d[k]) < lo or np.max(d[k]) > hi: bad.append("range of " + k)
    for k in ("facts", "cases"):
        if not np.all(np.isfinite(np.asarray(d[k]).astype(np.float32))): bad.append("not finite: " + k)
    return bad
def reference(refs, gloss, facts, cases, need, vp0, act0, dep0):
    R = refs.astype(np.int64).reshape(N, 8, 16, V); GL = gloss.astype(np.int64).reshape(N, 8, 16, W)
    X = facts.astype(np.float32).reshape(N, 8, 16, W); Z = cases.astype(np.float32).reshape(N, 8, 16, L)
    v = vp0[:, :8].astype(np.int64); p = vp0[:, 8:].astype(np.int64).reshape(N, DM, 8, L)
    a = act0.astype(np.int64).reshape(N, DM, 8, L); d = dep0[:, 0].astype(np.int64); c = need.astype(np.int64)
    gi = np.arange(8)[:, None, None]; lane = np.arange(L); shown = np.zeros((N, 8, 16, L), np.int64)
    for t in range(ST):
        writes = []
        for r in range(N):
            q = (r + 1 + t % (N - 1)) % N
            B = np.take_along_axis(R[r], v[r][:, None, :], 2)
            for j in range(DM, 1, -1): B = GL[r][gi, a[r, j - 1][:, None, :], B]
            a1 = np.array(a[r, 0]); T = GL[q][gi, a1[:, None, :], B]; shown[r] = T
            n = np.zeros((16, L), np.int64)
            for g in range(8): n = n + np.sum((X[q, g][:, T[g]] <= Z[r, g][:, None, :]).astype(np.int64), axis=0)
            met = n >= c[r, t][None, :]
            every = np.all(met, axis=0); some = np.any(met, axis=0); fu = np.argmin(met, axis=0); hm = np.argmax(met, axis=0)
            tf = T[:, fu, lane]; bf = B[:, fu, lane]; th = T[:, hm, lane]
            pop = every & (d[r] > 0); push = ~every & (d[r] < DM); put = ~every & some & (d[r] == DM)
            after = (v[r] + 1) & (V - 1); nv = np.where(push, tf & (V - 1), after)
            for j in range(1, DM + 1):
                leave = pop & (d[r] == j); enter = push & (d[r] == j - 1)
                nv = np.where(leave, p[r, j - 1], nv)
                a[r, j - 1] = np.where(enter, tf & 15, np.where(leave, 0, a[r, j - 1])); p[r, j - 1] = np.where(enter, after, p[r, j - 1])
            v[r] = nv; d[r] = d[r] + push.astype(np.int64) - pop.astype(np.int64)
            writes.append((q, a1, bf, th, np.nonzero(put)[0]))
        for q, a1, bf, th, who in writes:
            for g in range(8):
                places, first = np.unique(bf[g, who], return_index=True); w = who[first]
                GL[q, g, a1[g, w], bf[g, w]] = th[g, w]
    yvp = np.concatenate([v, p.reshape(N, 8 * DM, L)], axis=1)
    return {"yt": shown.reshape(N, 128, L).astype(np.float32), "yg": np.sum(GL.reshape(N, 128, 16, W // 16), axis=2).astype(np.float32), "yvp": yvp.astype(np.float32),
            "yact": a.reshape(N, 8 * DM, L).astype(np.float32), "ydep": d.reshape(N, 1, L).astype(np.float32)}

@@ -1,0 +1,691 @@
+from concourse.mybir import AluOpType, AxisListType, ActivationFunctionType
+
+A = AluOpType
+F = ActivationFunctionType
+ST, L, W, NV = 6, 256, 4096, 1024
+MG = 128
+HALF = MG + 8 * W
+SHARE = {(3, 0): "xx", (3, 1): "sv", (3, 2): "x", (3, 3): "xx", (2, 0): "x", (2, 1): "xx", (2, 2): "sv", (2, 3): "ssxx",
+         (1, 0): "ssss", (1, 1): "ssxx", (1, 2): "ss", (1, 3): "xxxx"}
+SMALL = {"ar": "s", "a3": "x", "Gf": "s", "Gh": "x", "val": "s", "k1": "s"}
+BANKS = [("B5", "B6", "B7", "B7"), ("B0", "B1", "B2", "B3")]
+CH = [(0, 32), (32, 96), (128, 64), (192, 64)]
+FP = 96
+EARLY = {(2, 0): 2.0, (3, 0): 1.3, ("f", 2): 4.5, "wide": 0.3, ("w", 1): 3.2, ("s", 1): -0.1, (1, 2): 2.8, ("w", 0): 9.1,
+         ("f", 0): 1.8, ("v", 1): 0.1, (3, 1): 4.7, ("r", 1): 8.9, (2, 2): 0.7, ("e", 1): -2.5, ("r", 0): 11.2, (1, 0): 5.4,
+         ("e", 0): -1.5, ("pre", 0): 2.3, ("f", 1): 9.3, ("pre", 1): 2.0, (1, 1): 19.7, ("f", 3): 8.5, ("z", 1): 3.2,
+         ("s", 0): -0.1, ("z", 0): 2.2, (2, 3): 11.3, (1, 3): -0.8, (3, 3): 0.9, "conv": 1.1}
+LIFT = {"small": 35.0, "gloss": 3.0, "pattern": 100.0, "cases": 16.0, "state": 20.0, "digits": 12.0, "rest": 16.0}
+FILL = {"v": 14, "s": 13, "g": 5}
+BF, F32, I32, U16 = "bfloat16", "float32", "int32", "uint16"
+
+
+def sb(n, dt):
+    return ("sbuf", [128, n], dt)
+
+
+SCRATCH = {
+    "tab": sb(16 * W + 2 * MG, BF), "gin": sb(2048, I32), "hl": sb(2 * W + 2 * MG, BF), "ex2": sb(W, BF), "G1": sb(W, BF),
+    "G": sb(W, BF), "fa": sb(W, BF), "rf": sb(NV, I32), "ID": sb(1040, F32), "FO": sb(1040, F32),
+    "F2": sb(512, F32), "RI": sb(256, I32), "NI": sb(256, I32), "CN": sb(512, BF), "CNI": sb(1536, BF),
+    "ci": sb(8, I32), "cf": sb(32, F32), "pw": sb(64, F32), "m2": sb(16, F32),
+    "CT": sb(144, BF), "CK": sb(144, BF), "C1": sb(144, BF), "CC": sb(144, BF), "km": sb(144, BF), "gm": sb(128, BF),
+    "IDN": sb(128, BF), "D01": sb(128, BF), "D2": sb(128, BF), "BDK": sb(128, BF), "BDB": sb(128, BF),
+    "BDW": sb(128, BF), "BD0": sb(128, BF), "BD8": sb(128, BF), "UP": sb(128, BF), "UN": sb(128, BF),
+    "t1": sb(128, BF), "t2": sb(128, BF), "nthr": sb(128, BF), "M16": sb(32, BF),
+    "NE": sb(768, BF), "c256": sb(32, BF), "AT": sb(16, BF), "J4": sb(192, I32), "J6": sb(288, I32),
+    "base": sb(16, F32), "CB": sb(144, BF), "RL": sb(8, U16),
+    "RO": sb(ST * 320, U16), "RQ": sb(ST * 288, U16), "PO": sb(ST * 48, I32), "PI": sb(ST * 32, I32),
+    "AR": sb(768, BF), "R0": sb(128, I32), "O3": sb(256, U16), "O2": sb(256, U16), "TU": sb(256, U16), "TI": sb(256, U16),
+    "vl": sb(16, U16), "FL": sb(128, U16), "SM0": sb(80, I32), "SM1": sb(80, I32), "W0": sb(200, I32), "W1": sb(200, I32),
+    "sg0": sb(128, BF), "isf0": sb(256, BF), "fl0": sb(16, U16), "Gf0": sb(256, BF), "kr0": sb(128, U16), "kc": sb(16, F32),
+    "sg1": sb(128, BF), "isf1": sb(256, BF), "fl1": sb(16, U16), "Gf1": sb(256, BF), "kr1": sb(128, U16), "val": sb(256, BF), "md": sb(256, BF), "nm": sb(256, BF), "kept": sb(256, BF),
+    "Q0": sb(128, F32), "Q1": sb(128, F32), "of": sb(32, U16),
+}
+for _b in range(8):
+    SCRATCH["B%d" % _b] = ("psum", [128, 512], F32)
+
+SEMAPHORES = (["cv", "cs", "cp", "cg", "sent", "small", "drf", "dfa", "perm", "back", "outs", "out0"]
+              + ["gl%d" % i for i in range(8)] + ["cn%d" % i for i in range(3)] + ["ti%d" % i for i in range(2)]
+              + ["rq%d_%d" % (t, c) for t in range(ST) for c in range(4)]
+              + ["rs%d_%d" % (t, h) for t in range(ST) for h in range(2)])
+
+CY, PCY = 1.04e-3, 0.52e-3
+GA, SC, TURNS, LEAN = 1.56, 3.8, 1, 0.2
+HOP, SYNC, SAME, DLAT, DBW = 3.0, 0.15, 0.08, 2.0, 250e3
+
+
+def record(g, core, T, topo, rank):
+    n_ranks = len(T.cores)
+    ops, lastw, readers, groups, boost, tag = [], {}, {}, {}, [0.0], [None]
+
+    def add(cost, fn, r=(), w=(), kind="c", sem=None, val=0, after=(), nbytes=0):
+        i = len(ops)
+        deps = {}
+        for k in r:
+            for d in lastw.get(k, ()):
+                deps[d] = True
+        for k in w:
+            hard = k[0] != "B" or not k[1:].isdigit()
+            for d in list(lastw.get(k, ())) + readers.get(k, []):
+                deps[d] = deps.get(d, False) or hard
+        for d in after:
+            deps[d] = True
+        for k in r:
+            readers.setdefault(k, []).append(i)
+        for k in w:
+            lastw[k] = [i]
+            readers[k] = []
+        ops.append({"cost": cost, "fn": fn, "deps": deps, "kind": kind, "sem": sem, "val": val, "bytes": nbytes,
+                    "boost": boost[0], "early": EARLY.get(tag[0], 0.0), "tag": tag[0]})
+        if kind == "dma":
+            groups.setdefault(sem, []).append(i)
+        return i
+
+    def users(*keys):
+        return [d for k in keys for d in list(lastw.get(k, ())) + readers.get(k, [])]
+
+    def wrote(ids, *keys):
+        for k in keys:
+            lastw[k] = ids
+            readers[k] = []
+
+    def vc(n, rate=1.0):
+        return max(64.0, n * rate) * CY
+
+    def ts(out, in0, s1, s2, o0, o1, r, w, n=64, rate=1.0, after=()):
+        if o1 is None:
+            return add({"v": vc(n, rate)}, lambda e: g.vector.tensor_scalar(out, in0, s1, None, o0), r, w, after=after)
+        return add({"v": vc(n, rate)}, lambda e: g.vector.tensor_scalar(out, in0, s1, s2, o0, o1), r, w, after=after)
+
+    def tt(out, in0, in1, op, r, w, n=32, rate=2.0):
+        return add({"v": vc(n, rate)}, lambda e: g.vector.tensor_tensor(out, in0, in1, op), r, w)
+
+    def ttg(out, in0, in1, op, r, w, n, rate=None, after=()):
+        return add({"v": 0.06 + n * (rate or GA) * CY}, lambda e: g.vector.tensor_tensor(out, in0, in1, op), r, w, after=after)
+
+    def cp(out, in_, r, w, n=64, rate=1.0):
+        return add({"v": vc(n, rate)}, lambda e: g.vector.tensor_copy(out, in_), r, w)
+
+    def either(out, in_):
+        return lambda e: g.vector.tensor_copy(out, in_) if e == "v" else g.scalar.activation(out, in_, F.Copy)
+
+    def only(cost, who):
+        return cost if who == "x" else {who: cost[who]}
+
+    def gat(out, in_, r, w, n, who="x", after=()):
+        return add(only({"v": 0.06 + n * GA * CY, "s": 0.08 + n * GA * CY}, who), either(out, in_), r, w, after=after)
+
+    def act(out, in_, func, bias, r, w, n):
+        return add({"s": vc(n)}, lambda e: g.scalar.activation(out, in_, func, bias=bias), r, w)
+
+    def ms(ap, c, w, n=64):
+        return add({"v": vc(n)}, lambda e: g.vector.memset(ap, c), (), w)
+
+    def io(out, pat, base, cm, w, n, small=True):
+        if small:
+            fn = lambda e: g.iota(out, pat, base, cm, allow_small_or_imprecise_dtypes=True)
+        else:
+            fn = lambda e: g.iota(out, pat, base, cm)
+        return add({"g": 0.16 + 2 * n * CY}, fn, (), w)
+
+    def mm(parts, r, w, cyc, first=True, final=True):
+        def fn(e):
+            ins = None
+            for j, (o, lt, rh) in enumerate(parts):
+                ins = g.tensor.matmul(o, lt, rh, first and j == 0, final and j == len(parts) - 1)
+            return ins
+        return add({"p": cyc * PCY}, fn, r, w)
+
+    def dma(q, out, in_, sem, r, w, nbytes, after=()):
+        eng = g.sync if q == "y" else g.scalar
+        return add({q: 0.1}, lambda e: eng.dma_start(out, in_), r, w, kind="dma", sem=sem, nbytes=nbytes, after=after)
+
+    def send(out, in_, peer, src, sem, r, w, extra=0.0):
+        dst = T.cores[peer]
+        assert topo.may_write(core, dst)
+        rid, pid, _se = topo.addr(dst)
+        m = topo.mask(core, dst)
+        i = add({"g": 0.5}, lambda e: g.remote_dma(out, in_, T.sem[sem], T.sem.sent, pid, rid, m), r, (), kind="rem",
+                val=len(topo.engines(core, dst)))
+        add({None: HOP + extra}, None, (), w, kind="recv", sem=sem, val=len(topo.engines(T.cores[src], core)), after=[i])
+
+    col = lambda j: T.cf[:, j:j + 1]
+    slide = lambda C, x: C[:, 15 - x:143 - x]
+    win = T.tab[:, MG:MG + 16 * W]
+    SM, WK, QQ = [T.SM0, T.SM1], [T.W0, T.W1], [T.Q0, T.Q1]
+    EXP = [(T.hl, 0, "hi"), (T.hl, W, "lo"), (T.ex2, 0, "ex2")]
+
+    def load_gloss(c):
+        dma("y", T.gin[:, 512 * (c % 4):512 * (c % 4) + 512], T.gloss[:, 512 * c:512 * c + 512], "gl%d" % c, (), ["gin%d" % (c % 4)], 262144)
+
+    boost[0] = LIFT["small"]
+    dma("s", T.RI[8:40, :], T.vp0[:], "small", (), ["RIa"], 32768)
+    dma("s", T.RI[40:64, :], T.act0[:], "small", (), ["RIb"], 24576)
+    for j in range(8):
+        dma("s", T.RI[j:j + 1, :], T.dep0[:], "small", (), ["RI%d" % j], 1024)
+    dma("s", T.CN[:, 0:256], T.cases[:], "small", (), ["CNa"], 65536)
+    dma("s", T.NI[0:6, :], T.need[:], "small", (), ["NI"], 6144)
+    boost[0] = LIFT["gloss"]
+    for c in range(4):
+        load_gloss(c)
+    boost[0] = 0.0
+
+    io(T.ci[:, 0:1], [[0, 1]], 0, 1, ["p"], 1, False)
+    io(T.ID[:, 0:144], [[1, 144]], 0, 0, ["ID0"], 144)
+    io(T.km[:], [[0, 9], [1, 16]], 0, 0, ["km"], 144)
+    io(T.gm[:], [[16, 8], [0, 16]], 0, 0, ["gm"], 128)
+    io(T.ID[:, 144:1040], [[1, 896]], 144, 0, ["ID1"], 896)
+    io(T.NE[0:32, :], [[1, 6], [0, 128]], 0, -1, ["NE"], 768)
+    io(T.c256[:, 0:16], [[0, 2], [256, 8]], 0, 0, ["c256"], 16)
+    ms(T.c256[:, 16:24], 1.0, ["one"])
+    io(T.AT[:], [[4096, 16]], 0, 0, ["AT"], 16)
+    io(T.base[:, 0:16], [[0, 2], [16, 8]], 0, 0, ["base"], 16)
+    io(T.J4[:], [[1, 6], [1, 4], [0, 8]], 0, 0, ["J4"], 192, False)
+    for t in range(ST):
+        io(T.J6[:, 48 * t:48 * t + 48], [[0, 2], [1, 3], [0, 8]], 1 + t, 0, ["J6%d" % t], 48, False)
+    p = T.ci[:, 0:1]
+    ts(T.ci[:, 1:2], p, 15, None, A.bitwise_and, None, ["p"], ["ki"])
+    ts(T.ci[:, 2:3], p, 7, None, A.bitwise_and, None, ["p"], ["xi"])
+    ki, xi = T.ci[:, 1:2], T.ci[:, 2:3]
+    K, NK, GB15, P16, WT, WKK, K1, M2, M3, NWT, X16, GB, PW2, PF, LT8, XF, K0, K8 = range(18)
+    cp(col(K), ki, ["ki"], ["k"])
+    ts(col(M3), ki, 3.0, None, A.is_equal, None, ["ki"], ["m3"])
+    ts(col(M2), ki, 2.0, None, A.is_equal, None, ["ki"], ["m2c"])
+    ms(T.pw[:, 16:32], 0.5, ["half"])
+    add({"v": vc(64)}, lambda e: g.vector.tensor_tensor_scan(T.pw[:, 0:16], T.pw[:, 16:32], T.pw[:, 16:32], 65536.0, A.mult, A.max),
+        ["half"], ["pw"])
+    ts(T.m2[:], T.pw[:, 0:16], col(M2), None, A.mult, None, ["pw", "m2c"], ["m2"])
+    ts(T.G1[:, 0:64], T.ID[:, 0:64], col(M3), None, A.mult, None, ["ID0", "m3"], ["G10", "G11"])
+    boost[0] = LIFT["pattern"]
+    for i in range(6):
+        w_ = 64 << i
+        ts(T.G1[:, w_:2 * w_], T.G1[:, 0:w_], T.m2[:, 9 - i:10 - i], None, A.add, None, ["G10", "G11", "m2"],
+           ["G10", "G11"] if i < 5 else ["G12", "G13"], w_, 0.5)
+    boost[0] = 0.0
+    ts(col(NK), ki, -1.0, None, A.mult, None, ["ki"], ["nk"])
+    ts(col(GB), p, col(K), None, A.subtract, None, ["p", "k"], ["gb"])
+    ts(col(GB15), p, col(K), 15.0, A.subtract, A.add, ["p", "k"], ["gb15"])
+    ts(col(P16), p, 16.0, 15.0, A.mult, A.add, ["p"], ["p16"])
+    ts(col(WT), xi, 0.0, None, A.is_equal, None, ["xi"], ["wt"])
+    ts(col(NWT), xi, 0.0, None, A.not_equal, None, ["xi"], ["nwt"])
+    ts(col(K0), ki, 0.0, None, A.is_equal, None, ["ki"], ["k0"])
+    ts(col(K8), ki, 8.0, None, A.is_equal, None, ["ki"], ["k8"])
+    tt(col(WKK), col(M2), col(M3), A.add, ["m2c", "m3"], ["wk"])
+    ts(col(K1), ki, 1.0, None, A.add, None, ["ki"], ["k1c"])
+    ts(col(X16), ki, 16.0, -1.0, A.mult, A.add, ["ki"], ["x16"])
+    cp(col(PF), p, ["p"], ["pf"])
+    cp(col(XF), xi, ["xi"], ["xf"])
+    ts(col(LT8), ki, 8.0, 8.0, A.is_lt, A.mult, ["ki"], ["lt8"])
+    ts(T.pw[:, 32:48], T.ID[:, 0:16], col(K), None, A.is_equal, None, ["ID0", "k"], ["pwa"])
+    cp(T.M16[:, 0:16], T.pw[:, 32:48], ["pwa"], ["M16a"])
+    ts(T.M16[:, 16:32], T.ID[:, 0:16], col(K), None, A.not_equal, None, ["ID0", "k"], ["M16b"])
+    tt(T.pw[:, 48:64], T.pw[:, 32:48], T.pw[:, 0:16], A.mult, ["pwa", "pw"], ["pwb"])
+    add({"v": vc(64)}, lambda e: g.vector.tensor_reduce(col(PW2), T.pw[:, 48:64], AxisListType.X, A.add), ["pwb"], ["pw2"])
+    ts(T.nthr[:, 0:16], T.pw[:, 0:16], -2.0, None, A.mult, None, ["pw"], ["nthr"])
+    for w_ in (16, 32, 64):
+        cp(T.nthr[:, w_:2 * w_], T.nthr[:, 0:w_], ["nthr"], ["nthr"])
+    for buf, wc, nm, wn in ((T.CT, WT, "CT", "wt"), (T.CK, WKK, "CK", "wk"), (T.C1, K1, "C1", "k1c")):
+        ts(buf[:], T.ID[:, 0:144], col(GB15), col(wc), A.is_equal, A.mult, ["ID0", "gb15", wn], [nm], 144)
+    ts(T.CC[:], T.km[:], 15.0, None, A.is_equal, None, ["km"], ["CC"], 144, 0.5)
+    ts(T.IDN[:], T.ID[:, 0:128], col(PF), None, A.is_equal, None, ["ID0", "pf"], ["IDN"], 128)
+    ts(T.D01[:], T.IDN[:], col(WT), None, A.mult, None, ["IDN", "wt"], ["D01"])
+    ts(T.D2[:], T.IDN[:], col(NWT), None, A.mult, None, ["IDN", "nwt"], ["D2"])
+    for buf, sc, nm, sn in ((T.BDK, col(WKK), "BDK", "wk"), (T.BDB, 65536.0, "BDB", "gb"), (T.BDW, col(PW2), "BDW", "pw2"),
+                            (T.BD0, col(K0), "BD0", "k0"), (T.BD8, col(K8), "BD8", "k8")):
+        ts(buf[:], T.gm[:], col(GB), sc, A.is_equal, A.mult, ["gm", "gb", sn], [nm])
+    ts(T.t1[:], T.km[:, 0:128], col(K), None, A.is_gt, None, ["km", "k"], ["t1"])
+    ts(T.t2[:], T.km[:, 0:128], col(K), None, A.is_equal, None, ["km", "k"], ["t2"])
+    tt(T.t1[:], T.t1[:], T.t2[:], A.subtract, ["t1", "t2"], ["t1"], 128)
+    ts(T.t2[:], T.gm[:], col(GB), None, A.is_equal, None, ["gm", "gb"], ["t2"])
+    tt(T.UP[:], T.t1[:], T.t2[:], A.mult, ["t1", "t2"], ["UP"], 128)
+    ts(T.UN[:], T.UP[:], -1.0, None, A.mult, None, ["UP"], ["UN"])
+    ts(T.NE[0:32, :], T.NE[0:32, :], 0.0, -1.0, A.is_equal, A.mult, ["NE"], ["NE"], 768, 0.5)
+    ts(T.base[:], T.base[:], col(K), None, A.add, None, ["base", "k"], ["base"])
+    cp(T.c256[:, 24:32], T.base[:, 0:8], ["base"], ["lnb"])
+    ts(T.CB[:], T.CT[:], 65536.0, None, A.mult, None, ["CT"], ["CB"])
+    for j in (0, 1, 4):
+        cp(T.RL[:, j:j + 1], xi, ["xi"], ["RL%d" % j])
+    ts(T.RL[:, 2:3], xi, 8.0, None, A.add, None, ["xi"], ["RL2"])
+    ts(T.RL[:, 3:4], col(LT8), col(XF), None, A.add, None, ["lt8", "xf"], ["RL3"])
+    RLK = ["RL%d" % j for j in range(5)]
+    rep2, rep4, rep6 = T.RL[:, 0:1], T.RL[:, 0:2], T.RL[:, 2:5]
+    ms(T.hl[:, 2 * W:2 * W + 2 * MG], 0.0, ["hlm"], 128)
+
+    ms(T.CN[:, 256:512], 0.0, ["CNb"], 128)
+    cp(T.CN[0:6, 256:512], T.NI[0:6, :], ["NI"], ["CNb"], 256)
+    boost[0] = LIFT["cases"]
+    for s in range(3):
+        send(T.CNI[:, 512 * s:512 * s + 512], T.CN[:], (rank + 1 + s) % n_ranks, (rank - 1 - s) % n_ranks, "cn%d" % s,
+             ["CNa", "CNb"], ["CNI%d" % s], 2.0 + 2.0 * s)
+    boost[0] = 0.0
+
+    def widen(s):
+        buf, o, key = EXP[s]
+        old = users(key)
+        tag[0] = "wide"
+        wrote([add({"v": vc(128), "s": vc(256)}, either(buf[:, o + k:o + W:16], T.CNI[:, 512 * s:512 * s + 256]),
+                   ["CNI%d" % s], (), after=old) for k in range(16)], key)
+
+    ts(T.FO[0:64, 0:1040], T.ID[0:64, :], T.cf[0:64, P16:P16 + 1], None, A.is_equal, None, ["ID0", "ID1", "p16"], ["FO0", "FO1"], 1040)
+    cp(T.F2[0:64, 0:256], T.RI[0:64, :], ["RIa", "RIb"] + ["RI%d" % j for j in range(8)], ["F2a"], 256)
+    for j in range(8):
+        for x0 in range(0, 16, 4):
+            boost[0] = LIFT["state"] if j == 0 and x0 == 0 else 0.0
+            mm([(T.B5[:, 16 * j:16 * j + 16], T.FO[0:64, 128 * j + 15 - x:128 * j + 143 - x], T.F2[0:64, x:256:16])
+                for x in range(x0, x0 + 4)], ["FO0", "FO1", "F2a"], ["B5"], 4 * 256, x0 == 0, x0 == 12)
+    place = [72, 64, 16, 24, 32, 40, 48, 56]
+    for h in range(2):
+        ids = [cp(SM[h][:, place[j]:place[j] + 8], T.B5[:, 16 * j + 8 * h:16 * j + 8 * h + 8], (), ["B5"]) for j in range(8)]
+        wrote(ids[0:1], "D%d" % h)
+        wrote(ids[1:2], "V%d" % h)
+        wrote(ids[2:8], "X%d" % h)
+
+    his, los = [], []
+    boost[0] = LIFT["digits"]
+    for c in range(8):
+        sl, gs, bk = slice(512 * c, 512 * c + 512), slice(512 * (c % 4), 512 * (c % 4) + 512), "B%d" % (c % 4)
+        his.append(cp(T.hl[:, sl], T.gin[:, gs], ["gin%d" % (c % 4)], ["hi%d" % c], 512))
+        mm([(T[bk][:], T.IDN[:], T.hl[:, sl])], ["IDN", "hi%d" % c], [bk], 512)
+        los.append(tt(T.hl[:, W + 512 * c:W + 512 * c + 512], T.gin[:, gs], T[bk][:], A.subtract,
+                      ["gin%d" % (c % 4)], [bk, "lo%d" % c], 512, 1.0))
+        if c < 4:
+            load_gloss(c + 4)
+    boost[0] = LIFT["rest"]
+    dma("y", T.rf[:], T.refs[:], "drf", (), ["rf"], 524288, [los[3]])
+    dma("y", T.fa[:], T.facts[:], "dfa", (), ["fa"], 1048576, [los[3]])
+    boost[0] = 0.0
+    wrote(his + los, "hi", "lo")
+    due = sorted([((j + 1.0) / n + (0.4 if e == "v" else 0.0), e) for e, n in FILL.items() for j in range(n)])
+    perm = []
+    for a in range(16):
+        for u in range(2):
+            e = due[2 * a + u][1]
+            o = T.tab[:, MG + W * a + 2048 * u:MG + W * a + 2048 * u + 2048]
+            i_ = T.G1[:, 2048 * u:2048 * u + 2048]
+            keys = ["G1%d" % (2 * u), "G1%d" % (2 * u + 1)]
+            if e == "g":
+                add({"g": 0.2 + 4096 * CY}, (lambda o, i_: lambda e: g.affine_select(o, i_, [[0, 2048]], A.is_ge, 0.0, 0, 0))(o, i_),
+                    keys, ["tb%d_%d" % (a, u)])
+            else:
+                add({e: vc(1024 if e == "v" else 2048)}, either(o, i_), keys, ["tb%d_%d" % (a, u)])
+        perm.append(dma("y", T.tab[0:128:8, MG + W * a:MG + W * a + W], T.hl[a:128:16, 0:2 * W], "perm", ["hi", "lo"],
+                        ["tb%d_0" % a, "tb%d_1" % a], 131072))
+    wrote(perm, "tab")
+    widen(2)
+    widen(0)
+
+    def level(lv, obuf, oo, okey, buf, gkey, c, lead, lkey, out, outkey):
+        tag[0] = (lv, c)
+        old, who = users(gkey), SHARE[(lv, c)]
+        l0, nl = CH[c]
+        n = 16 * nl // len(who)
+        wrote([gat(buf[:, 16 * l0 + n * u:16 * l0 + n * (u + 1)], win.indirect(obuf[:, oo + n // 16 * u:oo + n // 16 * (u + 1)]),
+                   ["tab", okey], (), n, e, old) for u, e in enumerate(who)], gkey)
+        ps = T["B%d" % c][:, 0:nl]
+        parts = [] if lead is None else [(ps, T.IDN[:], lead)]
+        parts += [(ps, slide(T.CT, x), buf[:, 16 * l0 + x:16 * (l0 + nl):16]) for x in range(16)]
+        mm(parts, [gkey, "CT", "IDN"] + ([lkey] if lkey else []), ["B%d" % c], max(64, nl) * len(parts))
+        tag[0] = "conv"
+        cp(out, ps, (), ["B%d" % c, outkey], nl)
+
+    def lists(t, h):
+        S, ro = SM[h], 320 * t + 160 * h
+        cp(T.vl[:, 8 * h:8 * h + 8], S[:, 64:72], ["V%d" % h], ["vl%d" % h])
+        cp(T.RO[:, ro + 136:ro + 160], S[:, 40:64], ["X%d" % h], ["al%d_%d" % (t, h)])
+        ts(T.RO[:, ro + 128:ro + 136], S[:, 72:80], 3.0 + t, None, A.is_equal, None, ["D%d" % h], ["d3%d_%d" % (t, h)])
+
+    tag[0] = None
+    for h in range(2):
+        lists(0, h)
+
+    for t in range(ST):
+        s = t % 3
+        peer, asker = (rank + 1 + s) % n_ranks, (rank - 1 - s) % n_ranks
+        last = t == ST - 1
+        if last:
+            old = users("hi", "lo")
+            tag[0] = None
+            wrote([dma("y", T.hl[a:128:16, 0:2 * W], T.tab[0:128:8, MG + W * a:MG + W * a + W], "back", ["tab"], (), 131072, old)
+                   for a in range(16)], "hl")
+        for h in range(2):
+            ro, ar = 320 * t + 160 * h, 384 * h
+            tag[0] = ("r", h)
+            gat(T.AR[:, ar + 256:ar + 384], T.AT[:].indirect(T.RO[:, ro + 152:ro + 160]), ["AT", "al%d_%d" % (t, h)], ["A3%d" % h], 128, SMALL["a3"])
+            ttg(T.R0[:], T.rf[:].indirect(T.vl[:, 8 * h:8 * h + 8]), T.AR[:, ar + 256:ar + 384], A.add,
+                ["rf", "vl%d" % h, "A3%d" % h], ["R0"], 128)
+            cp(T.O3[:, 128 * h:128 * h + 128], T.R0[:], ["R0"], ["O3%d" % h], 128)
+            gat(T.AR[:, ar:ar + 256], T.AT[:].indirect(T.RO[:, ro + 136:ro + 152]), ["AT", "al%d_%d" % (t, h)], ["AR%d" % h], 256, SMALL["ar"])
+        for c in range(4):
+            h, u = c // 2, c % 2
+            l0, nl = CH[c]
+            lh = l0 - 128 * h
+            ro, ar, rq = 320 * t + 160 * h + lh, 384 * h + lh, 288 * t + 144 * h + lh
+            level(3, T.O3, l0, "O3%d" % h, T.G, "G%d" % c, c, T.AR[:, ar + 128:ar + 128 + nl], "AR%d" % h,
+                  T.O2[:, l0:l0 + nl], "O2%d" % c)
+            level(2, T.O2, l0, "O2%d" % c, T.G, "G%d" % c, c, T.AR[:, ar:ar + nl], "AR%d" % h,
+                  T.RO[:, ro:ro + nl], "ro%d_%d" % (t, c))
+            n = nl + 16 * u
+            send(T.RQ[:, rq:rq + n], T.RO[:, ro:ro + n], peer, asker, "rq%d_%d" % (t, c),
+                 ["ro%d_%d" % (t, c)] + (["al%d_%d" % (t, h), "d3%d_%d" % (t, h)] if u else []), ["rq%d_%d" % (t, c)])
+        for h in range(2):
+            S, Wk, k = SM[h], WK[h], lambda s_, h=h: s_ + str(h)
+            tag[0] = ("pre", h)
+            ts(Wk[:, 0:8], S[:, 64:72], 1.0, None, A.add, None, [k("V")], [k("w0")])
+            ts(S[:, 8:16], Wk[:, 0:8], NV - 1, None, A.bitwise_and, None, [k("w0")], [k("AF")])
+            ttg(Wk[:, 8:40], S[:, 72:80].indirect(rep4), T.J4[:, 32 * t:32 * t + 32], A.is_equal, [k("D"), "J4"] + RLK, [k("w1")], 32)
+            tt(Wk[:, 8:40], Wk[:, 8:40], S[:, 8:40], A.mult, [k("w1"), k("AF"), k("X")], [k("w1")])
+            tt(Wk[:, 8:24], Wk[:, 8:24], Wk[:, 24:40], A.add, [k("w1")], [k("w1")])
+            tt(Wk[:, 40:48], Wk[:, 8:16], Wk[:, 16:24], A.add, [k("w1")], [k("aE")])
+            ts(Wk[:, 48:56], S[:, 72:80], 3.0 + t, None, A.is_lt, None, [k("D")], [k("c3")])
+            tt(Wk[:, 56:64], S[:, 8:16], Wk[:, 40:48], A.subtract, [k("AF"), k("aE")], [k("dE")])
+        ebuf, eo, ekey = EXP[s]
+        for c in range(4):
+            l0, nl = CH[c]
+            level(1, T.RQ, 288 * t + 16 * (c // 2) + l0, "rq%d_%d" % (t, c), T.G1, "G1%d" % c, c, None, None,
+                  T.TU[:, l0:l0 + nl], "TU%d" % c)
+        for h in range(2):
+            if last:
+                send(T.TI[:, 128 * h:128 * h + 128], T.TU[:, 128 * h:128 * h + 128], asker, peer, "ti%d" % h,
+                     ["TU%d" % (2 * h), "TU%d" % (2 * h + 1)], ["TI%d" % h])
+            for c in (2 * h, 2 * h + 1):
+                tag[0] = ("f", c)
+                l0, nl = CH[c]
+                co, ck, pc = 16 * l0, "G%d" % c, 16 * min(nl, FP)
+                old = users(ck)
+                wrote([ttg(T.G[:, co + a:co + a + pc], T.fa[:].indirect(T.TU[:, l0 + a // 16:l0 + (a + pc) // 16]),
+                           ebuf[:, eo + co + a:eo + co + a + pc], A.is_le, ["fa", "TU%d" % c, ekey], (), pc, None, old)
+                       for a in range(0, 16 * nl, pc)], ck)
+                ps = T.B4[:, l0:l0 + nl]
+                nd = 512 * s + 256 + l0
+                mm([(ps, T.NE[0:6, 128 * t:128 * t + 128], T.CNI[0:6, nd:nd + nl])]
+                   + [(ps, slide(T.CC, x), T.G[:, co + x:co + 16 * nl:16]) for x in range(16)],
+                   [ck, "NE", "CC", "CNI%d" % s], ["B4"], max(64, nl) * 17)
+            tag[0] = ("v", h)
+            Qh, k = QQ[h], lambda s_, h=h: s_ + str(h)
+            po, pi_, rq = 48 * t + 24 * h, 32 * t + 16 * h, 288 * t + 144 * h
+            rqk, pk = "rq%d_%d" % (t, 2 * h + 1), "po%d_%d" % (t, h)
+            na, nb, nc, nd_ = BANKS[h]
+            Ba, Bb, Bc, Bd = T[na], T[nb], T[nc], T[nd_]
+            sg, isf, fl, Gf, kr = (T[k(x)] for x in ("sg", "isf", "fl", "Gf", "kr"))
+            act(sg[:], T.B4[:, 128 * h:128 * h + 128], F.Sign, 0.5, (), ["B4", k("sg")], 128)
+            mm([(Ba[:, 0:128], T.UP[:], sg[:])], ["UP", k("sg")], [na], 128)
+            mm([(Ba[:, 128:256], T.UN[:], sg[:])], ["UN", k("sg")], [na], 128)
+            act(isf[:], Ba[:, 0:256], F.Relu, col(NK), ["nk"], [na, k("isf")], 256)
+            mm([(Bb[:, 0:16], T.IDN[:], T.c256[:, 0:16])] + [(Bb[:, 0:16], slide(T.C1, x), isf[:, x:256:16]) for x in range(16)],
+               ["IDN", "c256", "C1", k("isf")], [nb], 64 * 17)
+            ts(fl[:], Bb[:, 0:16], col(X16), None, A.add, None, ["x16"], [nb, k("fl")])
+            tt(T.PO[:, po + 8:po + 24], Bb[:, 0:16], T.c256[:, 0:16], A.is_gt, ["c256"], [nb, pk + "f"])
+            for u, nm in enumerate(("Gf", "Gh")):
+                gat(Gf[:, 128 * u:128 * u + 128], T.G1[:, 2048 * h:2048 * h + 2048].indirect(fl[:, 8 * u:8 * u + 8]),
+                    [k("fl"), "G1%d" % (2 * h), "G1%d" % (2 * h + 1)], [k(nm)], 128, SMALL[nm])
+            tag[0] = ("w", h)
+            cp(Qh[:, 8:16], T.RQ[:, rq + 128:rq + 136], [rqk], [k("d3")])
+            tt(Qh[:, 8:16], Qh[:, 8:16], T.PO[:, po + 8:po + 16], A.mult, [k("d3"), pk + "f"], [k("d3")])
+            tt(Qh[:, 48:56], Qh[:, 8:16], T.PO[:, po + 16:po + 24], A.mult, [k("d3"), pk + "f"], [k("ask")])
+            tag[0] = ("v", h)
+            mm([(Ba[:, 256:384], T.BDK[:], Gf[:, 0:128])], ["BDK", k("Gf")], [na], 128)
+            ts(kr[:], Ba[:, 256:384], 1.0, None, A.add, None, (), [na, k("kr")], 128)
+            mm([(Bb[:, 24:32], T.IDN[:], T.c256[:, 16:24])] + [(Bb[:, 24:32], slide(T.CK, x), Gf[:, x:128:16]) for x in range(16)],
+               ["CK", "IDN", "one", k("Gf")], [nb], 64 * 17)
+            tt(T.kc[:, 8 * h:8 * h + 8], Bb[:, 24:32], Qh[:, 48:56], A.mult, [k("ask")], [nb, k("kc")])
+            add(only({"s": vc(8), "v": vc(8)}, SMALL["k1"]), either(Qh[:, 0:8], Bb[:, 24:32]), (), [nb, k("k1")])
+            mm([(Bd[:, 16:24], slide(T.CT, x), Gf[:, x:128:16]) for x in range(16)], ["CT", k("Gf")], [nd_], 1024)
+            cp(T.PO[:, po:po + 8], Bd[:, 16:24], (), [nd_, pk + "t"])
+            send(T.PI[:, pi_:pi_ + 16], T.PO[:, po:po + 16], asker, peer, "rs%d_%d" % (t, h), [pk + "t", pk + "f"], ["rs%d_%d" % (t, h)])
+            tag[0] = ("w", h)
+            a1 = T.RQ[:, rq + 136:rq + 144]
+            if not last:
+                mm([(Ba[:, 384:512], T.D01[:], Gf[:, 128:256]), (Ba[:, 384:512], T.D2[:], Gf[:, 0:128])],
+                   ["D01", "D2", k("Gf"), k("Gh")], [na], 256)
+                add(only({"s": vc(128), "v": vc(128)}, SMALL["val"]), either(T.val[:, 128 * h:128 * h + 128], Ba[:, 384:512]), (),
+                    [na, k("val")])
+            else:
+                mm([(Ba[:, 0:128], T.BD0[:], Gf[:, 128:256])], ["BD0", k("Gh")], [na], 128)
+                mm([(Ba[:, 128:256], T.BD8[:], Gf[:, 128:256])], ["BD8", k("Gh")], [na], 128)
+                add({"s": vc(256)}, either(T.val[:], Ba[:, 0:256]), (), [na, "val0", "val1"])
+                for u in range(2):
+                    sl = slice(128 * u, 128 * u + 128)
+                    ttg(T.md[:, sl], T.M16[:, 0:16].indirect(a1), T.val[:, sl], A.mult, [rqk, "M16a", "val0"], ["md%d" % u], 128)
+                    gat(T.nm[:, sl], T.M16[:, 16:32].indirect(a1), [rqk, "M16b"], ["nm%d" % u], 128, "s")
+            if not last:
+                ts(Qh[:, 16:24], a1, float(W), float(MG - 1), A.mult, A.add, [rqk], [k("E")])
+                ts(Qh[:, 32:40], a1, 8.0, None, A.is_lt, None, [rqk], [k("LHa")])
+                ts(Qh[:, 40:48], a1, 8.0, None, A.is_ge, None, [rqk], [k("LHb")])
+                ttg(Qh[:, 64:80], Qh[:, 48:56].indirect(rep2), Qh[:, 32:48], A.mult, [k("ask"), k("LHa"), k("LHb")] + RLK, [k("LA")], 16)
+                tt(Qh[:, 16:24], Qh[:, 16:24], Qh[:, 0:8], A.add, [k("E"), k("k1")], [k("E")])
+                ts(Qh[:, 24:32], Qh[:, 16:24], -1.0, float(16 * W + 2 * MG - 1), A.mult, A.add, [k("E")], [k("Eb")])
+                tt(Qh[:, 80:96], Qh[:, 16:32], Qh[:, 64:80], A.mult, [k("E"), k("Eb"), k("LA")], [k("OO")])
+                ends = (None, 8 * W + MG - 1)
+            else:
+                ts(Qh[:, 64:72], Qh[:, 0:8], -1.0, float(2 * W + MG), A.mult, A.add, [k("k1")], [k("LA")])
+                ts(Qh[:, 72:80], Qh[:, 0:8], -1.0, float(W + 2 * MG), A.mult, A.add, [k("k1")], [k("Eb")])
+                ttg(Qh[:, 80:96], Qh[:, 48:56].indirect(rep2), Qh[:, 64:80], A.mult, [k("ask"), k("LA"), k("Eb")] + RLK, [k("OO")], 16)
+                ends = (2 * W + MG - 1, 2 * W + 2 * MG - 1)
+            tt(Qh[:, 80:96], Qh[:, 80:96], T.base[:], A.max, [k("OO"), "base"], [k("OO")])
+            tag[0] = ("e", h)
+            parts, o, eqs, every = [(Bc[:, 0:128], T.IDN[:], T.nthr[:])], 2048 * h, [], []
+            eqk = ["G%d" % (2 * h), "G%d" % (2 * h + 1)]
+            old = users(*eqk)
+            for c in range(8 * h + 8):
+                lo = max(0, 16 * (c - 8 * h))
+                n = 128 - lo
+                eqs.append(ts(T.G[:, o:o + n], kr[:, lo:128], T.kc[:, c:c + 1], None, A.is_equal, None, [k("kr"), "kc%d" % (c // 8)], (),
+                              n, 0.5, old))
+                if c < 8 * h:
+                    parts.append((Bc[:, 0:128], T.BDB[:], T.G[:, o:o + n]))
+                else:
+                    parts.append((Bc[:, lo:lo + 16], T.BDW[:], T.G[:, o:o + 16]))
+                    if n > 16:
+                        parts.append((Bc[:, lo + 16:128], T.BDB[:], T.G[:, o + 16:o + n]))
+                o += n
+                if c % 4 == 3:
+                    wrote(eqs, "EQ")
+                    every.append(mm(parts, ["EQ", "IDN", "nthr", "BDB", "BDW"], [nc], 80 * len(parts), c == 3, c == 8 * h + 7))
+                    parts, eqs = [], []
+            wrote(every, *eqk)
+            tag[0] = ("z", h)
+            add({"s": vc(128)}, (lambda o_, i_: lambda e: g.scalar.activation(o_, i_, F.Relu, scale=-1.0))(sg[:], Bc[:, 0:128]),
+                (), [nc, k("sg")])
+            mm([(Bb[:, 32:40], T.IDN[:], T.c256[:, 24:32])] + [(Bb[:, 32:40], slide(T.CB, x), sg[:, x:128:16]) for x in range(16)],
+               ["CB", "IDN", "lnb", k("sg")], [nb], 64 * 17)
+            for u in range(2):
+                tt(Qh[:, 96 + 8 * u:104 + 8 * u], Bb[:, 32:40], Qh[:, 80 + 8 * u:88 + 8 * u], A.min, [k("OO")], [nb, k("m%d" % u)])
+            for u in range(2):
+                o_, i_ = T.of[:, 16 * h + 8 * u:16 * h + 8 * u + 8], Qh[:, 96 + 8 * u:104 + 8 * u]
+                if ends[u] is None:
+                    cp(o_, i_, [k("m%d" % u)], [k("of%d" % u)])
+                else:
+                    ts(o_, i_, -1.0, float(ends[u]), A.mult, A.add, [k("m%d" % u)], [k("of%d" % u)])
+            of = T.of[:, 16 * h:16 * h + 16]
+            if last:
+                ttg(T.kept[:], T.hl[:].indirect(of), T.nm[:], A.mult, ["hl", "hlm", k("of0"), k("of1"), "nm0", "nm1"], ["kept"], 256)
+                ttg(T.hl[:].indirect(of), T.kept[:], T.md[:], A.add, [k("of0"), k("of1"), "kept", "md0", "md1"], ["hl", "hlm"], 256, SC)
+            else:
+                old = users("tab")
+                wrote([add({"v": 0.06 + 128 * SC * CY},
+                           either(wn.indirect(T.of[:, 16 * h + 8 * u:16 * h + 8 * u + 8]), T.val[:, 128 * h:128 * h + 128]),
+                           [k("of%d" % u), k("val")], (), after=old)
+                       for u, wn in enumerate((T.tab[:, 0:HALF], T.tab[:, HALF:16 * W + 2 * MG]))], "tab")
+        if t == 0:
+            widen(1)
+        for h in range(2):
+            S, Wk, k = SM[h], WK[h], lambda s_, h=h: s_ + str(h)
+            tag[0] = ("s", h)
+            pi_, rk = 32 * t + 16 * h, "rs%d_%d" % (t, h)
+            tf, ne = T.PI[:, pi_:pi_ + 8], T.PI[:, pi_ + 8:pi_ + 16]
+            tt(Wk[:, 64:72], S[:, 72:80], ne, A.add, [k("D"), rk], [k("lev")])
+            tt(Wk[:, 72:80], Wk[:, 64:72], ne, A.mult, [k("lev"), rk], [k("lvp")])
+            ts(Wk[:, 80:88], tf, 15, None, A.bitwise_and, None, [rk], [k("ta")])
+            ts(Wk[:, 88:96], tf, NV - 1, None, A.bitwise_and, None, [rk], [k("tv")])
+            tt(S[:, 0:8], Wk[:, 80:88], ne, A.mult, [k("ta"), rk], [k("VA")])
+            ttg(Wk[:, 96:144], Wk[:, 64:80].indirect(rep6), T.J6[:, 48 * t:48 * t + 48], A.is_equal,
+                [k("lev"), k("lvp"), "J6%d" % t] + RLK, [k("MM")], 48)
+            ttg(Wk[:, 144:192], S[:, 0:16].indirect(rep6), S[:, 16:64], A.subtract, [k("VA"), k("AF"), k("X")] + RLK, [k("DX")], 48)
+            tt(Wk[:, 144:192], Wk[:, 144:192], Wk[:, 96:144], A.mult, [k("DX"), k("MM")], [k("DX")], 48)
+            tt(S[:, 16:64], S[:, 16:64], Wk[:, 144:192], A.add, [k("X"), k("DX")], [k("X")], 48)
+            tt(Wk[:, 192:200], Wk[:, 64:72], ne, A.add, [k("lev"), rk], [k("dt")])
+            ts(S[:, 72:80], Wk[:, 192:200], float(1 + t), float(4 + t), A.max, A.min, [k("dt")], [k("D")])
+            tt(Wk[:, 88:96], Wk[:, 88:96], S[:, 8:16], A.subtract, [k("tv"), k("AF")], [k("tv")])
+            tt(Wk[:, 88:96], Wk[:, 88:96], Wk[:, 48:56], A.mult, [k("tv"), k("c3")], [k("tv")])
+            tt(Wk[:, 88:96], Wk[:, 88:96], Wk[:, 56:64], A.add, [k("tv"), k("dE")], [k("tv")])
+            tt(Wk[:, 88:96], Wk[:, 88:96], ne, A.mult, [k("tv"), rk], [k("tv")])
+            tt(S[:, 64:72], Wk[:, 88:96], Wk[:, 40:48], A.add, [k("tv"), k("aE")], [k("V")])
+            if not last:
+                lists(t + 1, h)
+
+    tag[0] = None
+    qs = ["y", "s"]
+    mm([(T.B4[:, 0:256], T.IDN[:], T.hl[:, 256 * m:256 * m + 256]) for m in range(32)], ["IDN", "hl"], ["B4"], 32 * 256)
+    add({"s": vc(256), "v": vc(256)}, either(T.F2[:, 0:256], T.B4[:, 0:256]), (), ["B4", "F2a"])
+    dma("y", T.yg[:], T.F2[:, 0:256], "outs", ["F2a"], (), 131072)
+    for h in range(2):
+        S, k = SM[h], lambda s_, h=h: s_ + str(h)
+        cp(T.F2[:, 256 + 128 * h:384 + 128 * h], T.TI[:, 128 * h:128 * h + 128], [k("TI")], [k("yt")], 128)
+        ts(S[:, 72:80], S[:, 72:80], -float(ST), None, A.add, None, [k("D")], [k("D")])
+        cp(T.FL[:, 64 * h:64 * h + 64], S[:, 16:80], [k("D"), k("V"), k("X")], [k("FL")])
+        for u in range(2):
+            gat(T.FO[:, 512 * u:512 * u + 512], T.ID[:, 0:NV].indirect(T.FL[:, 64 * h + 32 * u:64 * h + 32 * u + 32]),
+                [k("FL"), "ID0", "ID1"], ["FO%d" % u], 512)
+            for f in range(4 * u, 4 * u + 4):
+                src = T.FO[0:128:16, 128 * f:128 * f + 128]
+                ln = slice(128 * h, 128 * h + 128)
+                if f < 3:
+                    out = T.yvp[8 * f + 8:8 * f + 16, ln]
+                elif f < 6:
+                    out = T.yact[8 * f - 24:8 * f - 16, ln]
+                elif f == 6:
+                    out = T.yvp[0:8, ln]
+                else:
+                    out, src = T.ydep[0:1, ln], T.FO[0:1, 896:1024]
+                dma(qs[f % 2] if h else "y", out, src, "outs" if h else "out0", ["FO%d" % u], (), 4096)
+    dma("y", T.yt[:], T.F2[:, 256:512], "outs", ["yt0", "yt1"], (), 131072)
+    return ops, groups
+
+
+def order(ops, groups):
+    n = len(ops)
+    deps = []
+    for i, o in enumerate(ops):
+        d = set()
+        for j in o["deps"]:
+            d.update(groups[ops[j]["sem"]] if ops[j]["kind"] == "dma" else [j])
+        assert i not in d
+        deps.append(d)
+    users = [[] for _ in range(n)]
+    for i in range(n):
+        for j in deps[i]:
+            users[j].append(i)
+    left = [len(d) for d in deps]
+    seq, cnt = [i for i in range(n) if left[i] == 0], list(left)
+    for i in seq:
+        for u in users[i]:
+            cnt[u] -= 1
+            if cnt[u] == 0:
+                seq.append(u)
+    assert len(seq) == n
+    prio = [0.0] * n
+    for i in reversed(seq):
+        c = min(ops[i]["cost"].values()) + (DLAT + ops[i]["bytes"] / DBW if ops[i]["kind"] == "dma" else SYNC)
+        prio[i] = c + ops[i]["boost"] + max([prio[u] for u in users[i]], default=0.0)
+
+    def gap(line, at, c):
+        lo, hi = 0, len(line)
+        while lo < hi:
+            mid = (lo + hi) // 2
+            if line[mid][1] <= at:
+                lo = mid + 1
+            else:
+                hi = mid
+        while lo < len(line) and line[lo][0] < at + c - 1e-9:
+            at = max(at, line[lo][1])
+            lo += 1
+        return at, lo
+
+    def sweep(before, later, key, fixed, back):
+        left = [len(d) for d in before]
+        ready = [i for i in range(n) if left[i] == 0]
+        lines = {e: [] for e in "vspgyL"}
+        eng, start, done = [None] * n, [0.0] * n, [0.0] * n
+        while ready:
+            i = min(ready, key=key.get)
+            ready.remove(i)
+            o, best = ops[i], None
+            wire = o["bytes"] / DBW if o["kind"] == "dma" else 0.0
+            for e, c in o["cost"].items():
+                if fixed is not None and e != fixed[i]:
+                    continue
+                at = max([done[j] + (SAME if eng[j] == e else SYNC) for j in before[i]], default=0.0)
+                if wire and back:
+                    a2, p2 = gap(lines["L"], at + DLAT, wire)
+                    lines["L"].insert(p2, (a2, a2 + wire))
+                    at = a2 + wire
+                pos = None
+                if e is not None:
+                    at, pos = gap(lines[e], at, c)
+                if best is None or at + c + (LEAN if e == "v" else 0.0) < best[0] + (LEAN if best[1] == "v" else 0.0):
+                    best = (at + c, e, at, pos)
+            done[i], eng[i], start[i] = best[0], best[1], best[2]
+            if best[1] is not None:
+                lines[best[1]].insert(best[3], (best[2], best[0]))
+            if wire and not back:
+                a2, p2 = gap(lines["L"], done[i], wire)
+                lines["L"].insert(p2, (a2, a2 + wire))
+                done[i] = a2 + wire + DLAT
+            for u in later[i]:
+                left[u] -= 1
+                if left[u] == 0:
+                    ready.append(u)
+        return eng, start, done
+
+    key, best = {i: (-prio[i] - ops[i]["early"], i) for i in range(n)}, None
+    for turn in range(TURNS):
+        eng, start, done = sweep(deps, users, key, None, False)
+        if best is None or max(done) < max(best[2]):
+            best = (eng, start, done)
+        if turn + 1 < TURNS:
+            _e, _s, back = sweep(users, deps, {i: (-done[i], -i) for i in range(n)}, eng, True)
+            key = {i: (-back[i], i) for i in range(n)}
+    eng, start, done = best
+    return sorted(range(n), key=lambda i: (start[i], i)), eng, start, done
+
+
+def rank_program(g, core, T, topo):
+    rank = T.rank_of(core)
+    if rank is None:
+        return
+    ops, groups = record(g, core, T, topo, rank)
+    seq, eng, _start, _done = order(ops, groups)
+    Q = {"v": g.vector, "s": g.scalar, "p": g.tensor, "g": g, "y": g.sync}
+    count, mark, seen, sent = {e: 0 for e in "vspg"}, {}, {e: {} for e in Q}, 0
+    for i in seq:
+        o, e = ops[i], eng[i]
+        if o["kind"] == "recv":
+            mark[i] = (o["sem"], o["val"])
+            continue
+        need = {}
+        for d, hard in o["deps"].items():
+            if ops[d]["kind"] == "c" and eng[d] == e and not hard:
+                continue
+            sem, v = mark[d] if ops[d]["kind"] != "dma" else (ops[d]["sem"], 16 * len(groups[ops[d]["sem"]]))
+            need[sem] = max(need.get(sem, 0), v)
+        for sem, v in need.items():
+            if seen[e].get(sem, 0) < v:
+                Q[e].wait_ge(T.sem[sem], v)
+                seen[e][sem] = v
+        ins = o["fn"](e)
+        if o["kind"] == "c":
+            count[e] += 1
+            ins.then_inc(T.sem["c" + e], 1)
+            mark[i] = ("c" + e, count[e])
+        elif o["kind"] == "dma":
+            ins.then_inc(T.sem[o["sem"]], 16)
+        else:
+            sent += o["val"]
+    ends = {"c" + e: v for e, v in count.items()}
+    ends.update({sem: 16 * len(m) for sem, m in groups.items()})
+    ends.update({o["sem"]: o["val"] for o in ops if o["kind"] == "recv"})
+    ends["sent"] = sent
+    for sem, v in ends.items():
+        if not any(seen[e].get(sem, 0) >= v for e in Q):
+            g.wait_ge(T.sem[sem], v)

@@ -1,23 +1,29 @@
-from concourse.mybir import AluOpType, AxisListType, ActivationFunctionType
+from concourse.mybir import AluOpType, ActivationFunctionType
 
 A = AluOpType
 F = ActivationFunctionType
-ST, L, W, NV = 6, 256, 4096, 1024
-MG = 128
-HALF = MG + 8 * W
-SHARE = {(3, 0): "xx", (3, 1): "sv", (3, 2): "x", (3, 3): "xx", (2, 0): "x", (2, 1): "xx", (2, 2): "sv", (2, 3): "ssxx",
-         (1, 0): "ssss", (1, 1): "ssxx", (1, 2): "ss", (1, 3): "xxxx"}
-SMALL = {"ar": "s", "a3": "x", "Gf": "s", "Gh": "x", "val": "s", "k1": "s"}
-BANKS = [("B5", "B6", "B7", "B7"), ("B0", "B1", "B2", "B3")]
-CH = [(0, 32), (32, 96), (128, 64), (192, 64)]
-FP = 96
-EARLY = {(2, 0): 2.0, (3, 0): 1.3, ("f", 2): 4.5, "wide": 0.3, ("w", 1): 3.2, ("s", 1): -0.1, (1, 2): 2.8, ("w", 0): 9.1,
-         ("f", 0): 1.8, ("v", 1): 0.1, (3, 1): 4.7, ("r", 1): 8.9, (2, 2): 0.7, ("e", 1): -2.5, ("r", 0): 11.2, (1, 0): 5.4,
-         ("e", 0): -1.5, ("pre", 0): 2.3, ("f", 1): 9.3, ("pre", 1): 2.0, (1, 1): 19.7, ("f", 3): 8.5, ("z", 1): 3.2,
-         ("s", 0): -0.1, ("z", 0): 2.2, (2, 3): 11.3, (1, 3): -0.8, (3, 3): 0.9, "conv": 1.1}
-LIFT = {"small": 35.0, "gloss": 3.0, "pattern": 100.0, "cases": 16.0, "state": 20.0, "digits": 12.0, "rest": 16.0}
-FILL = {"v": 14, "s": 13, "g": 5}
-BF, F32, I32, U16 = "bfloat16", "float32", "int32", "uint16"
+ST = 6
+L, W, NV = 256, 4096, 1024
+M = 128
+BIG = 131072.0
+BATCH = [[64, 64], [64, 64]]
+PIECE = {}
+FILL = {"v": 27, "s": 24, "g": 1, "a": 11}
+LATE = {"v": 0.3, "a": 0.3, "b": 0.3}
+HANDS = "a"
+LOT = 2
+TWICE = []
+DIRECT = [1]
+BACK = 4
+ZEROS = ("tab", M + 1024 * 63, M + 1024 * 64)
+SETS = [("B0", "B1", "B2"), ("B3", "B4", "B5")]
+STATE = [("B7", "B2", "B0"), ("B3", "B5", "B6")]
+HOME = ["B0", "B1", "B2", "B6"]
+AWAY = ["B4", "B5", "B6", "B3"]
+BF, F16, F32, I32, U16 = "bfloat16", "float16", "float32", "int32", "uint16"
+MATS = ["IDN", "BDB", "PFB", "UP", "UN", "UPB", "LA3", "LA2", "LA1", "NLA", "QK", "QA", "QB", "BD0", "BD8", "gm",
+        "MA", "NA", "MB", "NB", "M0", "M1", "M2", "MO", "NE6", "LV", "LV1", "LV2", "L31", "L32"]
+NB_ = len(BATCH)
 
 
 def sb(n, dt):
@@ -25,541 +31,653 @@ def sb(n, dt):
 
 
 SCRATCH = {
-    "tab": sb(16 * W + 2 * MG, BF), "gin": sb(2048, I32), "hl": sb(2 * W + 2 * MG, BF), "ex2": sb(W, BF), "G1": sb(W, BF),
-    "G": sb(W, BF), "fa": sb(W, BF), "rf": sb(NV, I32), "ID": sb(1040, F32), "FO": sb(1040, F32),
-    "F2": sb(512, F32), "RI": sb(256, I32), "NI": sb(256, I32), "CN": sb(512, BF), "CNI": sb(1536, BF),
-    "ci": sb(8, I32), "cf": sb(32, F32), "pw": sb(64, F32), "m2": sb(16, F32),
-    "CT": sb(144, BF), "CK": sb(144, BF), "C1": sb(144, BF), "CC": sb(144, BF), "km": sb(144, BF), "gm": sb(128, BF),
-    "IDN": sb(128, BF), "D01": sb(128, BF), "D2": sb(128, BF), "BDK": sb(128, BF), "BDB": sb(128, BF),
-    "BDW": sb(128, BF), "BD0": sb(128, BF), "BD8": sb(128, BF), "UP": sb(128, BF), "UN": sb(128, BF),
-    "t1": sb(128, BF), "t2": sb(128, BF), "nthr": sb(128, BF), "M16": sb(32, BF),
-    "NE": sb(768, BF), "c256": sb(32, BF), "AT": sb(16, BF), "J4": sb(192, I32), "J6": sb(288, I32),
-    "base": sb(16, F32), "CB": sb(144, BF), "RL": sb(8, U16),
-    "RO": sb(ST * 320, U16), "RQ": sb(ST * 288, U16), "PO": sb(ST * 48, I32), "PI": sb(ST * 32, I32),
-    "AR": sb(768, BF), "R0": sb(128, I32), "O3": sb(256, U16), "O2": sb(256, U16), "TU": sb(256, U16), "TI": sb(256, U16),
-    "vl": sb(16, U16), "FL": sb(128, U16), "SM0": sb(80, I32), "SM1": sb(80, I32), "W0": sb(200, I32), "W1": sb(200, I32),
-    "sg0": sb(128, BF), "isf0": sb(256, BF), "fl0": sb(16, U16), "Gf0": sb(256, BF), "kr0": sb(128, U16), "kc": sb(16, F32),
-    "sg1": sb(128, BF), "isf1": sb(256, BF), "fl1": sb(16, U16), "Gf1": sb(256, BF), "kr1": sb(128, U16), "val": sb(256, BF), "md": sb(256, BF), "nm": sb(256, BF), "kept": sb(256, BF),
-    "Q0": sb(128, F32), "Q1": sb(128, F32), "of": sb(32, U16),
+    "tab": sb(16 * W + 2 * M + 16, BF), "gin": sb(1536, I32), "hl": sb(2 * W + M + 16, BF), "ex2": sb(W, BF), "G1": sb(W, BF),
+    "G": sb(W, BF), "fa": sb(W, BF), "DIG": sb(W + 16, BF), "RF": sb(NV + 8, F32),
+    "CN": sb(512, BF), "CNI": sb(1536, BF), "ZZ": sb(144, BF), "NE": sb(896, BF),
+    "ci": sb(8, I32), "cf": sb(32, F32), "pw": sb(48, F32), "ID": sb(144, F32), "km": sb(144, BF),
+    "CT": sb(144, BF), "C1": sb(144, BF), "CC": sb(144, BF),
+    "ID32": sb(128, F32), "BD16": sb(128, F16), "NB16": sb(128, F16), "RS": sb(128, F32), "B16": sb(2 * L, F16),
+    "ODK": sb(256, BF), "OD2": sb(256, BF), "OD3": sb(256, BF), "OD5": sb(256, BF), "c256": sb(64, BF),
+    "S": sb(2 * L, BF), "SQ": sb(L, BF), "RO": sb(ST * 2 * L, U16), "RQ": sb(ST * 2 * L, U16),
+    "PO": sb(ST * 8 * NB_, U16), "PI": sb(ST * 8 * NB_, U16), "O2": sb(L, U16), "TU": sb(L, U16), "TI": sb(L, U16),
+    "vl": sb(16, U16), "fl": sb(32, U16), "of": sb(32, U16),
+    "EF": sb(2 * L, F32), "KC": sb(L + 4, F32), "SC": sb(L, F32), "SD": sb(L, F32),
+    "sg": sb(L, BF), "isf": sb(2 * L, BF), "GF": sb(2 * L, BF), "R1": sb(L, BF), "R2": sb(L, BF),
 }
+for _m in MATS:
+    SCRATCH[_m] = sb(128, BF)
 for _b in range(8):
     SCRATCH["B%d" % _b] = ("psum", [128, 512], F32)
-
-SEMAPHORES = (["cv", "cs", "cp", "cg", "sent", "small", "drf", "dfa", "perm", "back", "outs", "out0"]
-              + ["gl%d" % i for i in range(8)] + ["cn%d" % i for i in range(3)] + ["ti%d" % i for i in range(2)]
-              + ["rq%d_%d" % (t, c) for t in range(ST) for c in range(4)]
-              + ["rs%d_%d" % (t, h) for t in range(ST) for h in range(2)])
+NCH = sum(len(b) for b in BATCH)
+SEMAPHORES = (["cv", "cs", "cp", "cg", "sent", "small", "drf", "dfa", "dig", "perm", "back", "outs", "out0"]
+              + ["gl%d" % i for i in range(8)] + ["cn%d" % i for i in range(3)] + ["ti%d" % i for i in range(len(BATCH))]
+              + ["rq%d_%d" % (t, c) for t in range(ST) for c in range(NCH)]
+              + ["fill%s%d" % (e, i) for e in HANDS for i in range(-(-FILL[e] // LOT))] + ["cases", "zeros", "gave"] + ["rs%d_%d" % (t, h) for t in range(ST) for h in range(len(BATCH))])
 
 CY, PCY = 1.04e-3, 0.52e-3
-GA, SC, TURNS, LEAN = 1.56, 3.8, 1, 0.2
-HOP, SYNC, SAME, DLAT, DBW = 3.0, 0.15, 0.08, 2.0, 250e3
+GA, SC = 1.25, 3.05
+LOOK = 477.59
+DELAY = 0.0
+HOP, SYNC, SAME, DLAT, DBW = 2.1, 0.15, 0.15, 1.6, 210e3
+ISSUE, ROW, RBW = 0.7, 0.04, 12e3
+LIFT = {'zeros': 93.0, 'gloss': 51.9, 'digits': 12.3, 'small': 7.0, 'cases': 16.3, 'late': -50.9, 'wide0': -25.0, 'wide': -15.2, 'back': 13.1, 'a0': 3.9, 'v0': 1.0, 's0': -0.5, 'u0': -3.8, 'r0': -0.5, 't30': -8.3, 't20': 12.0, 'g30': 5.3, 'g20': -0.1, 't10': 13.2, 'g10': -7.7, 's1': -2.3, 'u1': 0.6, 'r1': 5.9, 'a1': 1.2, 't12': -2.9, 't13': -5.2, 'e0': -2.4, 'k0': -1.5, 'o0': -1.9, 'z0': 5.5, 'w0': -9.1, 't21': -3.5, 'n0': 1.9, 'g31': 1.5, 'n2': 5.8, 'g33': 4.5, 'x2': 6.9, 'n1': -0.3, 'x1': 1.4, 'k1': -1.3, 'f2': 3.2, 'f1': -6.1, 'g13': -5.1, 'g21': -5.1, 'v1': 4.5, 'g11': 0.9, 'e1': -1.2, 't33': -2.7, 't11': 6.4, 't22': 6.1, 'z1': -0.8, 'g22': -3.9, 't23': 3.6, 'g32': 6.0, 'n3': 5.0, 'g23': -6.9, 'x3': 1.7, 'x0': 5.5, 'g12': 8.7, 'p1': -4.4, 'p0': -3.8, 'o1': 3.1, 'b1': 8.6, 'h0': -1.6, 'q1': -2.6, 't31': 0.7, 'b0': 6.7, 'h1': 3.5, 't32': -0.6, 'f0': -1.0, 'q0': -6.9, 'f3': -1.9, 'w1': -6.4, 'W1': 16.3, 'H1': -20.0, 'S0': -7.7, 'Z1': -2.5, 'W0': -9.4, 'U1': 8.5, 'perm': -9.5, 'S1': 17.3, 'E0': -20.4, 'out': -9.4, 'state': -20.3, 'Z0': 2.8, 'U0': -4.7, 'const': -0.1, 'fill': -12.3, 'E1': -0.2, 'A0': 10.4, 'A1': 7.4, 'rest': 10.5, 'H0': 3.1}
+WHO = {'v0': 'x', 'v1': 'x', 'h0': 'v', 'h1': 's', 's0': 'ssx', 's1': 'xss', 'u0': 's', 'u1': 'vs', 'r0': 's', 'x0': 's', 'x1': 's', 'x2': 'v', 'x3': 's', 'g12': 'xx', 'g13': 'ss', 'H0': 'x', 'H1': 's', 'S0': 'xxs', 'S1': 'xsx', 'U0': 's', 'U1': 'v', 'g30': 'sv', 'g20': 'xx', 'g10': 'sv', 'g11': 'xv', 'g33': 'xx', 'g32': 'xv', 'g22': 'sx', 'g31': 'vx', 'g21': 'vs', 'g23': 'sv'}
+SIZE = {BF: 2, F16: 2, U16: 2, F32: 4, I32: 4}
+
+
+def R(name, c0=0, c1=None, cs=1, p0=0, p1=128, ps=1):
+    return (name, p0, p1, ps, c0, SCRATCH[name][1][1] if c1 is None else c1, cs)
+
+
+def ind(win, off):
+    return ("ind", win, off)
+
+
+def width(a):
+    return 16 * width(a[2]) if a[0] == "ind" else len(range(a[4], a[5], a[6]))
+
+
+def meet(a, b, block):
+    if a[3] == 1 and b[3] == 1:
+        if a[2] <= b[1] or b[2] <= a[1]:
+            return False
+    elif not set(range(a[1], a[2], a[3])) & set(range(b[1], b[2], b[3])):
+        return False
+    if block:
+        return a[4] // block <= (b[5] - 1) // block and b[4] // block <= (a[5] - 1) // block
+    if a[5] <= b[4] or b[5] <= a[4]:
+        return False
+    return not (a[6] == b[6] and (a[4] - b[4]) % a[6])
+
+
+def helpers(core, ranks, topo):
+    return [c for c in topo.cores_of(core) if c not in ranks and topo.die(c) == topo.die(core)][:len(HANDS)]
+
+
+def helped(core, ranks, topo):
+    for c in ranks:
+        if core in helpers(c, ranks, topo):
+            return c
+    return None
+
+
+def fillers():
+    due = sorted([((j + 1.0) / n * (1 - LATE.get(e, 0.0)) + LATE.get(e, 0.0), e) for e, n in FILL.items() for j in range(n)])
+    pieces = [4 * a + 2 * u + w for u in range(2) for a in range(16) for w in range(2)]
+    return [(j, e) for j, (_d, e) in zip(pieces[:-1], due)]
 
 
 def record(g, core, T, topo, rank):
     n_ranks = len(T.cores)
-    ops, lastw, readers, groups, boost, tag = [], {}, {}, {}, [0.0], [None]
+    ops, seen, groups, tag, nth, step, hold = [], {}, {}, [None], {}, [-1], []
+
+    def ap(a):
+        if not isinstance(a, tuple):
+            return a
+        if a[0] == "ind":
+            return ap(a[1]).indirect(ap(a[2]))
+        return T[a[0]][slice(a[1], a[2], a[3] if a[3] > 1 else None), slice(a[4], a[5], a[6] if a[6] > 1 else None)]
 
     def add(cost, fn, r=(), w=(), kind="c", sem=None, val=0, after=(), nbytes=0):
-        i = len(ops)
-        deps = {}
-        for k in r:
-            for d in lastw.get(k, ()):
-                deps[d] = True
-        for k in w:
-            hard = k[0] != "B" or not k[1:].isdigit()
-            for d in list(lastw.get(k, ())) + readers.get(k, []):
-                deps[d] = deps.get(d, False) or hard
-        for d in after:
-            deps[d] = True
-        for k in r:
-            readers.setdefault(k, []).append(i)
-        for k in w:
-            lastw[k] = [i]
-            readers[k] = []
+        i, deps, acc = len(ops), {d: True for d in list(after) + hold}, []
+        for lst, wr in ((r, False), (w, True)):
+            for a in lst:
+                if isinstance(a, tuple):
+                    acc += [(a[1], wr), (a[2], False)] if a[0] == "ind" else [(a, wr)]
+        for a, wr in acc:
+            old = seen.setdefault(a[0], [])
+            if SCRATCH[a[0]][0] == "psum":
+                for _a, d, _w in old:
+                    if d != i:
+                        deps[d] = deps.get(d, False)
+                seen[a[0]] = [(a, i, True)]
+                continue
+            for b, d, w2 in old:
+                unlike = wr and w2 and d != i and (ops[d]["kind"] == "c") != (kind == "c")
+                if d != i and (wr or w2) and meet(a, b, 16 // SIZE[SCRATCH[a[0]][2]] if unlike else 0):
+                    deps[d] = True
+            if wr and a[3] == 1 and a[6] == 1:
+                old[:] = [x for x in old if x[1] == i or not (a[1] <= x[0][1] and x[0][2] <= a[2] and a[4] <= x[0][4] and x[0][5] <= a[5])]
+            old.append((a, i, wr))
         ops.append({"cost": cost, "fn": fn, "deps": deps, "kind": kind, "sem": sem, "val": val, "bytes": nbytes,
-                    "boost": boost[0], "early": EARLY.get(tag[0], 0.0), "tag": tag[0]})
+                    "tag": tag[0].upper() if step[0] == ST - 1 and len(tag[0]) == 2 and tag[0][0] in "ahzwesu" else tag[0], "w": [a[0] for a, wr in acc if wr][:1], "nth": nth.get(tag[0], 0), "step": step[0]})
+        nth[tag[0]] = nth.get(tag[0], 0) + (len(cost) > 1)
         if kind == "dma":
             groups.setdefault(sem, []).append(i)
         return i
 
-    def users(*keys):
-        return [d for k in keys for d in list(lastw.get(k, ())) + readers.get(k, [])]
+    def narrow(*a):
+        return all(SIZE[SCRATCH[x[0]][2]] == 2 for x in a)
 
-    def wrote(ids, *keys):
-        for k in keys:
-            lastw[k] = ids
-            readers[k] = []
+    def vcost(out, *ins, rate=None):
+        if out[0] == "ind":
+            return 0.05 + width(out) * SC * CY
+        if ins and ins[0][0] == "ind":
+            return 0.05 + width(out) * GA * CY
+        return max(64.0, width(out) * (rate or (0.5 if narrow(out, *ins) else 1.0))) * CY
 
-    def vc(n, rate=1.0):
-        return max(64.0, n * rate) * CY
-
-    def ts(out, in0, s1, s2, o0, o1, r, w, n=64, rate=1.0, after=()):
-        if o1 is None:
-            return add({"v": vc(n, rate)}, lambda e: g.vector.tensor_scalar(out, in0, s1, None, o0), r, w, after=after)
-        return add({"v": vc(n, rate)}, lambda e: g.vector.tensor_scalar(out, in0, s1, s2, o0, o1), r, w, after=after)
-
-    def tt(out, in0, in1, op, r, w, n=32, rate=2.0):
-        return add({"v": vc(n, rate)}, lambda e: g.vector.tensor_tensor(out, in0, in1, op), r, w)
-
-    def ttg(out, in0, in1, op, r, w, n, rate=None, after=()):
-        return add({"v": 0.06 + n * (rate or GA) * CY}, lambda e: g.vector.tensor_tensor(out, in0, in1, op), r, w, after=after)
-
-    def cp(out, in_, r, w, n=64, rate=1.0):
-        return add({"v": vc(n, rate)}, lambda e: g.vector.tensor_copy(out, in_), r, w)
-
-    def either(out, in_):
-        return lambda e: g.vector.tensor_copy(out, in_) if e == "v" else g.scalar.activation(out, in_, F.Copy)
+    def scost(out, in_):
+        return 0.065 + width(out) * GA * CY if in_[0] == "ind" else max(64.0, width(out)) * CY
 
     def only(cost, who):
         return cost if who == "x" else {who: cost[who]}
 
-    def gat(out, in_, r, w, n, who="x", after=()):
-        return add(only({"v": 0.06 + n * GA * CY, "s": 0.08 + n * GA * CY}, who), either(out, in_), r, w, after=after)
+    def ts(out, in0, s1, s2=None, o0=A.add, o1=None):
+        more = () if o1 is None else (o1,)
+        return add({"v": vcost(out, in0)}, lambda e: g.vector.tensor_scalar(ap(out), ap(in0), ap(s1), ap(s2), o0, *more), [in0, s1, s2], [out])
 
-    def act(out, in_, func, bias, r, w, n):
-        return add({"s": vc(n)}, lambda e: g.scalar.activation(out, in_, func, bias=bias), r, w)
+    def tt(out, in0, in1, op):
+        rate = 1.0 if "psum" in (SCRATCH[in1[0]][0], SCRATCH.get(in0[0], "-")[0]) else 2.0
+        return add({"v": vcost(out, in0, rate=rate)}, lambda e: g.vector.tensor_tensor(ap(out), ap(in0), ap(in1), op), [in0, in1], [out])
 
-    def ms(ap, c, w, n=64):
-        return add({"v": vc(n)}, lambda e: g.vector.memset(ap, c), (), w)
+    def cp(out, in_, who="v"):
+        fn = lambda e: g.vector.tensor_copy(ap(out), ap(in_)) if e == "v" else g.scalar.activation(ap(out), ap(in_), F.Copy)
+        return add(only({"v": vcost(out, in_), "s": scost(out, in_)}, who), fn, [in_], [out])
 
-    def io(out, pat, base, cm, w, n, small=True):
-        if small:
-            fn = lambda e: g.iota(out, pat, base, cm, allow_small_or_imprecise_dtypes=True)
-        else:
-            fn = lambda e: g.iota(out, pat, base, cm)
-        return add({"g": 0.16 + 2 * n * CY}, fn, (), w)
+    def relu(out, in_, bias, who="x"):
+        fn = lambda e: (g.vector.tensor_scalar(ap(out), ap(in_), ap(bias), 0.0, A.add, A.max) if e == "v"
+                        else g.scalar.activation(ap(out), ap(in_), F.Relu, bias=ap(bias)))
+        return add(only({"v": vcost(out, in_), "s": scost(out, in_)}, who), fn, [in_, bias], [out])
 
-    def mm(parts, r, w, cyc, first=True, final=True):
+    def scan(out, d0, d1):
+        return add({"v": vcost(out, rate=1.0)}, lambda e: g.vector.tensor_tensor_scan(ap(out), ap(d0), ap(d1), 0.0, A.max, A.min), [d0, d1], [out])
+
+    def ms(out, c):
+        return add({"v": vcost(out)}, lambda e: g.vector.memset(ap(out), c), (), [out])
+
+    def io(out, pat, base, cm):
+        kw = {} if SCRATCH[out[0]][2] == I32 else {"allow_small_or_imprecise_dtypes": True}
+        return add({"g": 0.14 + 2 * width(out) * CY}, lambda e: g.iota(ap(out), pat, base, cm, **kw), (), [out])
+
+    def aff(out, in_, pat, op, fill, base, cm):
+        return add({"g": 0.18 + 2 * width(out) * CY}, lambda e: g.affine_select(ap(out), ap(in_), pat, op, fill, base, cm), [in_], [out])
+
+    def mm(parts, first=True, final=True):
         def fn(e):
             ins = None
             for j, (o, lt, rh) in enumerate(parts):
-                ins = g.tensor.matmul(o, lt, rh, first and j == 0, final and j == len(parts) - 1)
+                ins = g.tensor.matmul(ap(o), ap(lt), ap(rh), first and j == 0, final and j == len(parts) - 1)
             return ins
-        return add({"p": cyc * PCY}, fn, r, w)
+        cyc = sum(max(64, width(rh)) * (4 if SCRATCH[rh[0]][2] == F32 else 1) for o, lt, rh in parts)
+        return add({"p": cyc * PCY}, fn, [x for p_ in parts for x in p_[1:]], [parts[0][0]])
 
-    def dma(q, out, in_, sem, r, w, nbytes, after=()):
+    def dma(q, out, in_, sem, nbytes, after=()):
         eng = g.sync if q == "y" else g.scalar
-        return add({q: 0.1}, lambda e: eng.dma_start(out, in_), r, w, kind="dma", sem=sem, nbytes=nbytes, after=after)
+        return add({q: 0.08}, lambda e: eng.dma_start(ap(out), ap(in_)), [in_], [out], kind="dma", sem=sem, nbytes=nbytes, after=after)
 
-    def send(out, in_, peer, src, sem, r, w, extra=0.0):
+    def send(out, in_, peer, src, sem, after=()):
         dst = T.cores[peer]
         assert topo.may_write(core, dst)
         rid, pid, _se = topo.addr(dst)
         m = topo.mask(core, dst)
-        i = add({"g": 0.5}, lambda e: g.remote_dma(out, in_, T.sem[sem], T.sem.sent, pid, rid, m), r, (), kind="rem",
-                val=len(topo.engines(core, dst)))
-        add({None: HOP + extra}, None, (), w, kind="recv", sem=sem, val=len(topo.engines(T.cores[src], core)), after=[i])
+        i = add({"g": ISSUE}, lambda e: g.remote_dma(ap(out), ap(in_), T.sem[sem], T.sem.sent, pid, rid, m), [in_], (), kind="rem",
+                val=len(topo.engines(core, dst)), after=after)
+        add({"R": 16 * (ROW + 2 * width(out) / RBW)}, None, (), [out], kind="recv", sem=sem, val=len(topo.engines(T.cores[src], core)), after=[i])
 
-    col = lambda j: T.cf[:, j:j + 1]
-    slide = lambda C, x: C[:, 15 - x:143 - x]
-    win = T.tab[:, MG:MG + 16 * W]
-    SM, WK, QQ = [T.SM0, T.SM1], [T.W0, T.W1], [T.Q0, T.Q1]
-    EXP = [(T.hl, 0, "hi"), (T.hl, W, "lo"), (T.ex2, 0, "ex2")]
+    col = lambda j, p0=0, p1=128: R("cf", j, j + 1, 1, p0, p1)
+    slide = lambda C, x: R(C, 15 - x, 143 - x)
+    win = R("tab", M, M + 16 * W)
+    EXP = [("ex2", 0), ("hl", W), ("ex2", 0), ("hl", 0), ("hl", W), ("ex2", 0)]
+    batches, chunks, l0 = [], [], 0
+    for b in BATCH:
+        batches.append((l0, sum(b), list(range(len(chunks), len(chunks) + len(b)))))
+        for n in b:
+            chunks.append((l0, n))
+            l0 += n
 
     def load_gloss(c):
-        dma("y", T.gin[:, 512 * (c % 4):512 * (c % 4) + 512], T.gloss[:, 512 * c:512 * c + 512], "gl%d" % c, (), ["gin%d" % (c % 4)], 262144)
+        dma("y", R("gin", 512 * (c % 3), 512 * (c % 3) + 512), T.gloss[:, 512 * c:512 * c + 512], "gl%d" % c, 262144)
 
-    boost[0] = LIFT["small"]
-    dma("s", T.RI[8:40, :], T.vp0[:], "small", (), ["RIa"], 32768)
-    dma("s", T.RI[40:64, :], T.act0[:], "small", (), ["RIb"], 24576)
-    for j in range(8):
-        dma("s", T.RI[j:j + 1, :], T.dep0[:], "small", (), ["RI%d" % j], 1024)
-    dma("s", T.CN[:, 0:256], T.cases[:], "small", (), ["CNa"], 65536)
-    dma("s", T.NI[0:6, :], T.need[:], "small", (), ["NI"], 6144)
-    boost[0] = LIFT["gloss"]
-    for c in range(4):
+    tag[0] = "gloss"
+    for c in range(3):
         load_gloss(c)
-    boost[0] = 0.0
 
-    io(T.ci[:, 0:1], [[0, 1]], 0, 1, ["p"], 1, False)
-    io(T.ID[:, 0:144], [[1, 144]], 0, 0, ["ID0"], 144)
-    io(T.km[:], [[0, 9], [1, 16]], 0, 0, ["km"], 144)
-    io(T.gm[:], [[16, 8], [0, 16]], 0, 0, ["gm"], 128)
-    io(T.ID[:, 144:1040], [[1, 896]], 144, 0, ["ID1"], 896)
-    io(T.NE[0:32, :], [[1, 6], [0, 128]], 0, -1, ["NE"], 768)
-    io(T.c256[:, 0:16], [[0, 2], [256, 8]], 0, 0, ["c256"], 16)
-    ms(T.c256[:, 16:24], 1.0, ["one"])
-    io(T.AT[:], [[4096, 16]], 0, 0, ["AT"], 16)
-    io(T.base[:, 0:16], [[0, 2], [16, 8]], 0, 0, ["base"], 16)
-    io(T.J4[:], [[1, 6], [1, 4], [0, 8]], 0, 0, ["J4"], 192, False)
-    for t in range(ST):
-        io(T.J6[:, 48 * t:48 * t + 48], [[0, 2], [1, 3], [0, 8]], 1 + t, 0, ["J6%d" % t], 48, False)
-    p = T.ci[:, 0:1]
-    ts(T.ci[:, 1:2], p, 15, None, A.bitwise_and, None, ["p"], ["ki"])
-    ts(T.ci[:, 2:3], p, 7, None, A.bitwise_and, None, ["p"], ["xi"])
-    ki, xi = T.ci[:, 1:2], T.ci[:, 2:3]
-    K, NK, GB15, P16, WT, WKK, K1, M2, M3, NWT, X16, GB, PW2, PF, LT8, XF, K0, K8 = range(18)
-    cp(col(K), ki, ["ki"], ["k"])
-    ts(col(M3), ki, 3.0, None, A.is_equal, None, ["ki"], ["m3"])
-    ts(col(M2), ki, 2.0, None, A.is_equal, None, ["ki"], ["m2c"])
-    ms(T.pw[:, 16:32], 0.5, ["half"])
-    add({"v": vc(64)}, lambda e: g.vector.tensor_tensor_scan(T.pw[:, 0:16], T.pw[:, 16:32], T.pw[:, 16:32], 65536.0, A.mult, A.max),
-        ["half"], ["pw"])
-    ts(T.m2[:], T.pw[:, 0:16], col(M2), None, A.mult, None, ["pw", "m2c"], ["m2"])
-    ts(T.G1[:, 0:64], T.ID[:, 0:64], col(M3), None, A.mult, None, ["ID0", "m3"], ["G10", "G11"])
-    boost[0] = LIFT["pattern"]
-    for i in range(6):
-        w_ = 64 << i
-        ts(T.G1[:, w_:2 * w_], T.G1[:, 0:w_], T.m2[:, 9 - i:10 - i], None, A.add, None, ["G10", "G11", "m2"],
-           ["G10", "G11"] if i < 5 else ["G12", "G13"], w_, 0.5)
-    boost[0] = 0.0
-    ts(col(NK), ki, -1.0, None, A.mult, None, ["ki"], ["nk"])
-    ts(col(GB), p, col(K), None, A.subtract, None, ["p", "k"], ["gb"])
-    ts(col(GB15), p, col(K), 15.0, A.subtract, A.add, ["p", "k"], ["gb15"])
-    ts(col(P16), p, 16.0, 15.0, A.mult, A.add, ["p"], ["p16"])
-    ts(col(WT), xi, 0.0, None, A.is_equal, None, ["xi"], ["wt"])
-    ts(col(NWT), xi, 0.0, None, A.not_equal, None, ["xi"], ["nwt"])
-    ts(col(K0), ki, 0.0, None, A.is_equal, None, ["ki"], ["k0"])
-    ts(col(K8), ki, 8.0, None, A.is_equal, None, ["ki"], ["k8"])
-    tt(col(WKK), col(M2), col(M3), A.add, ["m2c", "m3"], ["wk"])
-    ts(col(K1), ki, 1.0, None, A.add, None, ["ki"], ["k1c"])
-    ts(col(X16), ki, 16.0, -1.0, A.mult, A.add, ["ki"], ["x16"])
-    cp(col(PF), p, ["p"], ["pf"])
-    cp(col(XF), xi, ["xi"], ["xf"])
-    ts(col(LT8), ki, 8.0, 8.0, A.is_lt, A.mult, ["ki"], ["lt8"])
-    ts(T.pw[:, 32:48], T.ID[:, 0:16], col(K), None, A.is_equal, None, ["ID0", "k"], ["pwa"])
-    cp(T.M16[:, 0:16], T.pw[:, 32:48], ["pwa"], ["M16a"])
-    ts(T.M16[:, 16:32], T.ID[:, 0:16], col(K), None, A.not_equal, None, ["ID0", "k"], ["M16b"])
-    tt(T.pw[:, 48:64], T.pw[:, 32:48], T.pw[:, 0:16], A.mult, ["pwa", "pw"], ["pwb"])
-    add({"v": vc(64)}, lambda e: g.vector.tensor_reduce(col(PW2), T.pw[:, 48:64], AxisListType.X, A.add), ["pwb"], ["pw2"])
-    ts(T.nthr[:, 0:16], T.pw[:, 0:16], -2.0, None, A.mult, None, ["pw"], ["nthr"])
-    for w_ in (16, 32, 64):
-        cp(T.nthr[:, w_:2 * w_], T.nthr[:, 0:w_], ["nthr"], ["nthr"])
-    for buf, wc, nm, wn in ((T.CT, WT, "CT", "wt"), (T.CK, WKK, "CK", "wk"), (T.C1, K1, "C1", "k1c")):
-        ts(buf[:], T.ID[:, 0:144], col(GB15), col(wc), A.is_equal, A.mult, ["ID0", "gb15", wn], [nm], 144)
-    ts(T.CC[:], T.km[:], 15.0, None, A.is_equal, None, ["km"], ["CC"], 144, 0.5)
-    ts(T.IDN[:], T.ID[:, 0:128], col(PF), None, A.is_equal, None, ["ID0", "pf"], ["IDN"], 128)
-    ts(T.D01[:], T.IDN[:], col(WT), None, A.mult, None, ["IDN", "wt"], ["D01"])
-    ts(T.D2[:], T.IDN[:], col(NWT), None, A.mult, None, ["IDN", "nwt"], ["D2"])
-    for buf, sc, nm, sn in ((T.BDK, col(WKK), "BDK", "wk"), (T.BDB, 65536.0, "BDB", "gb"), (T.BDW, col(PW2), "BDW", "pw2"),
-                            (T.BD0, col(K0), "BD0", "k0"), (T.BD8, col(K8), "BD8", "k8")):
-        ts(buf[:], T.gm[:], col(GB), sc, A.is_equal, A.mult, ["gm", "gb", sn], [nm])
-    ts(T.t1[:], T.km[:, 0:128], col(K), None, A.is_gt, None, ["km", "k"], ["t1"])
-    ts(T.t2[:], T.km[:, 0:128], col(K), None, A.is_equal, None, ["km", "k"], ["t2"])
-    tt(T.t1[:], T.t1[:], T.t2[:], A.subtract, ["t1", "t2"], ["t1"], 128)
-    ts(T.t2[:], T.gm[:], col(GB), None, A.is_equal, None, ["gm", "gb"], ["t2"])
-    tt(T.UP[:], T.t1[:], T.t2[:], A.mult, ["t1", "t2"], ["UP"], 128)
-    ts(T.UN[:], T.UP[:], -1.0, None, A.mult, None, ["UP"], ["UN"])
-    ts(T.NE[0:32, :], T.NE[0:32, :], 0.0, -1.0, A.is_equal, A.mult, ["NE"], ["NE"], 768, 0.5)
-    ts(T.base[:], T.base[:], col(K), None, A.add, None, ["base", "k"], ["base"])
-    cp(T.c256[:, 24:32], T.base[:, 0:8], ["base"], ["lnb"])
-    ts(T.CB[:], T.CT[:], 65536.0, None, A.mult, None, ["CT"], ["CB"])
-    for j in (0, 1, 4):
-        cp(T.RL[:, j:j + 1], xi, ["xi"], ["RL%d" % j])
-    ts(T.RL[:, 2:3], xi, 8.0, None, A.add, None, ["xi"], ["RL2"])
-    ts(T.RL[:, 3:4], col(LT8), col(XF), None, A.add, None, ["lt8", "xf"], ["RL3"])
-    RLK = ["RL%d" % j for j in range(5)]
-    rep2, rep4, rep6 = T.RL[:, 0:1], T.RL[:, 0:2], T.RL[:, 2:5]
-    ms(T.hl[:, 2 * W:2 * W + 2 * MG], 0.0, ["hlm"], 128)
+    tag[0] = "const"
+    K, NK, NKB, X16, GB, GB15, WT, K1, PF, K4, SA1, SA2, EJ, B1, B2, B3, M0_, M1_, M2_, M3_, KB, C16 = range(22)
+    p, ki = R("ci", 0, 1), R("ci", 1, 2)
+    io(p, [[0, 1]], 0, 1)
+    io(R("ID"), [[1, 144]], 0, 0)
+    io(R("km"), [[0, 9], [1, 16]], 0, 0)
+    io(R("gm"), [[16, 8], [0, 16]], 0, 0)
+    ms(R("ZZ"), 0.0)
+    ts(ki, p, 15, None, A.bitwise_and)
+    ts(R("ci", 2, 3), p, 7, None, A.bitwise_and)
+    ts(R("ci", 3, 4), p, 3, None, A.arith_shift_right)
+    cp(col(K), ki)
+    cp(col(PF), p)
+    ts(col(GB), p, col(K), None, A.subtract)
+    ts(col(GB15), p, col(K), 15.0, A.subtract, A.add)
+    ts(col(WT), R("ci", 2, 3), 0.0, None, A.is_equal)
+    ts(col(EJ), R("ci", 3, 4), -1.0, 12.0, A.mult, A.add)
+    for c, mul, plus in ((NK, -1.0, 0.0), (NKB, -65536.0, -67584.0), (X16, 16.0, -1.0), (K1, 1.0, 1.0), (K4, 4096.0, 0.0)):
+        ts(col(c), ki, mul, plus, A.mult, A.add)
+    for c, k, v in ((M0_, 0, 1.0), (M1_, 1, 1.0), (M2_, 2, 64.0), (M3_, 3, 1.0)):
+        ts(col(c), ki, float(k), v, A.is_equal, A.mult)
+    ts(col(KB), ki, 1.0, -BIG, A.is_ge, A.mult)
+    ts(R("IDN"), R("ID", 0, 128), col(PF), None, A.is_equal)
+    ts(R("ID32"), R("ID", 0, 128), col(PF), None, A.is_equal)
+    for C, w_ in (("CT", col(WT)), ("C1", col(K1))):
+        ts(R(C), R("ID"), col(GB15), w_, A.is_equal, A.mult)
+    ts(R("CC"), R("km"), 15.0, None, A.is_equal)
+    io(col(C16), [[0, 1]], 1, 0)
+    for C, w_ in (("BD16", 1.0), ("NB16", -1.0), ("BDB", BIG), ("PFB", col(KB)), ("BD8", 1.0)):
+        ts(R(C), R("gm"), col(GB), w_, A.is_equal, A.mult)
+    aff(R("BD0"), R("BD8"), [[1, 128]], A.is_ge, 0.0, 0, -1)
+    aff(R("UP"), R("BD0"), [[1, 128]], A.not_equal, -1.0, 0, -1)
+    ts(R("UN"), R("UP"), -1.0, None, A.mult)
+    ts(R("UPB"), R("UP"), 65536.0, None, A.mult)
+    ts(R("NE6"), R("km", 0, 128), col(K), 6 * BIG, A.not_equal, A.mult)
+    ms(R("ODK", 128, 256), 32768.0)
+    for C, o, d in (("ODK", 0, 2 * BIG + 32768), ("OD2", 0, 0.0), ("OD2", 128, BIG), ("OD3", 0, 32768.0), ("OD3", 128, 2 * BIG),
+                    ("OD5", 0, 57344.0), ("OD5", 128, 61440.0)):
+        ts(R(C, o, o + 128), R("NE6"), d)
+    io(R("pw", 32, 40), [[16, 8]], 32769, 0)
+    ms(R("RS"), -1.0)
+    ts(R("RS", 0, 128, 16), R("pw", 32, 40), col(K))
+    ms(R("KC", 0, 4), 60000.0)
+    sizes = sorted(set(n for _l, n, _c in batches))
+    for j, n in enumerate(sizes):
+        io(R("c256", 16 * j, 16 * j + n // 8), [[0, 2], [256, n // 16]], 0, 0)
 
-    ms(T.CN[:, 256:512], 0.0, ["CNb"], 128)
-    cp(T.CN[0:6, 256:512], T.NI[0:6, :], ["NI"], ["CNb"], 256)
-    boost[0] = LIFT["cases"]
-    for s in range(3):
-        send(T.CNI[:, 512 * s:512 * s + 512], T.CN[:], (rank + 1 + s) % n_ranks, (rank - 1 - s) % n_ranks, "cn%d" % s,
-             ["CNa", "CNb"], ["CNI%d" % s], 2.0 + 2.0 * s)
-    boost[0] = 0.0
+    def steps(c, top, lower):
+        io(col(c), [[0, 1]], top, 0)
+        for bound, v in lower:
+            aff(col(c), col(c), [[0, 1]], A.is_ge, float(v), -bound, 1)
 
-    def widen(s):
-        buf, o, key = EXP[s]
-        old = users(key)
-        tag[0] = "wide"
-        wrote([add({"v": vc(128), "s": vc(256)}, either(buf[:, o + k:o + W:16], T.CNI[:, 512 * s:512 * s + 256]),
-                   ["CNI%d" % s], (), after=old) for k in range(16)], key)
+    def lead(name, src, f, v):
+        aff(R(name), R(src, 0, 128), [[-1, 8], [0, 16]], A.not_equal, v, -8 * f, 1)
 
-    ts(T.FO[0:64, 0:1040], T.ID[0:64, :], T.cf[0:64, P16:P16 + 1], None, A.is_equal, None, ["ID0", "ID1", "p16"], ["FO0", "FO1"], 1040)
-    cp(T.F2[0:64, 0:256], T.RI[0:64, :], ["RIa", "RIb"] + ["RI%d" % j for j in range(8)], ["F2a"], 256)
-    for j in range(8):
-        for x0 in range(0, 16, 4):
-            boost[0] = LIFT["state"] if j == 0 and x0 == 0 else 0.0
-            mm([(T.B5[:, 16 * j:16 * j + 16], T.FO[0:64, 128 * j + 15 - x:128 * j + 143 - x], T.F2[0:64, x:256:16])
-                for x in range(x0, x0 + 4)], ["FO0", "FO1", "F2a"], ["B5"], 4 * 256, x0 == 0, x0 == 12)
-    place = [72, 64, 16, 24, 32, 40, 48, 56]
-    for h in range(2):
-        ids = [cp(SM[h][:, place[j]:place[j] + 8], T.B5[:, 16 * j + 8 * h:16 * j + 8 * h + 8], (), ["B5"]) for j in range(8)]
-        wrote(ids[0:1], "D%d" % h)
-        wrote(ids[1:2], "V%d" % h)
-        wrote(ids[2:8], "X%d" % h)
+    def matrix(name, runs, wide=False):
+        done = set()
+        for i0, sl, j0, nj, v in runs + [(99, 0, 0, 16, 0.0)]:
+            j = j0
+            while j < j0 + nj:
+                e = j
+                while e < j0 + nj and (e in done) == (j in done):
+                    e += 1
+                if i0 != 99 or j not in done:
+                    o = R(name, 8 * j, 8 * e)
+                    u = 1 if wide else 8
+                    aff(o, o if j in done else R("ZZ", 0, 8 * (e - j)), [[-u * sl, e - j], [-16 if wide else -1, 8]], A.not_equal, v,
+                        -u * (i0 + sl * (j - j0)) - (999 if i0 == 99 else 0), 1)
+                j = e
+            done.update(range(j0, j0 + nj))
 
-    his, los = [], []
-    boost[0] = LIFT["digits"]
-    for c in range(8):
-        sl, gs, bk = slice(512 * c, 512 * c + 512), slice(512 * (c % 4), 512 * (c % 4) + 512), "B%d" % (c % 4)
-        his.append(cp(T.hl[:, sl], T.gin[:, gs], ["gin%d" % (c % 4)], ["hi%d" % c], 512))
-        mm([(T[bk][:], T.IDN[:], T.hl[:, sl])], ["IDN", "hi%d" % c], [bk], 512)
-        los.append(tt(T.hl[:, W + 512 * c:W + 512 * c + 512], T.gin[:, gs], T[bk][:], A.subtract,
-                      ["gin%d" % (c % 4)], [bk, "lo%d" % c], 512, 1.0))
-        if c < 4:
-            load_gloss(c + 4)
-    boost[0] = LIFT["rest"]
-    dma("y", T.rf[:], T.refs[:], "drf", (), ["rf"], 524288, [los[3]])
-    dma("y", T.fa[:], T.facts[:], "dfa", (), ["fa"], 1048576, [los[3]])
-    boost[0] = 0.0
-    wrote(his + los, "hi", "lo")
-    due = sorted([((j + 1.0) / n + (0.4 if e == "v" else 0.0), e) for e, n in FILL.items() for j in range(n)])
-    perm = []
-    for a in range(16):
-        for u in range(2):
-            e = due[2 * a + u][1]
-            o = T.tab[:, MG + W * a + 2048 * u:MG + W * a + 2048 * u + 2048]
-            i_ = T.G1[:, 2048 * u:2048 * u + 2048]
-            keys = ["G1%d" % (2 * u), "G1%d" % (2 * u + 1)]
-            if e == "g":
-                add({"g": 0.2 + 4096 * CY}, (lambda o, i_: lambda e: g.affine_select(o, i_, [[0, 2048]], A.is_ge, 0.0, 0, 0))(o, i_),
-                    keys, ["tb%d_%d" % (a, u)])
+    steps(SA1, 7, [(88, 0)])
+    steps(SA2, 1, [(88, 99)])
+    for name, f in (("LA3", 10), ("LA2", 9), ("LA1", 8)):
+        lead(name, "ZZ", f, 4096.0)
+    lead("LV", "ZZ", 0, 1.0)
+    lead("LV", "LV", 4, 16.0)
+    lead("NLA", "ZZ", 8, -4096.0)
+    lead("QK", "ZZ", 15, -BIG / 64)
+    lead("QA", "NLA", 11, BIG)
+    lead("QB", "LA1", 11, -BIG)
+    ms(R("CN", L, 2 * L), 0.0)
+    tag[0] = "zeros"
+    ms(R(*ZEROS), 0.0)
+    tag[0] = "const"
+    o = ZEROS[1]
+    aff(R("NE", 0, 896, 1, 0, 32), R("tab", o, o + 896, 1, 0, 32), [[1, 7], [0, 128]], A.not_equal, -1.0, 0, -1)
+
+    def widen(t, name, who):
+        (buf, o), s = EXP[t], t % 3
+        tag[0] = name
+        for k in range(16):
+            out, in_ = R(buf, o + k, o + W, 16), R("CNI", 512 * s, 512 * s + L)
+            if who == "g":
+                aff(out, in_, [[0, L]], A.is_ge, 0.0, 0, 0)
             else:
-                add({e: vc(1024 if e == "v" else 2048)}, either(o, i_), keys, ["tb%d_%d" % (a, u)])
-        perm.append(dma("y", T.tab[0:128:8, MG + W * a:MG + W * a + W], T.hl[a:128:16, 0:2 * W], "perm", ["hi", "lo"],
-                        ["tb%d_0" % a, "tb%d_1" % a], 131072))
-    wrote(perm, "tab")
-    widen(2)
-    widen(0)
+                cp(out, in_, who)
 
-    def level(lv, obuf, oo, okey, buf, gkey, c, lead, lkey, out, outkey):
-        tag[0] = (lv, c)
-        old, who = users(gkey), SHARE[(lv, c)]
-        l0, nl = CH[c]
-        n = 16 * nl // len(who)
-        wrote([gat(buf[:, 16 * l0 + n * u:16 * l0 + n * (u + 1)], win.indirect(obuf[:, oo + n // 16 * u:oo + n // 16 * (u + 1)]),
-                   ["tab", okey], (), n, e, old) for u, e in enumerate(who)], gkey)
-        ps = T["B%d" % c][:, 0:nl]
-        parts = [] if lead is None else [(ps, T.IDN[:], lead)]
-        parts += [(ps, slide(T.CT, x), buf[:, 16 * l0 + x:16 * (l0 + nl):16]) for x in range(16)]
-        mm(parts, [gkey, "CT", "IDN"] + ([lkey] if lkey else []), ["B%d" % c], max(64, nl) * len(parts))
-        tag[0] = "conv"
-        cp(out, ps, (), ["B%d" % c, outkey], nl)
+    tag[0] = "digits"
+    los = []
+    for c in range(8):
+        o, gs, bk = W * (c // 4) + 512 * (c % 4), R("gin", 512 * (c % 3), 512 * (c % 3) + 512), R("B%d" % (c % 4))
+        cp(R("hl", o, o + 512), gs)
+        mm([(bk, R("IDN"), R("hl", o, o + 512))])
+        los.append(tt(R("hl", o + 2048, o + 2560), gs, bk, A.subtract))
+        if c < 5:
+            load_gloss(c + 3)
+    tag[0] = "small"
+    ri = lambda p0, p1, o=0: R("gin", NV + o, NV + o + L, 1, p0, p1)
+    dma("s", R("CN", 0, L), T.cases[:], "cases", 65536)
+    for p0, p1, o, src in ((0, 32, 0, T.vp0[:]), (32, 64, 0, T.vp0[:]), (64, 88, 0, T.act0[:]), (88, 96, 0, T.act0[0:8, :]),
+                           (0, 6, L, T.need[:]), (6, 7, L, T.dep0[:])):
+        dma("y", ri(p0, p1, o), src, "small", (p1 - p0) * 1024)
+    tag[0] = "cases"
+    cp(R("CN", L, 2 * L, 1, 0, 7), ri(0, 7, L))
+    tag[0] = "state"
+    ts(ri(0, 32), ri(0, 32), 15, None, A.bitwise_and)
+    ts(ri(32, 64), ri(32, 64), 4, None, A.arith_shift_right)
+    cp(R("S", 0, L, 1, 0, 64), ri(0, 64))
+    acts = R("S", 0, L, 1, 64, 96)
+    ts(acts, ri(64, 96), col(SA1, 64, 96), 0.0, A.subtract, A.max)
+    ts(acts, acts, col(SA2, 64, 96), None, A.min)
+    mm([(R("B7", 0, L), R("NE", 768, 896, 1, 0, 7), R("CN", L, 2 * L, 1, 0, 7))])
+    ts(R("S", 0, L, 1, 96, 128), R("B7", 0, L, 1, 96, 128), col(EJ, 96, 128), 64.0, A.is_equal, A.mult)
+    tag[0] = "rest"
+    dma("y", R("gin", 0, NV), T.refs[:], "drf", 524288)
+    cp(R("RF", 0, NV), R("gin", 0, NV))
+    cp(R("RF", NV, NV + 8), R("gin", 0, 8))
+    tag[0] = "fill"
+    ms(R("tab", 0, M), 0.0)
+    ms(R("tab", M + 16 * W, 2 * M + 16 * W + 16), 0.0)
+    ms(R("hl", 2 * W, 2 * W + M + 16), 0.0)
+    turn = [2 * a + u for u in range(2) for a in range(16)]
+    zeros = R(*ZEROS)
+    gave, tag[0] = [], "zeros"
+    for h in helpers(core, T.cores, topo):
+        rid, pid, _se = topo.addr(h)
+        gave.append(add({"g": ISSUE + (0.0 if gave else 2.0)}, (lambda rid, pid, m: lambda e: g.remote_dma(ap(zeros), ap(zeros), T.sem.zeros, T.sem.gave, pid, rid, m))(
+            rid, pid, topo.mask(core, h)), [zeros], (), kind="rem", sem="gave", val=len(topo.engines(core, h))))
+        gave[-1] = add({"H%d" % len(gave): 3.5}, None, kind="recv", sem="none", after=gave[-1:])
+    handed, tag[0] = {}, "fill"
+    for j, e in fillers():
+        o = R("tab", M + 1024 * j, M + 1024 * j + 1024)
+        if e in HANDS:
+            h = HANDS.index(e)
+            n = handed.get(e, 0)
+            handed[e] = n + 1
+            i = add({"H%d" % (h + 1): 1.3}, None, (), [o], kind="recv", sem="fill%s%d" % (e, n // LOT), after=[gave[h]],
+                    val=len(topo.engines(helpers(core, T.cores, topo)[h], core)) * min(LOT, FILL[e] - n // LOT * LOT))
+            groups.setdefault(ops[i]["sem"], []).append(i)
+        elif e == "v":
+            ms(o, 0.0)
+        elif e == "s":
+            cp(o, zeros, "s")
+        else:
+            aff(o, zeros, [[0, 1024]], A.is_ge, 0.0, 0, 0)
+    tag[0] = "perm"
+    for j in turn:
+        perm = dma("y", R("tab", M + 2048 * j, M + 2048 * j + 2048, 1, 0, 128, 8), R("hl", W * (j % 2), W * (j % 2) + W, 1, j // 2, 128, 16),
+                   "perm", 65536, [los[4]])
+    dma("y", R("fa"), T.facts[:], "dfa", 1048576, [perm])
+    tag[0] = "cases"
 
-    def lists(t, h):
-        S, ro = SM[h], 320 * t + 160 * h
-        cp(T.vl[:, 8 * h:8 * h + 8], S[:, 64:72], ["V%d" % h], ["vl%d" % h])
-        cp(T.RO[:, ro + 136:ro + 160], S[:, 40:64], ["X%d" % h], ["al%d_%d" % (t, h)])
-        ts(T.RO[:, ro + 128:ro + 136], S[:, 72:80], 3.0 + t, None, A.is_equal, None, ["D%d" % h], ["d3%d_%d" % (t, h)])
+    def cases(s, after):
+        send(R("CNI", 512 * s, 512 * s + 512), R("CN"), (rank + 1 + s) % n_ranks, (rank - 1 - s) % n_ranks, "cn%d" % s, after)
 
-    tag[0] = None
-    for h in range(2):
-        lists(0, h)
+    cases(0, [los[7]])
+    widen(0, "wide0", "s")
+
+    tag[0] = "late"
+    ms(R("pw", 16, 32), 0.5)
+    add({"v": 64 * CY}, lambda e: g.vector.tensor_tensor_scan(ap(R("pw", 0, 16)), ap(R("pw", 16, 32)), ap(R("pw", 16, 32)), 65536.0, A.mult, A.max),
+        [R("pw", 16, 32)], [R("pw", 0, 16)])
+    ts(R("pw", 16, 32), R("pw", 0, 16), col(M1_), None, A.mult)
+    ts(R("DIG", 16, 32), R("ID", 0, 16), col(M0_), col(M2_), A.mult, A.add)
+    ts(R("DIG", 24, 32), R("DIG", 24, 32), col(M3_))
+    for i in range(6):
+        ts(R("DIG", 16 + (16 << i), 16 + (32 << i)), R("DIG", 16, 16 + (16 << i)), R("pw", 31 - i, 32 - i))
+    ms(R("DIG", 0, 16), 0.0)
+
+    steps(B1, -192, [(104, -64), (96, -192), (40, -64), (32, -191), (8, -65)])
+    steps(B2, 64, [(120, -64), (96, -128), (64, -64), (32, -65)])
+    steps(B3, 0, [(8, 1)])
+    matrix("MA", [(0, 1, 0, 12, -1.0), (0, 0, 1, 3, 1.0), (4, 0, 5, 3, 1.0), (15, 0, 0, 1, -2.0), (15, 0, 4, 1, -2.0), (15, 0, 12, 1, -2.0),
+                  (12, 1, 1, 3, 2.0), (12, 1, 5, 3, 2.0), (12, 1, 8, 3, 2.0), (12, 1, 13, 3, 2.0), (12, 0, 11, 1, 2.0)])
+    matrix("NA", [(2, 0, 0, 16, 2.0), (0, 0, 0, 1, 1.0), (0, 0, 8, 3, 1.0), (1, 0, 4, 1, 1.0), (3, 0, 11, 1, 1.0)], True)
+    matrix("MB", [(1, 1, 1, 11, 1.0), (0, 0, 1, 3, -1.0), (4, 0, 5, 3, -1.0), (13, 1, 1, 3, 2.0), (13, 1, 5, 3, 2.0), (13, 1, 8, 3, 2.0),
+                  (13, 1, 12, 3, 2.0), (13, 0, 11, 1, 2.0), (12, 0, 15, 1, -2.0)])
+    matrix("NB", [(2, 0, 0, 16, -2.0)], True)
+    matrix("M0", [(0, 1, 0, 13, 1.0), (15, 0, 15, 1, 1.0)])
+    matrix("M1", [(0, 1, 0, 12, 1.0), (13, 1, 13, 3, 1.0), (13, 1, 1, 3, -1.0), (13, 1, 5, 3, -1.0), (13, 1, 8, 3, -1.0), (13, 0, 11, 2, -1.0),
+                  (12, 0, 0, 1, -1.0), (12, 0, 4, 1, -1.0)])
+    matrix("M2", [(8, 1, 8, 4, -1.0), (12, 1, 12, 3, 1.0), (14, 0, 15, 1, -1.0), (15, 0, 0, 1, -1.0), (15, 0, 4, 1, -1.0)]
+           + [(j, 0, 0, 1, 1.0) for j in (1, 2, 3)] + [(j, 0, 4, 1, 1.0) for j in (5, 6, 7)])
+
+    for name, src, rows in (("LV1", "LV", [(12, -17.0)]), ("L31", "LA3", [(15, -4096.0)]), ("L32", "ZZ", [(10, -4096.0)]),
+                            ("LV2", "ZZ", [(15, -17.0)] + [(j, 1.0 if j < 4 else 16.0) for j in (1, 2, 3, 5, 6, 7)])):
+        for f, v in rows:
+            lead(name, src, f, v)
+            src = name
+
+    bank = [0]
+
+    def level(lv, offs, o0, buf, c, first, out):
+        tag[0] = "g%d%d" % (lv, c)
+        l0, nl = chunks[c]
+        n = 16 * nl // PIECE.get(tag[0], 2)
+        for u in range(0, 16 * nl, n):
+            cp(R(buf, 16 * l0 + u, 16 * l0 + u + n), ind(win, R(offs, o0 + u // 16, o0 + (u + n) // 16)), "x")
+        tag[0] = "t%d%d" % (lv, c)
+        ps = R(AWAY[c % len(AWAY)] if lv == 1 else HOME[bank[0] % len(HOME)], 0, nl)
+        bank[0] = 0 if lv == 1 else bank[0] + 1
+        mm([(ps,) + x for x in first] + [(ps, slide("CT", x), R(buf, 16 * l0 + x, 16 * (l0 + nl), 16)) for x in range(16)])
+        cp(out, ps)
+        return ps
+
+    def verses(b, parts):
+        l0, nl, _c = batches[b]
+        ps = R(STATE[b][0], 384, 384 + nl)
+        mm([(ps, R("IDN"), R("NE6", 0, nl))] + [(ps,) + x for x in parts])
+        return ps
+
+    def refs(t, b, ps, plus):
+        l0, nl, _c = batches[b]
+        tag[0] = "q%d" % b
+        St, vl, row = R("S", L * (t % 2) + l0, L * (t % 2) + l0 + nl), R("vl", l0 // 16, (l0 + nl) // 16), R("SC", l0, l0 + nl)
+        o = 2 * (L * t + l0) + (0 if l0 else nl)
+        cp(R("RO", o, o + nl), St)
+        tag[0] = "r%d" % b
+        ts(vl, R("SC", l0 + 15, l0 + nl, 16), plus)
+        if b in DIRECT:
+            tt(row, ind(R("RF"), vl), R("sg", l0, l0 + nl), A.add)
+            cp(R("O2", l0, l0 + nl), row)
+            return
+        cp(row, ind(R("RF"), vl), "x")
+        ps = R(STATE[b][2], 0, nl)
+        mm([(ps, R("LA3"), St), (ps, R("ID32"), row)])
+        cp(R("O2", l0, l0 + nl), ps)
+
+    def third(b, parts):
+        l0, nl, _c = batches[b]
+        if b in DIRECT:
+            mm([(R(STATE[b][2], 0, nl),) + x for x in parts])
+            cp(R("sg", l0, l0 + nl), R(STATE[b][2], 0, nl), "x")
+
+    for b, (b0, nb, _c) in enumerate(batches):
+        ps = verses(b, [(R("LV"), R("S", b0, b0 + nb))])
+        scan(R("SC", b0, b0 + nb), R("RS", 0, nb), ps)
+        third(b, [(R("LA3"), R("S", b0, b0 + nb))])
+        refs(0, b, ps, 0.0)
 
     for t in range(ST):
         s = t % 3
         peer, asker = (rank + 1 + s) % n_ranks, (rank - 1 - s) % n_ranks
         last = t == ST - 1
+        nth.clear()
+        step[0] = t
+        lanes = lambda name, l0, nl, o=0: R(name, o + l0, o + l0 + nl)
+        if t == ST - 2:
+            tag[0] = "wide"
+            hold.append(len(ops) - 1)
+            for name, i, v in (("BD0", 0, 1.0), ("BD8", 8, 1.0), ("gm", 0, -1.0), ("km", 8, -1.0)):
+                aff(R(name, 0, 128), R("ZZ", 0, 128), [[-16, 8], [0, 16]], A.not_equal, v, -i, 1)
+            matrix("MO", [(0, 1, 0, 4, 1.0), (4, 1, 0, 4, 16.0), (8, 1, 4, 3, 1.0)] + [(12 + j, 0, 8, 1, j / 64.0) for j in (1, 2, 3)])
+            hold.clear()
+        asks = []
+        for c in range(len(chunks) + 1):
+            if c < len(chunks):
+                l0, nl = chunks[c]
+                level(3, "O2", l0, "G", c, [(R("LA2"), lanes("S", l0, nl, L * (t % 2)))], lanes("O2", l0, nl))
+            if c > 0:
+                l0, nl = chunks[c - 1]
+                b0, nb = [x[:2] for x in batches if c - 1 in x[2]][0]
+                o = 2 * L * t + b0 + l0 + (nb if b0 else 0)
+                level(2, "O2", l0, "G", c - 1, [(R("LA1"), lanes("S", l0, nl, L * (t % 2)))], R("RO", o, o + nl))
+                u = o + nl + (nb if l0 + nl == nb else 0)
+                o -= nb if l0 == b0 > 0 else 0
+                send(R("RQ", o, u), R("RO", o, u), peer, asker, "rq%d_%d" % (t, c - 1))
+                asks.append(len(ops) - 1)
+        asked = asks[-2]
+        tag[0] = "back"
+        for i in range(1, 4 if t == 0 else 0):
+            dma("y", R("DIG", 16 + NV * i, 16 + NV * i + NV), R("DIG", 16, 16 + NV), "dig", 262144, [asked])
+        if t < 2:
+            cases(t + 1, [asked])
         if last:
-            old = users("hi", "lo")
-            tag[0] = None
-            wrote([dma("y", T.hl[a:128:16, 0:2 * W], T.tab[0:128:8, MG + W * a:MG + W * a + W], "back", ["tab"], (), 131072, old)
-                   for a in range(16)], "hl")
-        for h in range(2):
-            ro, ar = 320 * t + 160 * h, 384 * h
-            tag[0] = ("r", h)
-            gat(T.AR[:, ar + 256:ar + 384], T.AT[:].indirect(T.RO[:, ro + 152:ro + 160]), ["AT", "al%d_%d" % (t, h)], ["A3%d" % h], 128, SMALL["a3"])
-            ttg(T.R0[:], T.rf[:].indirect(T.vl[:, 8 * h:8 * h + 8]), T.AR[:, ar + 256:ar + 384], A.add,
-                ["rf", "vl%d" % h, "A3%d" % h], ["R0"], 128)
-            cp(T.O3[:, 128 * h:128 * h + 128], T.R0[:], ["R0"], ["O3%d" % h], 128)
-            gat(T.AR[:, ar:ar + 256], T.AT[:].indirect(T.RO[:, ro + 136:ro + 152]), ["AT", "al%d_%d" % (t, h)], ["AR%d" % h], 256, SMALL["ar"])
-        for c in range(4):
-            h, u = c // 2, c % 2
-            l0, nl = CH[c]
-            lh = l0 - 128 * h
-            ro, ar, rq = 320 * t + 160 * h + lh, 384 * h + lh, 288 * t + 144 * h + lh
-            level(3, T.O3, l0, "O3%d" % h, T.G, "G%d" % c, c, T.AR[:, ar + 128:ar + 128 + nl], "AR%d" % h,
-                  T.O2[:, l0:l0 + nl], "O2%d" % c)
-            level(2, T.O2, l0, "O2%d" % c, T.G, "G%d" % c, c, T.AR[:, ar:ar + nl], "AR%d" % h,
-                  T.RO[:, ro:ro + nl], "ro%d_%d" % (t, c))
-            n = nl + 16 * u
-            send(T.RQ[:, rq:rq + n], T.RO[:, ro:ro + n], peer, asker, "rq%d_%d" % (t, c),
-                 ["ro%d_%d" % (t, c)] + (["al%d_%d" % (t, h), "d3%d_%d" % (t, h)] if u else []), ["rq%d_%d" % (t, c)])
-        for h in range(2):
-            S, Wk, k = SM[h], WK[h], lambda s_, h=h: s_ + str(h)
-            tag[0] = ("pre", h)
-            ts(Wk[:, 0:8], S[:, 64:72], 1.0, None, A.add, None, [k("V")], [k("w0")])
-            ts(S[:, 8:16], Wk[:, 0:8], NV - 1, None, A.bitwise_and, None, [k("w0")], [k("AF")])
-            ttg(Wk[:, 8:40], S[:, 72:80].indirect(rep4), T.J4[:, 32 * t:32 * t + 32], A.is_equal, [k("D"), "J4"] + RLK, [k("w1")], 32)
-            tt(Wk[:, 8:40], Wk[:, 8:40], S[:, 8:40], A.mult, [k("w1"), k("AF"), k("X")], [k("w1")])
-            tt(Wk[:, 8:24], Wk[:, 8:24], Wk[:, 24:40], A.add, [k("w1")], [k("w1")])
-            tt(Wk[:, 40:48], Wk[:, 8:16], Wk[:, 16:24], A.add, [k("w1")], [k("aE")])
-            ts(Wk[:, 48:56], S[:, 72:80], 3.0 + t, None, A.is_lt, None, [k("D")], [k("c3")])
-            tt(Wk[:, 56:64], S[:, 8:16], Wk[:, 40:48], A.subtract, [k("AF"), k("aE")], [k("dE")])
-        ebuf, eo, ekey = EXP[s]
-        for c in range(4):
-            l0, nl = CH[c]
-            level(1, T.RQ, 288 * t + 16 * (c // 2) + l0, "rq%d_%d" % (t, c), T.G1, "G1%d" % c, c, None, None,
-                  T.TU[:, l0:l0 + nl], "TU%d" % c)
-        for h in range(2):
+            for a in range(16):
+                dma("y", R("hl", 0, 2 * W, 1, a, 128, 16), R("tab", M + W * a, M + W * a + W, 1, 0, 128, 8), "back", 131072,
+                    asks[-2:-1] if a >= BACK else [])
+        ebuf, eo = EXP[t]
+        for b0, nb, cs in batches:
+            for c in cs:
+                l0, nl = chunks[c]
+                ps = level(1, "RQ", 2 * L * t + b0 + l0 + (nb if b0 else 0), "G1", c, [], lanes("TU", l0, nl))
+                tag[0] = "x%d" % c
+                relu(lanes("EF", l0, nl, b0 + nb), ps, col(C16))
+                cp(lanes("EF", l0, nl, b0), lanes("RQ", l0, nl, 2 * L * t + b0 + (nb if b0 else 0)))
+        for b, (b0, nb, cs) in enumerate(batches):
+            X, Y, Z = SETS[b % 2]
             if last:
-                send(T.TI[:, 128 * h:128 * h + 128], T.TU[:, 128 * h:128 * h + 128], asker, peer, "ti%d" % h,
-                     ["TU%d" % (2 * h), "TU%d" % (2 * h + 1)], ["TI%d" % h])
-            for c in (2 * h, 2 * h + 1):
-                tag[0] = ("f", c)
-                l0, nl = CH[c]
-                co, ck, pc = 16 * l0, "G%d" % c, 16 * min(nl, FP)
-                old = users(ck)
-                wrote([ttg(T.G[:, co + a:co + a + pc], T.fa[:].indirect(T.TU[:, l0 + a // 16:l0 + (a + pc) // 16]),
-                           ebuf[:, eo + co + a:eo + co + a + pc], A.is_le, ["fa", "TU%d" % c, ekey], (), pc, None, old)
-                       for a in range(0, 16 * nl, pc)], ck)
-                ps = T.B4[:, l0:l0 + nl]
-                nd = 512 * s + 256 + l0
-                mm([(ps, T.NE[0:6, 128 * t:128 * t + 128], T.CNI[0:6, nd:nd + nl])]
-                   + [(ps, slide(T.CC, x), T.G[:, co + x:co + 16 * nl:16]) for x in range(16)],
-                   [ck, "NE", "CC", "CNI%d" % s], ["B4"], max(64, nl) * 17)
-            tag[0] = ("v", h)
-            Qh, k = QQ[h], lambda s_, h=h: s_ + str(h)
-            po, pi_, rq = 48 * t + 24 * h, 32 * t + 16 * h, 288 * t + 144 * h
-            rqk, pk = "rq%d_%d" % (t, 2 * h + 1), "po%d_%d" % (t, h)
-            na, nb, nc, nd_ = BANKS[h]
-            Ba, Bb, Bc, Bd = T[na], T[nb], T[nc], T[nd_]
-            sg, isf, fl, Gf, kr = (T[k(x)] for x in ("sg", "isf", "fl", "Gf", "kr"))
-            act(sg[:], T.B4[:, 128 * h:128 * h + 128], F.Sign, 0.5, (), ["B4", k("sg")], 128)
-            mm([(Ba[:, 0:128], T.UP[:], sg[:])], ["UP", k("sg")], [na], 128)
-            mm([(Ba[:, 128:256], T.UN[:], sg[:])], ["UN", k("sg")], [na], 128)
-            act(isf[:], Ba[:, 0:256], F.Relu, col(NK), ["nk"], [na, k("isf")], 256)
-            mm([(Bb[:, 0:16], T.IDN[:], T.c256[:, 0:16])] + [(Bb[:, 0:16], slide(T.C1, x), isf[:, x:256:16]) for x in range(16)],
-               ["IDN", "c256", "C1", k("isf")], [nb], 64 * 17)
-            ts(fl[:], Bb[:, 0:16], col(X16), None, A.add, None, ["x16"], [nb, k("fl")])
-            tt(T.PO[:, po + 8:po + 24], Bb[:, 0:16], T.c256[:, 0:16], A.is_gt, ["c256"], [nb, pk + "f"])
-            for u, nm in enumerate(("Gf", "Gh")):
-                gat(Gf[:, 128 * u:128 * u + 128], T.G1[:, 2048 * h:2048 * h + 2048].indirect(fl[:, 8 * u:8 * u + 8]),
-                    [k("fl"), "G1%d" % (2 * h), "G1%d" % (2 * h + 1)], [k(nm)], 128, SMALL[nm])
-            tag[0] = ("w", h)
-            cp(Qh[:, 8:16], T.RQ[:, rq + 128:rq + 136], [rqk], [k("d3")])
-            tt(Qh[:, 8:16], Qh[:, 8:16], T.PO[:, po + 8:po + 16], A.mult, [k("d3"), pk + "f"], [k("d3")])
-            tt(Qh[:, 48:56], Qh[:, 8:16], T.PO[:, po + 16:po + 24], A.mult, [k("d3"), pk + "f"], [k("ask")])
-            tag[0] = ("v", h)
-            mm([(Ba[:, 256:384], T.BDK[:], Gf[:, 0:128])], ["BDK", k("Gf")], [na], 128)
-            ts(kr[:], Ba[:, 256:384], 1.0, None, A.add, None, (), [na, k("kr")], 128)
-            mm([(Bb[:, 24:32], T.IDN[:], T.c256[:, 16:24])] + [(Bb[:, 24:32], slide(T.CK, x), Gf[:, x:128:16]) for x in range(16)],
-               ["CK", "IDN", "one", k("Gf")], [nb], 64 * 17)
-            tt(T.kc[:, 8 * h:8 * h + 8], Bb[:, 24:32], Qh[:, 48:56], A.mult, [k("ask")], [nb, k("kc")])
-            add(only({"s": vc(8), "v": vc(8)}, SMALL["k1"]), either(Qh[:, 0:8], Bb[:, 24:32]), (), [nb, k("k1")])
-            mm([(Bd[:, 16:24], slide(T.CT, x), Gf[:, x:128:16]) for x in range(16)], ["CT", k("Gf")], [nd_], 1024)
-            cp(T.PO[:, po:po + 8], Bd[:, 16:24], (), [nd_, pk + "t"])
-            send(T.PI[:, pi_:pi_ + 16], T.PO[:, po:po + 16], asker, peer, "rs%d_%d" % (t, h), [pk + "t", pk + "f"], ["rs%d_%d" % (t, h)])
-            tag[0] = ("w", h)
-            a1 = T.RQ[:, rq + 136:rq + 144]
-            if not last:
-                mm([(Ba[:, 384:512], T.D01[:], Gf[:, 128:256]), (Ba[:, 384:512], T.D2[:], Gf[:, 0:128])],
-                   ["D01", "D2", k("Gf"), k("Gh")], [na], 256)
-                add(only({"s": vc(128), "v": vc(128)}, SMALL["val"]), either(T.val[:, 128 * h:128 * h + 128], Ba[:, 384:512]), (),
-                    [na, k("val")])
+                send(lanes("TI", b0, nb), lanes("TU", b0, nb), asker, peer, "ti%d" % b)
+            for c in cs:
+                tag[0] = "f%d" % c
+                l0, nl = chunks[c]
+                n = 16 * nl // PIECE.get(tag[0], 1)
+                for u in range(16 * l0, 16 * (l0 + nl), n):
+                    tt(R("G", u, u + n), ind(R("fa"), R("TU", u // 16, (u + n) // 16)), R(ebuf, eo + u, eo + u + n), A.is_le)
+                tag[0] = "n%d" % c
+                ps = R(X, l0 - b0, l0 - b0 + nl)
+                nd = 512 * s + L + l0
+                mm([(ps, R("NE", 128 * t, 128 * t + 128, 1, 0, 7), R("CNI", nd, nd + nl, 1, 0, 7))]
+                   + [(ps, slide("CC", x), R("G", 16 * l0 + x, 16 * (l0 + nl), 16)) for x in range(16)])
+            tag[0] = "p%d" % b
+            nh = nb // 16
+            sg, es, sq, kr = lanes("sg", b0, nb), lanes("EF", b0, nb, b0), lanes("SQ", b0, nb), lanes("O2", b0, nb)
+            tsel, both = lanes("EF", b0, nb, b0 + nb), R("EF", 2 * b0, 2 * b0 + 2 * nb)
+            b16, t16 = lanes("B16", b0, nb, b0), lanes("B16", b0, nb, b0 + nb)
+            cp(sq, lanes("RQ", b0, nb, 2 * L * t + b0 + (0 if b0 else nb)))
+            isf, ish = R("isf", 2 * b0, 2 * b0 + nb), R("isf", 2 * b0 + nb, 2 * b0 + 2 * nb)
+            gf, gh = R("GF", 2 * b0, 2 * b0 + nb), R("GF", 2 * b0 + nb, 2 * b0 + 2 * nb)
+            mm([(R(Z, 0, 2 * nb), R("ID32"), both), (R(Z, 0, nb), R("NLA"), sq)], True, False)
+            mm([(R(Y, 0, 256), R("IDN"), R("ODK")), (R(Y, 0, nb), R("QK"), sq)], True, False)
+            tag[0] = "v%d" % b
+            add({"s": scost(sg, sg)}, (lambda o, i_: lambda e: g.scalar.activation(ap(o), ap(i_), F.Sign, bias=0.5))(sg, R(X, 0, nb)),
+                [R(X, 0, nb)], [sg])
+            mm([(R(Z, 0, nb), R("UPB"), sg), (R(Z, nb, 2 * nb), R("UPB"), sg)], False, True)
+            mm([(R(X, 0, nb), R("UP"), sg)])
+            mm([(R(X, nb, 2 * nb), R("UN"), sg)])
+            ts(R("B16", 2 * b0, 2 * b0 + 2 * nb), R(Z, 0, 2 * nb), col(NKB), -2048.0, A.add, A.max)
+            relu(R("isf", 2 * b0, 2 * b0 + 2 * nb), R(X, 0, 2 * nb), col(NK))
+            mm([(R(Y, 128, 128 + nb), R("BD16"), b16), (R(Y, 0, nb), R("BD16"), b16), (R(Y, 0, nb), R("PFB"), isf), (R(Y, 0, nb), R("PFB"), ish)],
+               False, True)
+            tag[0] = "a%d" % b
+            po = 8 * (NB_ * t + b)
+            ps = R(Z, 0, nb)
+            mm([(ps, R("IDN"), R("OD3", 0, nb)), (ps, R("BD16"), t16)])
+            scan(tsel, R("RS", 0, nb), ps)
+            ts(R("PO", po, po + nh), R("EF", 2 * b0 + nb + 15, 2 * b0 + 2 * nb, 16), 15.0)
+            send(R("PI", po, po + nh), R("PO", po, po + nh), asker, peer, "rs%d_%d" % (t, b))
+            tag[0] = "b%d" % b
+            za, zb = R(Z, 0, nb), R(Z, 128, 128 + nb)
+            gate = lambda z: [(z, R("QK"), sq), (z, R("PFB"), isf), (z, R("PFB"), ish)]
+            more = [(z, R("IDN"), R("OD3", 128, 128 + nb)) for z in (za, zb)] + gate(za) + gate(zb) if b in TWICE else []
+            mm([(R(Z, 0, 256), R("IDN"), R("OD5" if last else "OD2"))] + ([] if last else [(za, R("QA"), sq), (zb, R("QB"), sq)])
+               + [(za, R("BD16" if last else "NB16"), b16), (zb, R("BD16"), b16)] + more, True, b not in TWICE)
+            tag[0] = "o%d" % b
+            if b not in TWICE:
+                scan(lanes("SC", b0, nb), R("RS", 0, nb), za)
+                scan(lanes("SD", b0, nb), R("RS", 0, nb), zb)
+            tag[0] = "h%d" % b
+            j, u = 16 * sizes.index(nb), 0 if last else 1
+            ps, fl = R(X, 0, (2 - u) * nh), R("fl", b0 // 8, b0 // 8 + (2 - u) * nh)
+            mm([(ps, R("IDN"), R("c256", j, j + (2 - u) * nh))]
+               + [(ps, slide("C1", x), R("isf", 2 * b0 + u * nb + x, 2 * b0 + 2 * nb, 16)) for x in range(16)])
+            ts(fl, ps, col(X16))
+            cp(R("GF", 2 * b0 + u * nb, 2 * b0 + 2 * nb), ind(R("G1", 16 * b0, 16 * (b0 + nb)), fl), "x")
+            tag[0] = "k%d" % b
+            cp(kr, R(Y, 128, 128 + nb))
+            scan(R("KC", 1 + b0, 1 + b0 + nb), R("RS", 0, nb), R(Y, 0, nb))
+            o, parts = 16 * b0, []
+            tt(R("G", o, o + nb), R("KC", b0, b0 + nb), R(Y, 128, 128 + nb), A.is_equal)
+            into = [(Z, 0), (Z, 128)] if b in TWICE else [(Y, 0)]
+            if b not in TWICE:
+                parts += [(R(Y, 0, nb), R("IDN"), R("OD3", 128, 128 + nb))] + gate(R(Y, 0, nb))
+            parts += [(R(bk, z, z + nb), R("BDB"), R("G", o, o + nb)) for bk, z in into]
+            o += nb
+            blocks = list(range((b0 + nb) // 16 - 1))
+            begun, tag[0] = False, "e%d" % b
+            for c in blocks:
+                lo = max(0, 16 * (c + 1) - b0)
+                ts(R("G", o, o + nb - lo), R("O2", b0 + lo, b0 + nb), R("KC", 16 * c + 16, 16 * c + 17), None, A.is_equal)
+                parts += [(R(bk, z + lo, z + nb), R("BDB"), R("G", o, o + nb - lo)) for bk, z in into]
+                o += nb - lo
+                if len(parts) >= 4 * len(into) or c == blocks[-1]:
+                    mm(parts, not begun and b not in TWICE, c == blocks[-1])
+                    parts, begun = [], True
+            tag[0] = "z%d" % b
+            oa, ob = R("of", b0 // 8, b0 // 8 + nh), R("of", b0 // 8 + nh, b0 // 8 + 2 * nh)
+            sa, sd = R("SC", b0 + 15, b0 + nb, 16), R("SD", b0 + 15, b0 + nb, 16)
+            if b in TWICE:
+                scan(lanes("SC", b0, nb), R("RS", 0, nb), za)
+                scan(lanes("SD", b0, nb), R("RS", 0, nb), zb)
             else:
-                mm([(Ba[:, 0:128], T.BD0[:], Gf[:, 128:256])], ["BD0", k("Gh")], [na], 128)
-                mm([(Ba[:, 128:256], T.BD8[:], Gf[:, 128:256])], ["BD8", k("Gh")], [na], 128)
-                add({"s": vc(256)}, either(T.val[:], Ba[:, 0:256]), (), [na, "val0", "val1"])
-                for u in range(2):
-                    sl = slice(128 * u, 128 * u + 128)
-                    ttg(T.md[:, sl], T.M16[:, 0:16].indirect(a1), T.val[:, sl], A.mult, [rqk, "M16a", "val0"], ["md%d" % u], 128)
-                    gat(T.nm[:, sl], T.M16[:, 16:32].indirect(a1), [rqk, "M16b"], ["nm%d" % u], 128, "s")
+                scan(es, R("RS", 0, nb), R(Y, 0, nb))
+                for x in (sa, sd):
+                    tt(x, x, R("EF", 2 * b0 + 15, 2 * b0 + nb, 16), A.max)
             if not last:
-                ts(Qh[:, 16:24], a1, float(W), float(MG - 1), A.mult, A.add, [rqk], [k("E")])
-                ts(Qh[:, 32:40], a1, 8.0, None, A.is_lt, None, [rqk], [k("LHa")])
-                ts(Qh[:, 40:48], a1, 8.0, None, A.is_ge, None, [rqk], [k("LHb")])
-                ttg(Qh[:, 64:80], Qh[:, 48:56].indirect(rep2), Qh[:, 32:48], A.mult, [k("ask"), k("LHa"), k("LHb")] + RLK, [k("LA")], 16)
-                tt(Qh[:, 16:24], Qh[:, 16:24], Qh[:, 0:8], A.add, [k("E"), k("k1")], [k("E")])
-                ts(Qh[:, 24:32], Qh[:, 16:24], -1.0, float(16 * W + 2 * MG - 1), A.mult, A.add, [k("E")], [k("Eb")])
-                tt(Qh[:, 80:96], Qh[:, 16:32], Qh[:, 64:80], A.mult, [k("E"), k("Eb"), k("LA")], [k("OO")])
-                ends = (None, 8 * W + MG - 1)
+                ts(oa, sa, -1.0, float(32768 + M), A.mult, A.add)
+                cp(ob, sd)
+                tag[0] = "w%d" % b
+                cp(ind(R("tab", 0, M + 8 * W), oa), gh)
+                cp(ind(R("tab", M + 8 * W, 2 * M + 16 * W + 16), ob), gh)
             else:
-                ts(Qh[:, 64:72], Qh[:, 0:8], -1.0, float(2 * W + MG), A.mult, A.add, [k("k1")], [k("LA")])
-                ts(Qh[:, 72:80], Qh[:, 0:8], -1.0, float(W + 2 * MG), A.mult, A.add, [k("k1")], [k("Eb")])
-                ttg(Qh[:, 80:96], Qh[:, 48:56].indirect(rep2), Qh[:, 64:80], A.mult, [k("ask"), k("LA"), k("Eb")] + RLK, [k("OO")], 16)
-                ends = (2 * W + MG - 1, 2 * W + 2 * MG - 1)
-            tt(Qh[:, 80:96], Qh[:, 80:96], T.base[:], A.max, [k("OO"), "base"], [k("OO")])
-            tag[0] = ("e", h)
-            parts, o, eqs, every = [(Bc[:, 0:128], T.IDN[:], T.nthr[:])], 2048 * h, [], []
-            eqk = ["G%d" % (2 * h), "G%d" % (2 * h + 1)]
-            old = users(*eqk)
-            for c in range(8 * h + 8):
-                lo = max(0, 16 * (c - 8 * h))
-                n = 128 - lo
-                eqs.append(ts(T.G[:, o:o + n], kr[:, lo:128], T.kc[:, c:c + 1], None, A.is_equal, None, [k("kr"), "kc%d" % (c // 8)], (),
-                              n, 0.5, old))
-                if c < 8 * h:
-                    parts.append((Bc[:, 0:128], T.BDB[:], T.G[:, o:o + n]))
-                else:
-                    parts.append((Bc[:, lo:lo + 16], T.BDW[:], T.G[:, o:o + 16]))
-                    if n > 16:
-                        parts.append((Bc[:, lo + 16:128], T.BDB[:], T.G[:, o + 16:o + n]))
-                o += n
-                if c % 4 == 3:
-                    wrote(eqs, "EQ")
-                    every.append(mm(parts, ["EQ", "IDN", "nthr", "BDB", "BDW"], [nc], 80 * len(parts), c == 3, c == 8 * h + 7))
-                    parts, eqs = [], []
-            wrote(every, *eqk)
-            tag[0] = ("z", h)
-            add({"s": vc(128)}, (lambda o_, i_: lambda e: g.scalar.activation(o_, i_, F.Relu, scale=-1.0))(sg[:], Bc[:, 0:128]),
-                (), [nc, k("sg")])
-            mm([(Bb[:, 32:40], T.IDN[:], T.c256[:, 24:32])] + [(Bb[:, 32:40], slide(T.CB, x), sg[:, x:128:16]) for x in range(16)],
-               ["CB", "IDN", "lnb", k("sg")], [nb], 64 * 17)
-            for u in range(2):
-                tt(Qh[:, 96 + 8 * u:104 + 8 * u], Bb[:, 32:40], Qh[:, 80 + 8 * u:88 + 8 * u], A.min, [k("OO")], [nb, k("m%d" % u)])
-            for u in range(2):
-                o_, i_ = T.of[:, 16 * h + 8 * u:16 * h + 8 * u + 8], Qh[:, 96 + 8 * u:104 + 8 * u]
-                if ends[u] is None:
-                    cp(o_, i_, [k("m%d" % u)], [k("of%d" % u)])
-                else:
-                    ts(o_, i_, -1.0, float(ends[u]), A.mult, A.add, [k("m%d" % u)], [k("of%d" % u)])
-            of = T.of[:, 16 * h:16 * h + 16]
-            if last:
-                ttg(T.kept[:], T.hl[:].indirect(of), T.nm[:], A.mult, ["hl", "hlm", k("of0"), k("of1"), "nm0", "nm1"], ["kept"], 256)
-                ttg(T.hl[:].indirect(of), T.kept[:], T.md[:], A.add, [k("of0"), k("of1"), "kept", "md0", "md1"], ["hl", "hlm"], 256, SC)
-            else:
-                old = users("tab")
-                wrote([add({"v": 0.06 + 128 * SC * CY},
-                           either(wn.indirect(T.of[:, 16 * h + 8 * u:16 * h + 8 * u + 8]), T.val[:, 128 * h:128 * h + 128]),
-                           [k("of%d" % u), k("val")], (), after=old)
-                       for u, wn in enumerate((T.tab[:, 0:HALF], T.tab[:, HALF:16 * W + 2 * MG]))], "tab")
-        if t == 0:
-            widen(1)
-        for h in range(2):
-            S, Wk, k = SM[h], WK[h], lambda s_, h=h: s_ + str(h)
-            tag[0] = ("s", h)
-            pi_, rk = 32 * t + 16 * h, "rs%d_%d" % (t, h)
-            tf, ne = T.PI[:, pi_:pi_ + 8], T.PI[:, pi_ + 8:pi_ + 16]
-            tt(Wk[:, 64:72], S[:, 72:80], ne, A.add, [k("D"), rk], [k("lev")])
-            tt(Wk[:, 72:80], Wk[:, 64:72], ne, A.mult, [k("lev"), rk], [k("lvp")])
-            ts(Wk[:, 80:88], tf, 15, None, A.bitwise_and, None, [rk], [k("ta")])
-            ts(Wk[:, 88:96], tf, NV - 1, None, A.bitwise_and, None, [rk], [k("tv")])
-            tt(S[:, 0:8], Wk[:, 80:88], ne, A.mult, [k("ta"), rk], [k("VA")])
-            ttg(Wk[:, 96:144], Wk[:, 64:80].indirect(rep6), T.J6[:, 48 * t:48 * t + 48], A.is_equal,
-                [k("lev"), k("lvp"), "J6%d" % t] + RLK, [k("MM")], 48)
-            ttg(Wk[:, 144:192], S[:, 0:16].indirect(rep6), S[:, 16:64], A.subtract, [k("VA"), k("AF"), k("X")] + RLK, [k("DX")], 48)
-            tt(Wk[:, 144:192], Wk[:, 144:192], Wk[:, 96:144], A.mult, [k("DX"), k("MM")], [k("DX")], 48)
-            tt(S[:, 16:64], S[:, 16:64], Wk[:, 144:192], A.add, [k("X"), k("DX")], [k("X")], 48)
-            tt(Wk[:, 192:200], Wk[:, 64:72], ne, A.add, [k("lev"), rk], [k("dt")])
-            ts(S[:, 72:80], Wk[:, 192:200], float(1 + t), float(4 + t), A.max, A.min, [k("dt")], [k("D")])
-            tt(Wk[:, 88:96], Wk[:, 88:96], S[:, 8:16], A.subtract, [k("tv"), k("AF")], [k("tv")])
-            tt(Wk[:, 88:96], Wk[:, 88:96], Wk[:, 48:56], A.mult, [k("tv"), k("c3")], [k("tv")])
-            tt(Wk[:, 88:96], Wk[:, 88:96], Wk[:, 56:64], A.add, [k("tv"), k("dE")], [k("tv")])
-            tt(Wk[:, 88:96], Wk[:, 88:96], ne, A.mult, [k("tv"), rk], [k("tv")])
-            tt(S[:, 64:72], Wk[:, 88:96], Wk[:, 40:48], A.add, [k("tv"), k("aE")], [k("V")])
+                ts(oa, sa, -24576.0)
+                ts(ob, sd, -28672.0)
+                tag[0] = "w%d" % b
+                mm([(R(Y, 0, nb), R("LA1"), sq)])
+                mm([(R(Y, 128, 128 + nb), R("BD0"), gh), (R(Y, 128, 128 + nb), R("gm"), gf)])
+                mm([(R(Y, 256, 256 + nb), R("BD8"), gh), (R(Y, 256, 256 + nb), R("km", 0, 128), gf)])
+                ts(sg, R(Y, 0, nb), col(K4), None, A.is_equal)
+                for u, (of, dl, new) in enumerate(((oa, lanes("SC", b0, nb), isf), (ob, lanes("SD", b0, nb), ish))):
+                    wn = R("hl", W * u, 2 * W + M + 16)
+                    tt(dl, sg, R(Y, 128 + 128 * u, 128 + 128 * u + nb), A.mult)
+                    tt(new, ind(wn, of), dl, A.add)
+                    cp(ind(wn, of), new)
+        if t < min(3, ST - 1):
+            hold.append(asked)
+            widen(t + 1, "wide", "g")
+            hold.clear()
+        for b, (b0, nb, cs) in enumerate(batches):
+            tag[0] = "s%d" % b
+            po = 8 * (NB_ * t + b)
+            St, Sn, D = lanes("S", b0, nb, L * (t % 2)), lanes("S", b0, nb, L * (1 - t % 2)), lanes("sg", b0, nb)
+            r1, r2 = lanes("R1", b0, nb), lanes("R2", b0, nb)
+            cp(D, ind(R("DIG"), R("PI", po, po + nb // 16)), "x")
+            pa, pb = R(STATE[b][0], 0, nb), R(STATE[b][1], 128, 128 + nb)
+            mm([(pa, R("MA"), St), (pa, R("NA"), D)])
+            mm([(pb, R("MB"), St), (pb, R("NB"), D)])
+            relu(r1, pa, col(B1))
+            relu(r2, pb, col(B2))
+            ps, tag[0] = R(STATE[b][1], 256, 256 + nb), "u%d" % b
             if not last:
-                lists(t + 1, h)
+                pv = verses(b, [(R("LV"), St), (R("LV1"), r1), (R("LV2"), r2)])
+                scan(lanes("SC", b0, nb), R("RS", 0, nb), pv)
+                third(b, [(R("LA3"), St), (R("L31"), r1), (R("L32"), r2)])
+            mm([(ps, R("M0"), St), (ps, R("M1"), r1), (ps, R("M2"), r2)])
+            relu(Sn, ps, col(B3))
+            if not last:
+                refs(t + 1, b, pv, 1.0)
+            else:
+                ln, q = slice(b0, b0 + nb), "out0" if b + 1 < len(batches) else "outs"
+                ps, y, z = R(STATE[b][2], 0, nb), lanes("SC", b0, nb), lanes("SD", b0, nb)
+                mm([(ps, R("MO"), Sn)])
+                ts(y, ps, float(NV), -float(NV), A.is_ge, A.mult)
+                tt(z, y, ps, A.add)
+                dma("y", T.yvp[:, ln], R("SD", b0, b0 + nb, 1, 0, 32), q, 128 * nb)
+                dma("s", T.yact[:, ln], R("SD", b0, b0 + nb, 1, 32, 56), q, 96 * nb)
+                dma("y", T.ydep[:, ln], R("SD", b0, b0 + nb, 1, 64, 65), q, 4 * nb)
 
-    tag[0] = None
-    qs = ["y", "s"]
-    mm([(T.B4[:, 0:256], T.IDN[:], T.hl[:, 256 * m:256 * m + 256]) for m in range(32)], ["IDN", "hl"], ["B4"], 32 * 256)
-    add({"s": vc(256), "v": vc(256)}, either(T.F2[:, 0:256], T.B4[:, 0:256]), (), ["B4", "F2a"])
-    dma("y", T.yg[:], T.F2[:, 0:256], "outs", ["F2a"], (), 131072)
-    for h in range(2):
-        S, k = SM[h], lambda s_, h=h: s_ + str(h)
-        cp(T.F2[:, 256 + 128 * h:384 + 128 * h], T.TI[:, 128 * h:128 * h + 128], [k("TI")], [k("yt")], 128)
-        ts(S[:, 72:80], S[:, 72:80], -float(ST), None, A.add, None, [k("D")], [k("D")])
-        cp(T.FL[:, 64 * h:64 * h + 64], S[:, 16:80], [k("D"), k("V"), k("X")], [k("FL")])
-        for u in range(2):
-            gat(T.FO[:, 512 * u:512 * u + 512], T.ID[:, 0:NV].indirect(T.FL[:, 64 * h + 32 * u:64 * h + 32 * u + 32]),
-                [k("FL"), "ID0", "ID1"], ["FO%d" % u], 512)
-            for f in range(4 * u, 4 * u + 4):
-                src = T.FO[0:128:16, 128 * f:128 * f + 128]
-                ln = slice(128 * h, 128 * h + 128)
-                if f < 3:
-                    out = T.yvp[8 * f + 8:8 * f + 16, ln]
-                elif f < 6:
-                    out = T.yact[8 * f - 24:8 * f - 16, ln]
-                elif f == 6:
-                    out = T.yvp[0:8, ln]
-                else:
-                    out, src = T.ydep[0:1, ln], T.FO[0:1, 896:1024]
-                dma(qs[f % 2] if h else "y", out, src, "outs" if h else "out0", ["FO%d" % u], (), 4096)
-    dma("y", T.yt[:], T.F2[:, 256:512], "outs", ["yt0", "yt1"], (), 131072)
+    tag[0] = "out"
+    for b0, nb, _c in batches:
+        cp(lanes("RF", b0, nb), lanes("TI", b0, nb))
+    dma("y", T.yt[:], R("RF", 0, L), "out0", 131072)
+    mm([(R("B0", 0, L), R("IDN"), R("hl", L * m, L * m + L)) for m in range(32)])
+    cp(R("RF", L, 2 * L), R("B0", 0, L), "x")
+    dma("s", T.yg[:], R("RF", L, 2 * L), "outs", 131072)
     return ops, groups
 
 
@@ -569,7 +687,7 @@ def order(ops, groups):
     for i, o in enumerate(ops):
         d = set()
         for j in o["deps"]:
-            d.update(groups[ops[j]["sem"]] if ops[j]["kind"] == "dma" else [j])
+            d.update(groups.get(ops[j]["sem"], [j]))
         assert i not in d
         deps.append(d)
     users = [[] for _ in range(n)]
@@ -586,78 +704,87 @@ def order(ops, groups):
     assert len(seq) == n
     prio = [0.0] * n
     for i in reversed(seq):
-        c = min(ops[i]["cost"].values()) + (DLAT + ops[i]["bytes"] / DBW if ops[i]["kind"] == "dma" else SYNC)
-        prio[i] = c + ops[i]["boost"] + max([prio[u] for u in users[i]], default=0.0)
+        c = min(ops[i]["cost"].values()) + {"dma": DLAT + ops[i]["bytes"] / DBW, "recv": HOP}.get(ops[i]["kind"], SYNC)
+        prio[i] = c + max([prio[u] for u in users[i]], default=0.0)
 
-    def gap(line, at, c):
-        lo, hi = 0, len(line)
-        while lo < hi:
-            mid = (lo + hi) // 2
-            if line[mid][1] <= at:
-                lo = mid + 1
-            else:
-                hi = mid
-        while lo < len(line) and line[lo][0] < at + c - 1e-9:
-            at = max(at, line[lo][1])
-            lo += 1
-        return at, lo
+    prio = [prio[i] + LIFT.get(ops[i]["tag"], 0.0) for i in range(n)]
+    eng, start, done, seq = [None] * n, [0.0] * n, [0.0] * n, []
+    free = {e: 0.0 for e in ["H1", "H2"] + list("vspgyLR")}
+    ready = {e: {} for e in free}
 
-    def sweep(before, later, key, fixed, back):
-        left = [len(d) for d in before]
-        ready = [i for i in range(n) if left[i] == 0]
-        lines = {e: [] for e in "vspgyL"}
-        eng, start, done = [None] * n, [0.0] * n, [0.0] * n
-        while ready:
-            i = min(ready, key=key.get)
-            ready.remove(i)
-            o, best = ops[i], None
-            wire = o["bytes"] / DBW if o["kind"] == "dma" else 0.0
-            for e, c in o["cost"].items():
-                if fixed is not None and e != fixed[i]:
-                    continue
-                at = max([done[j] + (SAME if eng[j] == e else SYNC) for j in before[i]], default=0.0)
-                if wire and back:
-                    a2, p2 = gap(lines["L"], at + DLAT, wire)
-                    lines["L"].insert(p2, (a2, a2 + wire))
-                    at = a2 + wire
-                pos = None
-                if e is not None:
-                    at, pos = gap(lines[e], at, c)
-                if best is None or at + c + (LEAN if e == "v" else 0.0) < best[0] + (LEAN if best[1] == "v" else 0.0):
-                    best = (at + c, e, at, pos)
-            done[i], eng[i], start[i] = best[0], best[1], best[2]
-            if best[1] is not None:
-                lines[best[1]].insert(best[3], (best[2], best[0]))
-            if wire and not back:
-                a2, p2 = gap(lines["L"], done[i], wire)
-                lines["L"].insert(p2, (a2, a2 + wire))
-                done[i] = a2 + wire + DLAT
-            for u in later[i]:
-                left[u] -= 1
-                if left[u] == 0:
-                    ready.append(u)
-        return eng, start, done
+    def offer(i):
+        o = ops[i]
+        who = WHO.get(o["tag"], "x")
+        for e, c in o["cost"].items():
+            if len(o["cost"]) == 1 or who[o["nth"] % len(who)] in ("x", e):
+                ready[e][i] = (max([done[j] + (SYNC if eng[j] != e else SAME if o["deps"].get(j, True) else 0.0) for j in deps[i]],
+                                   default=0.0), c)
 
-    key, best = {i: (-prio[i] - ops[i]["early"], i) for i in range(n)}, None
-    for turn in range(TURNS):
-        eng, start, done = sweep(deps, users, key, None, False)
-        if best is None or max(done) < max(best[2]):
-            best = (eng, start, done)
-        if turn + 1 < TURNS:
-            _e, _s, back = sweep(users, deps, {i: (-done[i], -i) for i in range(n)}, eng, True)
-            key = {i: (-back[i], i) for i in range(n)}
-    eng, start, done = best
-    return sorted(range(n), key=lambda i: (start[i], i)), eng, start, done
+    for i in range(n):
+        if not left[i]:
+            offer(i)
+    while len(seq) < n:
+        e, now, soon = None, 1e18, 1e18
+        for q, cd in ready.items():
+            if cd:
+                t = max(min(cd.values())[0], free[q])
+                u = t + (DELAY if q in "vs" else 0.0)
+                if u < soon or (u == soon and q == "s"):
+                    e, now, soon = q, t, u
+        best, top = None, None
+        for i, (at, c) in ready[e].items():
+            if at <= now + 1e-9 and (top is None or prio[i] > top):
+                best, top = i, prio[i]
+        first = best
+        for i, (at, c) in ready[e].items():
+            if now < at < now + ready[e][first][1] and prio[i] - LOOK * (at - now) > top and prio[i] > prio[first] + 0.3:
+                best, top = i, prio[i] - LOOK * (at - now)
+        at, c = ready[e][best]
+        for q in ops[best]["cost"]:
+            ready[q].pop(best, None)
+        eng[best], start[best] = e, max(at, now)
+        free[e] = done[best] = start[best] + c
+        if ops[best]["kind"] == "recv":
+            done[best] += HOP
+        if ops[best]["kind"] == "dma":
+            free["L"] = max(done[best], free["L"]) + ops[best]["bytes"] / DBW
+            done[best] = free["L"] + DLAT
+        seq.append(best)
+        for u in users[best]:
+            left[u] -= 1
+            if not left[u]:
+                offer(u)
+    return seq, eng, start, done
+
+
+KEPT = {}
+
+
+def hand_on(g, core, home, T, topo):
+    e = HANDS[helpers(home, T.cores, topo).index(core)]
+    rid, pid, _se = topo.addr(home)
+    g.wait_ge(T.sem.zeros, len(topo.engines(home, core)))
+    mine = [j for j, x in fillers() if x == e]
+    for n, j in enumerate(mine):
+        g.remote_dma(T.tab[:, M + 1024 * j:M + 1024 * j + 1024], T.tab[:, ZEROS[1]:ZEROS[2]], T.sem["fill%s%d" % (e, n // LOT)], T.sem.sent,
+                     pid, rid, topo.mask(core, home))
+    g.wait_ge(T.sem.sent, len(mine) * len(topo.engines(core, home)))
 
 
 def rank_program(g, core, T, topo):
     rank = T.rank_of(core)
     if rank is None:
+        home = helped(core, T.cores, topo)
+        if home is not None:
+            hand_on(g, core, home, T, topo)
         return
     ops, groups = record(g, core, T, topo, rank)
-    seq, eng, _start, _done = order(ops, groups)
+    if "order" not in KEPT:
+        KEPT["order"] = order(ops, groups)
+    seq, eng, _start, _done = KEPT["order"]
     Q = {"v": g.vector, "s": g.scalar, "p": g.tensor, "g": g, "y": g.sync}
     count, mark, seen, sent = {e: 0 for e in "vspg"}, {}, {e: {} for e in Q}, 0
+    gave = sum(o["val"] for o in ops if o["sem"] == "gave")
     for i in seq:
         o, e = ops[i], eng[i]
         if o["kind"] == "recv":
@@ -680,12 +807,14 @@ def rank_program(g, core, T, topo):
             mark[i] = ("c" + e, count[e])
         elif o["kind"] == "dma":
             ins.then_inc(T.sem[o["sem"]], 16)
+        elif o["sem"]:
+            mark[i] = (o["sem"], gave)
         else:
             sent += o["val"]
     ends = {"c" + e: v for e, v in count.items()}
     ends.update({sem: 16 * len(m) for sem, m in groups.items()})
-    ends.update({o["sem"]: o["val"] for o in ops if o["kind"] == "recv"})
-    ends["sent"] = sent
+    ends.update({o["sem"]: o["val"] for o in ops if o["kind"] == "recv" and o["val"]})
+    ends["sent"], ends["gave"] = sent, gave
     for sem, v in ends.items():
         if not any(seen[e].get(sem, 0) >= v for e in Q):
             g.wait_ge(T.sem[sem], v)

from concourse.mybir import AluOpType, ActivationFunctionType

A = AluOpType
F = ActivationFunctionType
ST = 6
L, W, NV = 256, 4096, 1024
M = 128
BIG = 131072.0
BATCH = [[64, 64], [64, 64]]
PIECE = {}
FILL = {"v": 27, "s": 24, "g": 1, "a": 11}
LATE = {"v": 0.3, "a": 0.3, "b": 0.3}
HANDS = "a"
LOT = 2
TWICE = []
DIRECT = [1]
BACK = 4
ZEROS = ("tab", M + 1024 * 63, M + 1024 * 64)
SETS = [("B0", "B1", "B2"), ("B3", "B4", "B5")]
STATE = [("B7", "B2", "B0"), ("B3", "B5", "B6")]
HOME = ["B0", "B1", "B2", "B6"]
AWAY = ["B4", "B5", "B6", "B3"]
BF, F16, F32, I32, U16 = "bfloat16", "float16", "float32", "int32", "uint16"
MATS = ["IDN", "BDB", "PFB", "UP", "UN", "UPB", "LA3", "LA2", "LA1", "NLA", "QK", "QA", "QB", "BD0", "BD8", "gm",
        "MA", "NA", "MB", "NB", "M0", "M1", "M2", "MO", "NE6", "LV", "LV1", "LV2", "L31", "L32"]
NB_ = len(BATCH)


def sb(n, dt):
    return ("sbuf", [128, n], dt)


SCRATCH = {
    "tab": sb(16 * W + 2 * M + 16, BF), "gin": sb(1536, I32), "hl": sb(2 * W + M + 16, BF), "ex2": sb(W, BF), "G1": sb(W, BF),
    "G": sb(W, BF), "fa": sb(W, BF), "DIG": sb(W + 16, BF), "RF": sb(NV + 8, F32),
    "CN": sb(512, BF), "CNI": sb(1536, BF), "ZZ": sb(144, BF), "NE": sb(896, BF),
    "ci": sb(8, I32), "cf": sb(32, F32), "pw": sb(48, F32), "ID": sb(144, F32), "km": sb(144, BF),
    "CT": sb(144, BF), "C1": sb(144, BF), "CC": sb(144, BF),
    "ID32": sb(128, F32), "BD16": sb(128, F16), "NB16": sb(128, F16), "RS": sb(128, F32), "B16": sb(2 * L, F16),
    "ODK": sb(256, BF), "OD2": sb(256, BF), "OD3": sb(256, BF), "OD5": sb(256, BF), "c256": sb(64, BF),
    "S": sb(2 * L, BF), "SQ": sb(L, BF), "RO": sb(ST * 2 * L, U16), "RQ": sb(ST * 2 * L, U16),
    "PO": sb(ST * 8 * NB_, U16), "PI": sb(ST * 8 * NB_, U16), "O2": sb(L, U16), "TU": sb(L, U16), "TI": sb(L, U16),
    "vl": sb(16, U16), "fl": sb(32, U16), "of": sb(32, U16),
    "EF": sb(2 * L, F32), "KC": sb(L + 4, F32), "SC": sb(L, F32), "SD": sb(L, F32),
    "sg": sb(L, BF), "isf": sb(2 * L, BF), "GF": sb(2 * L, BF), "R1": sb(L, BF), "R2": sb(L, BF),
}
for _m in MATS:
    SCRATCH[_m] = sb(128, BF)
for _b in range(8):
    SCRATCH["B%d" % _b] = ("psum", [128, 512], F32)
NCH = sum(len(b) for b in BATCH)
SEMAPHORES = (["cv", "cs", "cp", "cg", "sent", "small", "drf", "dfa", "dig", "perm", "back", "outs", "out0"]
              + ["gl%d" % i for i in range(8)] + ["cn%d" % i for i in range(3)] + ["ti%d" % i for i in range(len(BATCH))]
              + ["rq%d_%d" % (t, c) for t in range(ST) for c in range(NCH)]
              + ["fill%s%d" % (e, i) for e in HANDS for i in range(-(-FILL[e] // LOT))] + ["cases", "zeros", "gave"] + ["rs%d_%d" % (t, h) for t in range(ST) for h in range(len(BATCH))])

CY, PCY = 1.04e-3, 0.52e-3
GA, SC = 1.25, 3.05
LOOK = 477.59
DELAY = 0.0
HOP, SYNC, SAME, DLAT, DBW = 2.1, 0.15, 0.15, 1.6, 210e3
ISSUE, ROW, RBW = 0.7, 0.04, 12e3
LIFT = {'zeros': 93.0, 'gloss': 51.9, 'digits': 12.3, 'small': 7.0, 'cases': 16.3, 'late': -50.9, 'wide0': -25.0, 'wide': -15.2, 'back': 13.1, 'a0': 3.9, 'v0': 1.0, 's0': -0.5, 'u0': -3.8, 'r0': -0.5, 't30': -8.3, 't20': 12.0, 'g30': 5.3, 'g20': -0.1, 't10': 13.2, 'g10': -7.7, 's1': -2.3, 'u1': 0.6, 'r1': 5.9, 'a1': 1.2, 't12': -2.9, 't13': -5.2, 'e0': -2.4, 'k0': -1.5, 'o0': -1.9, 'z0': 5.5, 'w0': -9.1, 't21': -3.5, 'n0': 1.9, 'g31': 1.5, 'n2': 5.8, 'g33': 4.5, 'x2': 6.9, 'n1': -0.3, 'x1': 1.4, 'k1': -1.3, 'f2': 3.2, 'f1': -6.1, 'g13': -5.1, 'g21': -5.1, 'v1': 4.5, 'g11': 0.9, 'e1': -1.2, 't33': -2.7, 't11': 6.4, 't22': 6.1, 'z1': -0.8, 'g22': -3.9, 't23': 3.6, 'g32': 6.0, 'n3': 5.0, 'g23': -6.9, 'x3': 1.7, 'x0': 5.5, 'g12': 8.7, 'p1': -4.4, 'p0': -3.8, 'o1': 3.1, 'b1': 8.6, 'h0': -1.6, 'q1': -2.6, 't31': 0.7, 'b0': 6.7, 'h1': 3.5, 't32': -0.6, 'f0': -1.0, 'q0': -6.9, 'f3': -1.9, 'w1': -6.4, 'W1': 16.3, 'H1': -20.0, 'S0': -7.7, 'Z1': -2.5, 'W0': -9.4, 'U1': 8.5, 'perm': -9.5, 'S1': 17.3, 'E0': -20.4, 'out': -9.4, 'state': -20.3, 'Z0': 2.8, 'U0': -4.7, 'const': -0.1, 'fill': -12.3, 'E1': -0.2, 'A0': 10.4, 'A1': 7.4, 'rest': 10.5, 'H0': 3.1}
WHO = {'v0': 'x', 'v1': 'x', 'h0': 'v', 'h1': 's', 's0': 'ssx', 's1': 'xss', 'u0': 's', 'u1': 'vs', 'r0': 's', 'x0': 's', 'x1': 's', 'x2': 'v', 'x3': 's', 'g12': 'xx', 'g13': 'ss', 'H0': 'x', 'H1': 's', 'S0': 'xxs', 'S1': 'xsx', 'U0': 's', 'U1': 'v', 'g30': 'sv', 'g20': 'xx', 'g10': 'sv', 'g11': 'xv', 'g33': 'xx', 'g32': 'xv', 'g22': 'sx', 'g31': 'vx', 'g21': 'vs', 'g23': 'sv'}
SIZE = {BF: 2, F16: 2, U16: 2, F32: 4, I32: 4}


def R(name, c0=0, c1=None, cs=1, p0=0, p1=128, ps=1):
    return (name, p0, p1, ps, c0, SCRATCH[name][1][1] if c1 is None else c1, cs)


def ind(win, off):
    return ("ind", win, off)


def width(a):
    return 16 * width(a[2]) if a[0] == "ind" else len(range(a[4], a[5], a[6]))


def meet(a, b, block):
    if a[3] == 1 and b[3] == 1:
        if a[2] <= b[1] or b[2] <= a[1]:
            return False
    elif not set(range(a[1], a[2], a[3])) & set(range(b[1], b[2], b[3])):
        return False
    if block:
        return a[4] // block <= (b[5] - 1) // block and b[4] // block <= (a[5] - 1) // block
    if a[5] <= b[4] or b[5] <= a[4]:
        return False
    return not (a[6] == b[6] and (a[4] - b[4]) % a[6])


def helpers(core, ranks, topo):
    return [c for c in topo.cores_of(core) if c not in ranks and topo.die(c) == topo.die(core)][:len(HANDS)]


def helped(core, ranks, topo):
    for c in ranks:
        if core in helpers(c, ranks, topo):
            return c
    return None


def fillers():
    due = sorted([((j + 1.0) / n * (1 - LATE.get(e, 0.0)) + LATE.get(e, 0.0), e) for e, n in FILL.items() for j in range(n)])
    pieces = [4 * a + 2 * u + w for u in range(2) for a in range(16) for w in range(2)]
    return [(j, e) for j, (_d, e) in zip(pieces[:-1], due)]


def record(g, core, T, topo, rank):
    n_ranks = len(T.cores)
    ops, seen, groups, tag, nth, step, hold = [], {}, {}, [None], {}, [-1], []

    def ap(a):
        if not isinstance(a, tuple):
            return a
        if a[0] == "ind":
            return ap(a[1]).indirect(ap(a[2]))
        return T[a[0]][slice(a[1], a[2], a[3] if a[3] > 1 else None), slice(a[4], a[5], a[6] if a[6] > 1 else None)]

    def add(cost, fn, r=(), w=(), kind="c", sem=None, val=0, after=(), nbytes=0):
        i, deps, acc = len(ops), {d: True for d in list(after) + hold}, []
        for lst, wr in ((r, False), (w, True)):
            for a in lst:
                if isinstance(a, tuple):
                    acc += [(a[1], wr), (a[2], False)] if a[0] == "ind" else [(a, wr)]
        for a, wr in acc:
            old = seen.setdefault(a[0], [])
            if SCRATCH[a[0]][0] == "psum":
                for _a, d, _w in old:
                    if d != i:
                        deps[d] = deps.get(d, False)
                seen[a[0]] = [(a, i, True)]
                continue
            for b, d, w2 in old:
                unlike = wr and w2 and d != i and (ops[d]["kind"] == "c") != (kind == "c")
                if d != i and (wr or w2) and meet(a, b, 16 // SIZE[SCRATCH[a[0]][2]] if unlike else 0):
                    deps[d] = True
            if wr and a[3] == 1 and a[6] == 1:
                old[:] = [x for x in old if x[1] == i or not (a[1] <= x[0][1] and x[0][2] <= a[2] and a[4] <= x[0][4] and x[0][5] <= a[5])]
            old.append((a, i, wr))
        ops.append({"cost": cost, "fn": fn, "deps": deps, "kind": kind, "sem": sem, "val": val, "bytes": nbytes,
                    "tag": tag[0].upper() if step[0] == ST - 1 and len(tag[0]) == 2 and tag[0][0] in "ahzwesu" else tag[0], "w": [a[0] for a, wr in acc if wr][:1], "nth": nth.get(tag[0], 0), "step": step[0]})
        nth[tag[0]] = nth.get(tag[0], 0) + (len(cost) > 1)
        if kind == "dma":
            groups.setdefault(sem, []).append(i)
        return i

    def narrow(*a):
        return all(SIZE[SCRATCH[x[0]][2]] == 2 for x in a)

    def vcost(out, *ins, rate=None):
        if out[0] == "ind":
            return 0.05 + width(out) * SC * CY
        if ins and ins[0][0] == "ind":
            return 0.05 + width(out) * GA * CY
        return max(64.0, width(out) * (rate or (0.5 if narrow(out, *ins) else 1.0))) * CY

    def scost(out, in_):
        return 0.065 + width(out) * GA * CY if in_[0] == "ind" else max(64.0, width(out)) * CY

    def only(cost, who):
        return cost if who == "x" else {who: cost[who]}

    def ts(out, in0, s1, s2=None, o0=A.add, o1=None):
        more = () if o1 is None else (o1,)
        return add({"v": vcost(out, in0)}, lambda e: g.vector.tensor_scalar(ap(out), ap(in0), ap(s1), ap(s2), o0, *more), [in0, s1, s2], [out])

    def tt(out, in0, in1, op):
        rate = 1.0 if "psum" in (SCRATCH[in1[0]][0], SCRATCH.get(in0[0], "-")[0]) else 2.0
        return add({"v": vcost(out, in0, rate=rate)}, lambda e: g.vector.tensor_tensor(ap(out), ap(in0), ap(in1), op), [in0, in1], [out])

    def cp(out, in_, who="v"):
        fn = lambda e: g.vector.tensor_copy(ap(out), ap(in_)) if e == "v" else g.scalar.activation(ap(out), ap(in_), F.Copy)
        return add(only({"v": vcost(out, in_), "s": scost(out, in_)}, who), fn, [in_], [out])

    def relu(out, in_, bias, who="x"):
        fn = lambda e: (g.vector.tensor_scalar(ap(out), ap(in_), ap(bias), 0.0, A.add, A.max) if e == "v"
                        else g.scalar.activation(ap(out), ap(in_), F.Relu, bias=ap(bias)))
        return add(only({"v": vcost(out, in_), "s": scost(out, in_)}, who), fn, [in_, bias], [out])

    def scan(out, d0, d1):
        return add({"v": vcost(out, rate=1.0)}, lambda e: g.vector.tensor_tensor_scan(ap(out), ap(d0), ap(d1), 0.0, A.max, A.min), [d0, d1], [out])

    def ms(out, c):
        return add({"v": vcost(out)}, lambda e: g.vector.memset(ap(out), c), (), [out])

    def io(out, pat, base, cm):
        kw = {} if SCRATCH[out[0]][2] == I32 else {"allow_small_or_imprecise_dtypes": True}
        return add({"g": 0.14 + 2 * width(out) * CY}, lambda e: g.iota(ap(out), pat, base, cm, **kw), (), [out])

    def aff(out, in_, pat, op, fill, base, cm):
        return add({"g": 0.18 + 2 * width(out) * CY}, lambda e: g.affine_select(ap(out), ap(in_), pat, op, fill, base, cm), [in_], [out])

    def mm(parts, first=True, final=True):
        def fn(e):
            ins = None
            for j, (o, lt, rh) in enumerate(parts):
                ins = g.tensor.matmul(ap(o), ap(lt), ap(rh), first and j == 0, final and j == len(parts) - 1)
            return ins
        cyc = sum(max(64, width(rh)) * (4 if SCRATCH[rh[0]][2] == F32 else 1) for o, lt, rh in parts)
        return add({"p": cyc * PCY}, fn, [x for p_ in parts for x in p_[1:]], [parts[0][0]])

    def dma(q, out, in_, sem, nbytes, after=()):
        eng = g.sync if q == "y" else g.scalar
        return add({q: 0.08}, lambda e: eng.dma_start(ap(out), ap(in_)), [in_], [out], kind="dma", sem=sem, nbytes=nbytes, after=after)

    def send(out, in_, peer, src, sem, after=()):
        dst = T.cores[peer]
        assert topo.may_write(core, dst)
        rid, pid, _se = topo.addr(dst)
        m = topo.mask(core, dst)
        i = add({"g": ISSUE}, lambda e: g.remote_dma(ap(out), ap(in_), T.sem[sem], T.sem.sent, pid, rid, m), [in_], (), kind="rem",
                val=len(topo.engines(core, dst)), after=after)
        add({"R": 16 * (ROW + 2 * width(out) / RBW)}, None, (), [out], kind="recv", sem=sem, val=len(topo.engines(T.cores[src], core)), after=[i])

    col = lambda j, p0=0, p1=128: R("cf", j, j + 1, 1, p0, p1)
    slide = lambda C, x: R(C, 15 - x, 143 - x)
    win = R("tab", M, M + 16 * W)
    EXP = [("ex2", 0), ("hl", W), ("ex2", 0), ("hl", 0), ("hl", W), ("ex2", 0)]
    batches, chunks, l0 = [], [], 0
    for b in BATCH:
        batches.append((l0, sum(b), list(range(len(chunks), len(chunks) + len(b)))))
        for n in b:
            chunks.append((l0, n))
            l0 += n

    def load_gloss(c):
        dma("y", R("gin", 512 * (c % 3), 512 * (c % 3) + 512), T.gloss[:, 512 * c:512 * c + 512], "gl%d" % c, 262144)

    tag[0] = "gloss"
    for c in range(3):
        load_gloss(c)

    tag[0] = "const"
    K, NK, NKB, X16, GB, GB15, WT, K1, PF, K4, SA1, SA2, EJ, B1, B2, B3, M0_, M1_, M2_, M3_, KB, C16 = range(22)
    p, ki = R("ci", 0, 1), R("ci", 1, 2)
    io(p, [[0, 1]], 0, 1)
    io(R("ID"), [[1, 144]], 0, 0)
    io(R("km"), [[0, 9], [1, 16]], 0, 0)
    io(R("gm"), [[16, 8], [0, 16]], 0, 0)
    ms(R("ZZ"), 0.0)
    ts(ki, p, 15, None, A.bitwise_and)
    ts(R("ci", 2, 3), p, 7, None, A.bitwise_and)
    ts(R("ci", 3, 4), p, 3, None, A.arith_shift_right)
    cp(col(K), ki)
    cp(col(PF), p)
    ts(col(GB), p, col(K), None, A.subtract)
    ts(col(GB15), p, col(K), 15.0, A.subtract, A.add)
    ts(col(WT), R("ci", 2, 3), 0.0, None, A.is_equal)
    ts(col(EJ), R("ci", 3, 4), -1.0, 12.0, A.mult, A.add)
    for c, mul, plus in ((NK, -1.0, 0.0), (NKB, -65536.0, -67584.0), (X16, 16.0, -1.0), (K1, 1.0, 1.0), (K4, 4096.0, 0.0)):
        ts(col(c), ki, mul, plus, A.mult, A.add)
    for c, k, v in ((M0_, 0, 1.0), (M1_, 1, 1.0), (M2_, 2, 64.0), (M3_, 3, 1.0)):
        ts(col(c), ki, float(k), v, A.is_equal, A.mult)
    ts(col(KB), ki, 1.0, -BIG, A.is_ge, A.mult)
    ts(R("IDN"), R("ID", 0, 128), col(PF), None, A.is_equal)
    ts(R("ID32"), R("ID", 0, 128), col(PF), None, A.is_equal)
    for C, w_ in (("CT", col(WT)), ("C1", col(K1))):
        ts(R(C), R("ID"), col(GB15), w_, A.is_equal, A.mult)
    ts(R("CC"), R("km"), 15.0, None, A.is_equal)
    io(col(C16), [[0, 1]], 1, 0)
    for C, w_ in (("BD16", 1.0), ("NB16", -1.0), ("BDB", BIG), ("PFB", col(KB)), ("BD8", 1.0)):
        ts(R(C), R("gm"), col(GB), w_, A.is_equal, A.mult)
    aff(R("BD0"), R("BD8"), [[1, 128]], A.is_ge, 0.0, 0, -1)
    aff(R("UP"), R("BD0"), [[1, 128]], A.not_equal, -1.0, 0, -1)
    ts(R("UN"), R("UP"), -1.0, None, A.mult)
    ts(R("UPB"), R("UP"), 65536.0, None, A.mult)
    ts(R("NE6"), R("km", 0, 128), col(K), 6 * BIG, A.not_equal, A.mult)
    ms(R("ODK", 128, 256), 32768.0)
    for C, o, d in (("ODK", 0, 2 * BIG + 32768), ("OD2", 0, 0.0), ("OD2", 128, BIG), ("OD3", 0, 32768.0), ("OD3", 128, 2 * BIG),
                    ("OD5", 0, 57344.0), ("OD5", 128, 61440.0)):
        ts(R(C, o, o + 128), R("NE6"), d)
    io(R("pw", 32, 40), [[16, 8]], 32769, 0)
    ms(R("RS"), -1.0)
    ts(R("RS", 0, 128, 16), R("pw", 32, 40), col(K))
    ms(R("KC", 0, 4), 60000.0)
    sizes = sorted(set(n for _l, n, _c in batches))
    for j, n in enumerate(sizes):
        io(R("c256", 16 * j, 16 * j + n // 8), [[0, 2], [256, n // 16]], 0, 0)

    def steps(c, top, lower):
        io(col(c), [[0, 1]], top, 0)
        for bound, v in lower:
            aff(col(c), col(c), [[0, 1]], A.is_ge, float(v), -bound, 1)

    def lead(name, src, f, v):
        aff(R(name), R(src, 0, 128), [[-1, 8], [0, 16]], A.not_equal, v, -8 * f, 1)

    def matrix(name, runs, wide=False):
        done = set()
        for i0, sl, j0, nj, v in runs + [(99, 0, 0, 16, 0.0)]:
            j = j0
            while j < j0 + nj:
                e = j
                while e < j0 + nj and (e in done) == (j in done):
                    e += 1
                if i0 != 99 or j not in done:
                    o = R(name, 8 * j, 8 * e)
                    u = 1 if wide else 8
                    aff(o, o if j in done else R("ZZ", 0, 8 * (e - j)), [[-u * sl, e - j], [-16 if wide else -1, 8]], A.not_equal, v,
                        -u * (i0 + sl * (j - j0)) - (999 if i0 == 99 else 0), 1)
                j = e
            done.update(range(j0, j0 + nj))

    steps(SA1, 7, [(88, 0)])
    steps(SA2, 1, [(88, 99)])
    for name, f in (("LA3", 10), ("LA2", 9), ("LA1", 8)):
        lead(name, "ZZ", f, 4096.0)
    lead("LV", "ZZ", 0, 1.0)
    lead("LV", "LV", 4, 16.0)
    lead("NLA", "ZZ", 8, -4096.0)
    lead("QK", "ZZ", 15, -BIG / 64)
    lead("QA", "NLA", 11, BIG)
    lead("QB", "LA1", 11, -BIG)
    ms(R("CN", L, 2 * L), 0.0)
    tag[0] = "zeros"
    ms(R(*ZEROS), 0.0)
    tag[0] = "const"
    o = ZEROS[1]
    aff(R("NE", 0, 896, 1, 0, 32), R("tab", o, o + 896, 1, 0, 32), [[1, 7], [0, 128]], A.not_equal, -1.0, 0, -1)

    def widen(t, name, who):
        (buf, o), s = EXP[t], t % 3
        tag[0] = name
        for k in range(16):
            out, in_ = R(buf, o + k, o + W, 16), R("CNI", 512 * s, 512 * s + L)
            if who == "g":
                aff(out, in_, [[0, L]], A.is_ge, 0.0, 0, 0)
            else:
                cp(out, in_, who)

    tag[0] = "digits"
    los = []
    for c in range(8):
        o, gs, bk = W * (c // 4) + 512 * (c % 4), R("gin", 512 * (c % 3), 512 * (c % 3) + 512), R("B%d" % (c % 4))
        cp(R("hl", o, o + 512), gs)
        mm([(bk, R("IDN"), R("hl", o, o + 512))])
        los.append(tt(R("hl", o + 2048, o + 2560), gs, bk, A.subtract))
        if c < 5:
            load_gloss(c + 3)
    tag[0] = "small"
    ri = lambda p0, p1, o=0: R("gin", NV + o, NV + o + L, 1, p0, p1)
    dma("s", R("CN", 0, L), T.cases[:], "cases", 65536)
    for p0, p1, o, src in ((0, 32, 0, T.vp0[:]), (32, 64, 0, T.vp0[:]), (64, 88, 0, T.act0[:]), (88, 96, 0, T.act0[0:8, :]),
                           (0, 6, L, T.need[:]), (6, 7, L, T.dep0[:])):
        dma("y", ri(p0, p1, o), src, "small", (p1 - p0) * 1024)
    tag[0] = "cases"
    cp(R("CN", L, 2 * L, 1, 0, 7), ri(0, 7, L))
    tag[0] = "state"
    ts(ri(0, 32), ri(0, 32), 15, None, A.bitwise_and)
    ts(ri(32, 64), ri(32, 64), 4, None, A.arith_shift_right)
    cp(R("S", 0, L, 1, 0, 64), ri(0, 64))
    acts = R("S", 0, L, 1, 64, 96)
    ts(acts, ri(64, 96), col(SA1, 64, 96), 0.0, A.subtract, A.max)
    ts(acts, acts, col(SA2, 64, 96), None, A.min)
    mm([(R("B7", 0, L), R("NE", 768, 896, 1, 0, 7), R("CN", L, 2 * L, 1, 0, 7))])
    ts(R("S", 0, L, 1, 96, 128), R("B7", 0, L, 1, 96, 128), col(EJ, 96, 128), 64.0, A.is_equal, A.mult)
    tag[0] = "rest"
    dma("y", R("gin", 0, NV), T.refs[:], "drf", 524288)
    cp(R("RF", 0, NV), R("gin", 0, NV))
    cp(R("RF", NV, NV + 8), R("gin", 0, 8))
    tag[0] = "fill"
    ms(R("tab", 0, M), 0.0)
    ms(R("tab", M + 16 * W, 2 * M + 16 * W + 16), 0.0)
    ms(R("hl", 2 * W, 2 * W + M + 16), 0.0)
    turn = [2 * a + u for u in range(2) for a in range(16)]
    zeros = R(*ZEROS)
    gave, tag[0] = [], "zeros"
    for h in helpers(core, T.cores, topo):
        rid, pid, _se = topo.addr(h)
        gave.append(add({"g": ISSUE + (0.0 if gave else 2.0)}, (lambda rid, pid, m: lambda e: g.remote_dma(ap(zeros), ap(zeros), T.sem.zeros, T.sem.gave, pid, rid, m))(
            rid, pid, topo.mask(core, h)), [zeros], (), kind="rem", sem="gave", val=len(topo.engines(core, h))))
        gave[-1] = add({"H%d" % len(gave): 3.5}, None, kind="recv", sem="none", after=gave[-1:])
    handed, tag[0] = {}, "fill"
    for j, e in fillers():
        o = R("tab", M + 1024 * j, M + 1024 * j + 1024)
        if e in HANDS:
            h = HANDS.index(e)
            n = handed.get(e, 0)
            handed[e] = n + 1
            i = add({"H%d" % (h + 1): 1.3}, None, (), [o], kind="recv", sem="fill%s%d" % (e, n // LOT), after=[gave[h]],
                    val=len(topo.engines(helpers(core, T.cores, topo)[h], core)) * min(LOT, FILL[e] - n // LOT * LOT))
            groups.setdefault(ops[i]["sem"], []).append(i)
        elif e == "v":
            ms(o, 0.0)
        elif e == "s":
            cp(o, zeros, "s")
        else:
            aff(o, zeros, [[0, 1024]], A.is_ge, 0.0, 0, 0)
    tag[0] = "perm"
    for j in turn:
        perm = dma("y", R("tab", M + 2048 * j, M + 2048 * j + 2048, 1, 0, 128, 8), R("hl", W * (j % 2), W * (j % 2) + W, 1, j // 2, 128, 16),
                   "perm", 65536, [los[4]])
    dma("y", R("fa"), T.facts[:], "dfa", 1048576, [perm])
    tag[0] = "cases"

    def cases(s, after):
        send(R("CNI", 512 * s, 512 * s + 512), R("CN"), (rank + 1 + s) % n_ranks, (rank - 1 - s) % n_ranks, "cn%d" % s, after)

    cases(0, [los[7]])
    widen(0, "wide0", "s")

    tag[0] = "late"
    ms(R("pw", 16, 32), 0.5)
    add({"v": 64 * CY}, lambda e: g.vector.tensor_tensor_scan(ap(R("pw", 0, 16)), ap(R("pw", 16, 32)), ap(R("pw", 16, 32)), 65536.0, A.mult, A.max),
        [R("pw", 16, 32)], [R("pw", 0, 16)])
    ts(R("pw", 16, 32), R("pw", 0, 16), col(M1_), None, A.mult)
    ts(R("DIG", 16, 32), R("ID", 0, 16), col(M0_), col(M2_), A.mult, A.add)
    ts(R("DIG", 24, 32), R("DIG", 24, 32), col(M3_))
    for i in range(6):
        ts(R("DIG", 16 + (16 << i), 16 + (32 << i)), R("DIG", 16, 16 + (16 << i)), R("pw", 31 - i, 32 - i))
    ms(R("DIG", 0, 16), 0.0)

    steps(B1, -192, [(104, -64), (96, -192), (40, -64), (32, -191), (8, -65)])
    steps(B2, 64, [(120, -64), (96, -128), (64, -64), (32, -65)])
    steps(B3, 0, [(8, 1)])
    matrix("MA", [(0, 1, 0, 12, -1.0), (0, 0, 1, 3, 1.0), (4, 0, 5, 3, 1.0), (15, 0, 0, 1, -2.0), (15, 0, 4, 1, -2.0), (15, 0, 12, 1, -2.0),
                  (12, 1, 1, 3, 2.0), (12, 1, 5, 3, 2.0), (12, 1, 8, 3, 2.0), (12, 1, 13, 3, 2.0), (12, 0, 11, 1, 2.0)])
    matrix("NA", [(2, 0, 0, 16, 2.0), (0, 0, 0, 1, 1.0), (0, 0, 8, 3, 1.0), (1, 0, 4, 1, 1.0), (3, 0, 11, 1, 1.0)], True)
    matrix("MB", [(1, 1, 1, 11, 1.0), (0, 0, 1, 3, -1.0), (4, 0, 5, 3, -1.0), (13, 1, 1, 3, 2.0), (13, 1, 5, 3, 2.0), (13, 1, 8, 3, 2.0),
                  (13, 1, 12, 3, 2.0), (13, 0, 11, 1, 2.0), (12, 0, 15, 1, -2.0)])
    matrix("NB", [(2, 0, 0, 16, -2.0)], True)
    matrix("M0", [(0, 1, 0, 13, 1.0), (15, 0, 15, 1, 1.0)])
    matrix("M1", [(0, 1, 0, 12, 1.0), (13, 1, 13, 3, 1.0), (13, 1, 1, 3, -1.0), (13, 1, 5, 3, -1.0), (13, 1, 8, 3, -1.0), (13, 0, 11, 2, -1.0),
                  (12, 0, 0, 1, -1.0), (12, 0, 4, 1, -1.0)])
    matrix("M2", [(8, 1, 8, 4, -1.0), (12, 1, 12, 3, 1.0), (14, 0, 15, 1, -1.0), (15, 0, 0, 1, -1.0), (15, 0, 4, 1, -1.0)]
           + [(j, 0, 0, 1, 1.0) for j in (1, 2, 3)] + [(j, 0, 4, 1, 1.0) for j in (5, 6, 7)])

    for name, src, rows in (("LV1", "LV", [(12, -17.0)]), ("L31", "LA3", [(15, -4096.0)]), ("L32", "ZZ", [(10, -4096.0)]),
                            ("LV2", "ZZ", [(15, -17.0)] + [(j, 1.0 if j < 4 else 16.0) for j in (1, 2, 3, 5, 6, 7)])):
        for f, v in rows:
            lead(name, src, f, v)
            src = name

    bank = [0]

    def level(lv, offs, o0, buf, c, first, out):
        tag[0] = "g%d%d" % (lv, c)
        l0, nl = chunks[c]
        n = 16 * nl // PIECE.get(tag[0], 2)
        for u in range(0, 16 * nl, n):
            cp(R(buf, 16 * l0 + u, 16 * l0 + u + n), ind(win, R(offs, o0 + u // 16, o0 + (u + n) // 16)), "x")
        tag[0] = "t%d%d" % (lv, c)
        ps = R(AWAY[c % len(AWAY)] if lv == 1 else HOME[bank[0] % len(HOME)], 0, nl)
        bank[0] = 0 if lv == 1 else bank[0] + 1
        mm([(ps,) + x for x in first] + [(ps, slide("CT", x), R(buf, 16 * l0 + x, 16 * (l0 + nl), 16)) for x in range(16)])
        cp(out, ps)
        return ps

    def verses(b, parts):
        l0, nl, _c = batches[b]
        ps = R(STATE[b][0], 384, 384 + nl)
        mm([(ps, R("IDN"), R("NE6", 0, nl))] + [(ps,) + x for x in parts])
        return ps

    def refs(t, b, ps, plus):
        l0, nl, _c = batches[b]
        tag[0] = "q%d" % b
        St, vl, row = R("S", L * (t % 2) + l0, L * (t % 2) + l0 + nl), R("vl", l0 // 16, (l0 + nl) // 16), R("SC", l0, l0 + nl)
        o = 2 * (L * t + l0) + (0 if l0 else nl)
        cp(R("RO", o, o + nl), St)
        tag[0] = "r%d" % b
        ts(vl, R("SC", l0 + 15, l0 + nl, 16), plus)
        if b in DIRECT:
            tt(row, ind(R("RF"), vl), R("sg", l0, l0 + nl), A.add)
            cp(R("O2", l0, l0 + nl), row)
            return
        cp(row, ind(R("RF"), vl), "x")
        ps = R(STATE[b][2], 0, nl)
        mm([(ps, R("LA3"), St), (ps, R("ID32"), row)])
        cp(R("O2", l0, l0 + nl), ps)

    def third(b, parts):
        l0, nl, _c = batches[b]
        if b in DIRECT:
            mm([(R(STATE[b][2], 0, nl),) + x for x in parts])
            cp(R("sg", l0, l0 + nl), R(STATE[b][2], 0, nl), "x")

    for b, (b0, nb, _c) in enumerate(batches):
        ps = verses(b, [(R("LV"), R("S", b0, b0 + nb))])
        scan(R("SC", b0, b0 + nb), R("RS", 0, nb), ps)
        third(b, [(R("LA3"), R("S", b0, b0 + nb))])
        refs(0, b, ps, 0.0)

    for t in range(ST):
        s = t % 3
        peer, asker = (rank + 1 + s) % n_ranks, (rank - 1 - s) % n_ranks
        last = t == ST - 1
        nth.clear()
        step[0] = t
        lanes = lambda name, l0, nl, o=0: R(name, o + l0, o + l0 + nl)
        if t == ST - 2:
            tag[0] = "wide"
            hold.append(len(ops) - 1)
            for name, i, v in (("BD0", 0, 1.0), ("BD8", 8, 1.0), ("gm", 0, -1.0), ("km", 8, -1.0)):
                aff(R(name, 0, 128), R("ZZ", 0, 128), [[-16, 8], [0, 16]], A.not_equal, v, -i, 1)
            matrix("MO", [(0, 1, 0, 4, 1.0), (4, 1, 0, 4, 16.0), (8, 1, 4, 3, 1.0)] + [(12 + j, 0, 8, 1, j / 64.0) for j in (1, 2, 3)])
            hold.clear()
        asks = []
        for c in range(len(chunks) + 1):
            if c < len(chunks):
                l0, nl = chunks[c]
                level(3, "O2", l0, "G", c, [(R("LA2"), lanes("S", l0, nl, L * (t % 2)))], lanes("O2", l0, nl))
            if c > 0:
                l0, nl = chunks[c - 1]
                b0, nb = [x[:2] for x in batches if c - 1 in x[2]][0]
                o = 2 * L * t + b0 + l0 + (nb if b0 else 0)
                level(2, "O2", l0, "G", c - 1, [(R("LA1"), lanes("S", l0, nl, L * (t % 2)))], R("RO", o, o + nl))
                u = o + nl + (nb if l0 + nl == nb else 0)
                o -= nb if l0 == b0 > 0 else 0
                send(R("RQ", o, u), R("RO", o, u), peer, asker, "rq%d_%d" % (t, c - 1))
                asks.append(len(ops) - 1)
        asked = asks[-2]
        tag[0] = "back"
        for i in range(1, 4 if t == 0 else 0):
            dma("y", R("DIG", 16 + NV * i, 16 + NV * i + NV), R("DIG", 16, 16 + NV), "dig", 262144, [asked])
        if t < 2:
            cases(t + 1, [asked])
        if last:
            for a in range(16):
                dma("y", R("hl", 0, 2 * W, 1, a, 128, 16), R("tab", M + W * a, M + W * a + W, 1, 0, 128, 8), "back", 131072,
                    asks[-2:-1] if a >= BACK else [])
        ebuf, eo = EXP[t]
        for b0, nb, cs in batches:
            for c in cs:
                l0, nl = chunks[c]
                ps = level(1, "RQ", 2 * L * t + b0 + l0 + (nb if b0 else 0), "G1", c, [], lanes("TU", l0, nl))
                tag[0] = "x%d" % c
                relu(lanes("EF", l0, nl, b0 + nb), ps, col(C16))
                cp(lanes("EF", l0, nl, b0), lanes("RQ", l0, nl, 2 * L * t + b0 + (nb if b0 else 0)))
        for b, (b0, nb, cs) in enumerate(batches):
            X, Y, Z = SETS[b % 2]
            if last:
                send(lanes("TI", b0, nb), lanes("TU", b0, nb), asker, peer, "ti%d" % b)
            for c in cs:
                tag[0] = "f%d" % c
                l0, nl = chunks[c]
                n = 16 * nl // PIECE.get(tag[0], 1)
                for u in range(16 * l0, 16 * (l0 + nl), n):
                    tt(R("G", u, u + n), ind(R("fa"), R("TU", u // 16, (u + n) // 16)), R(ebuf, eo + u, eo + u + n), A.is_le)
                tag[0] = "n%d" % c
                ps = R(X, l0 - b0, l0 - b0 + nl)
                nd = 512 * s + L + l0
                mm([(ps, R("NE", 128 * t, 128 * t + 128, 1, 0, 7), R("CNI", nd, nd + nl, 1, 0, 7))]
                   + [(ps, slide("CC", x), R("G", 16 * l0 + x, 16 * (l0 + nl), 16)) for x in range(16)])
            tag[0] = "p%d" % b
            nh = nb // 16
            sg, es, sq, kr = lanes("sg", b0, nb), lanes("EF", b0, nb, b0), lanes("SQ", b0, nb), lanes("O2", b0, nb)
            tsel, both = lanes("EF", b0, nb, b0 + nb), R("EF", 2 * b0, 2 * b0 + 2 * nb)
            b16, t16 = lanes("B16", b0, nb, b0), lanes("B16", b0, nb, b0 + nb)
            cp(sq, lanes("RQ", b0, nb, 2 * L * t + b0 + (0 if b0 else nb)))
            isf, ish = R("isf", 2 * b0, 2 * b0 + nb), R("isf", 2 * b0 + nb, 2 * b0 + 2 * nb)
            gf, gh = R("GF", 2 * b0, 2 * b0 + nb), R("GF", 2 * b0 + nb, 2 * b0 + 2 * nb)
            mm([(R(Z, 0, 2 * nb), R("ID32"), both), (R(Z, 0, nb), R("NLA"), sq)], True, False)
            mm([(R(Y, 0, 256), R("IDN"), R("ODK")), (R(Y, 0, nb), R("QK"), sq)], True, False)
            tag[0] = "v%d" % b
            add({"s": scost(sg, sg)}, (lambda o, i_: lambda e: g.scalar.activation(ap(o), ap(i_), F.Sign, bias=0.5))(sg, R(X, 0, nb)),
                [R(X, 0, nb)], [sg])
            mm([(R(Z, 0, nb), R("UPB"), sg), (R(Z, nb, 2 * nb), R("UPB"), sg)], False, True)
            mm([(R(X, 0, nb), R("UP"), sg)])
            mm([(R(X, nb, 2 * nb), R("UN"), sg)])
            ts(R("B16", 2 * b0, 2 * b0 + 2 * nb), R(Z, 0, 2 * nb), col(NKB), -2048.0, A.add, A.max)
            relu(R("isf", 2 * b0, 2 * b0 + 2 * nb), R(X, 0, 2 * nb), col(NK))
            mm([(R(Y, 128, 128 + nb), R("BD16"), b16), (R(Y, 0, nb), R("BD16"), b16), (R(Y, 0, nb), R("PFB"), isf), (R(Y, 0, nb), R("PFB"), ish)],
               False, True)
            tag[0] = "a%d" % b
            po = 8 * (NB_ * t + b)
            ps = R(Z, 0, nb)
            mm([(ps, R("IDN"), R("OD3", 0, nb)), (ps, R("BD16"), t16)])
            scan(tsel, R("RS", 0, nb), ps)
            ts(R("PO", po, po + nh), R("EF", 2 * b0 + nb + 15, 2 * b0 + 2 * nb, 16), 15.0)
            send(R("PI", po, po + nh), R("PO", po, po + nh), asker, peer, "rs%d_%d" % (t, b))
            tag[0] = "b%d" % b
            za, zb = R(Z, 0, nb), R(Z, 128, 128 + nb)
            gate = lambda z: [(z, R("QK"), sq), (z, R("PFB"), isf), (z, R("PFB"), ish)]
            more = [(z, R("IDN"), R("OD3", 128, 128 + nb)) for z in (za, zb)] + gate(za) + gate(zb) if b in TWICE else []
            mm([(R(Z, 0, 256), R("IDN"), R("OD5" if last else "OD2"))] + ([] if last else [(za, R("QA"), sq), (zb, R("QB"), sq)])
               + [(za, R("BD16" if last else "NB16"), b16), (zb, R("BD16"), b16)] + more, True, b not in TWICE)
            tag[0] = "o%d" % b
            if b not in TWICE:
                scan(lanes("SC", b0, nb), R("RS", 0, nb), za)
                scan(lanes("SD", b0, nb), R("RS", 0, nb), zb)
            tag[0] = "h%d" % b
            j, u = 16 * sizes.index(nb), 0 if last else 1
            ps, fl = R(X, 0, (2 - u) * nh), R("fl", b0 // 8, b0 // 8 + (2 - u) * nh)
            mm([(ps, R("IDN"), R("c256", j, j + (2 - u) * nh))]
               + [(ps, slide("C1", x), R("isf", 2 * b0 + u * nb + x, 2 * b0 + 2 * nb, 16)) for x in range(16)])
            ts(fl, ps, col(X16))
            cp(R("GF", 2 * b0 + u * nb, 2 * b0 + 2 * nb), ind(R("G1", 16 * b0, 16 * (b0 + nb)), fl), "x")
            tag[0] = "k%d" % b
            cp(kr, R(Y, 128, 128 + nb))
            scan(R("KC", 1 + b0, 1 + b0 + nb), R("RS", 0, nb), R(Y, 0, nb))
            o, parts = 16 * b0, []
            tt(R("G", o, o + nb), R("KC", b0, b0 + nb), R(Y, 128, 128 + nb), A.is_equal)
            into = [(Z, 0), (Z, 128)] if b in TWICE else [(Y, 0)]
            if b not in TWICE:
                parts += [(R(Y, 0, nb), R("IDN"), R("OD3", 128, 128 + nb))] + gate(R(Y, 0, nb))
            parts += [(R(bk, z, z + nb), R("BDB"), R("G", o, o + nb)) for bk, z in into]
            o += nb
            blocks = list(range((b0 + nb) // 16 - 1))
            begun, tag[0] = False, "e%d" % b
            for c in blocks:
                lo = max(0, 16 * (c + 1) - b0)
                ts(R("G", o, o + nb - lo), R("O2", b0 + lo, b0 + nb), R("KC", 16 * c + 16, 16 * c + 17), None, A.is_equal)
                parts += [(R(bk, z + lo, z + nb), R("BDB"), R("G", o, o + nb - lo)) for bk, z in into]
                o += nb - lo
                if len(parts) >= 4 * len(into) or c == blocks[-1]:
                    mm(parts, not begun and b not in TWICE, c == blocks[-1])
                    parts, begun = [], True
            tag[0] = "z%d" % b
            oa, ob = R("of", b0 // 8, b0 // 8 + nh), R("of", b0 // 8 + nh, b0 // 8 + 2 * nh)
            sa, sd = R("SC", b0 + 15, b0 + nb, 16), R("SD", b0 + 15, b0 + nb, 16)
            if b in TWICE:
                scan(lanes("SC", b0, nb), R("RS", 0, nb), za)
                scan(lanes("SD", b0, nb), R("RS", 0, nb), zb)
            else:
                scan(es, R("RS", 0, nb), R(Y, 0, nb))
                for x in (sa, sd):
                    tt(x, x, R("EF", 2 * b0 + 15, 2 * b0 + nb, 16), A.max)
            if not last:
                ts(oa, sa, -1.0, float(32768 + M), A.mult, A.add)
                cp(ob, sd)
                tag[0] = "w%d" % b
                cp(ind(R("tab", 0, M + 8 * W), oa), gh)
                cp(ind(R("tab", M + 8 * W, 2 * M + 16 * W + 16), ob), gh)
            else:
                ts(oa, sa, -24576.0)
                ts(ob, sd, -28672.0)
                tag[0] = "w%d" % b
                mm([(R(Y, 0, nb), R("LA1"), sq)])
                mm([(R(Y, 128, 128 + nb), R("BD0"), gh), (R(Y, 128, 128 + nb), R("gm"), gf)])
                mm([(R(Y, 256, 256 + nb), R("BD8"), gh), (R(Y, 256, 256 + nb), R("km", 0, 128), gf)])
                ts(sg, R(Y, 0, nb), col(K4), None, A.is_equal)
                for u, (of, dl, new) in enumerate(((oa, lanes("SC", b0, nb), isf), (ob, lanes("SD", b0, nb), ish))):
                    wn = R("hl", W * u, 2 * W + M + 16)
                    tt(dl, sg, R(Y, 128 + 128 * u, 128 + 128 * u + nb), A.mult)
                    tt(new, ind(wn, of), dl, A.add)
                    cp(ind(wn, of), new)
        if t < min(3, ST - 1):
            hold.append(asked)
            widen(t + 1, "wide", "g")
            hold.clear()
        for b, (b0, nb, cs) in enumerate(batches):
            tag[0] = "s%d" % b
            po = 8 * (NB_ * t + b)
            St, Sn, D = lanes("S", b0, nb, L * (t % 2)), lanes("S", b0, nb, L * (1 - t % 2)), lanes("sg", b0, nb)
            r1, r2 = lanes("R1", b0, nb), lanes("R2", b0, nb)
            cp(D, ind(R("DIG"), R("PI", po, po + nb // 16)), "x")
            pa, pb = R(STATE[b][0], 0, nb), R(STATE[b][1], 128, 128 + nb)
            mm([(pa, R("MA"), St), (pa, R("NA"), D)])
            mm([(pb, R("MB"), St), (pb, R("NB"), D)])
            relu(r1, pa, col(B1))
            relu(r2, pb, col(B2))
            ps, tag[0] = R(STATE[b][1], 256, 256 + nb), "u%d" % b
            if not last:
                pv = verses(b, [(R("LV"), St), (R("LV1"), r1), (R("LV2"), r2)])
                scan(lanes("SC", b0, nb), R("RS", 0, nb), pv)
                third(b, [(R("LA3"), St), (R("L31"), r1), (R("L32"), r2)])
            mm([(ps, R("M0"), St), (ps, R("M1"), r1), (ps, R("M2"), r2)])
            relu(Sn, ps, col(B3))
            if not last:
                refs(t + 1, b, pv, 1.0)
            else:
                ln, q = slice(b0, b0 + nb), "out0" if b + 1 < len(batches) else "outs"
                ps, y, z = R(STATE[b][2], 0, nb), lanes("SC", b0, nb), lanes("SD", b0, nb)
                mm([(ps, R("MO"), Sn)])
                ts(y, ps, float(NV), -float(NV), A.is_ge, A.mult)
                tt(z, y, ps, A.add)
                dma("y", T.yvp[:, ln], R("SD", b0, b0 + nb, 1, 0, 32), q, 128 * nb)
                dma("s", T.yact[:, ln], R("SD", b0, b0 + nb, 1, 32, 56), q, 96 * nb)
                dma("y", T.ydep[:, ln], R("SD", b0, b0 + nb, 1, 64, 65), q, 4 * nb)

    tag[0] = "out"
    for b0, nb, _c in batches:
        cp(lanes("RF", b0, nb), lanes("TI", b0, nb))
    dma("y", T.yt[:], R("RF", 0, L), "out0", 131072)
    mm([(R("B0", 0, L), R("IDN"), R("hl", L * m, L * m + L)) for m in range(32)])
    cp(R("RF", L, 2 * L), R("B0", 0, L), "x")
    dma("s", T.yg[:], R("RF", L, 2 * L), "outs", 131072)
    return ops, groups


def order(ops, groups):
    n = len(ops)
    deps = []
    for i, o in enumerate(ops):
        d = set()
        for j in o["deps"]:
            d.update(groups.get(ops[j]["sem"], [j]))
        assert i not in d
        deps.append(d)
    users = [[] for _ in range(n)]
    for i in range(n):
        for j in deps[i]:
            users[j].append(i)
    left = [len(d) for d in deps]
    seq, cnt = [i for i in range(n) if left[i] == 0], list(left)
    for i in seq:
        for u in users[i]:
            cnt[u] -= 1
            if cnt[u] == 0:
                seq.append(u)
    assert len(seq) == n
    prio = [0.0] * n
    for i in reversed(seq):
        c = min(ops[i]["cost"].values()) + {"dma": DLAT + ops[i]["bytes"] / DBW, "recv": HOP}.get(ops[i]["kind"], SYNC)
        prio[i] = c + max([prio[u] for u in users[i]], default=0.0)

    prio = [prio[i] + LIFT.get(ops[i]["tag"], 0.0) for i in range(n)]
    eng, start, done, seq = [None] * n, [0.0] * n, [0.0] * n, []
    free = {e: 0.0 for e in ["H1", "H2"] + list("vspgyLR")}
    ready = {e: {} for e in free}

    def offer(i):
        o = ops[i]
        who = WHO.get(o["tag"], "x")
        for e, c in o["cost"].items():
            if len(o["cost"]) == 1 or who[o["nth"] % len(who)] in ("x", e):
                ready[e][i] = (max([done[j] + (SYNC if eng[j] != e else SAME if o["deps"].get(j, True) else 0.0) for j in deps[i]],
                                   default=0.0), c)

    for i in range(n):
        if not left[i]:
            offer(i)
    while len(seq) < n:
        e, now, soon = None, 1e18, 1e18
        for q, cd in ready.items():
            if cd:
                t = max(min(cd.values())[0], free[q])
                u = t + (DELAY if q in "vs" else 0.0)
                if u < soon or (u == soon and q == "s"):
                    e, now, soon = q, t, u
        best, top = None, None
        for i, (at, c) in ready[e].items():
            if at <= now + 1e-9 and (top is None or prio[i] > top):
                best, top = i, prio[i]
        first = best
        for i, (at, c) in ready[e].items():
            if now < at < now + ready[e][first][1] and prio[i] - LOOK * (at - now) > top and prio[i] > prio[first] + 0.3:
                best, top = i, prio[i] - LOOK * (at - now)
        at, c = ready[e][best]
        for q in ops[best]["cost"]:
            ready[q].pop(best, None)
        eng[best], start[best] = e, max(at, now)
        free[e] = done[best] = start[best] + c
        if ops[best]["kind"] == "recv":
            done[best] += HOP
        if ops[best]["kind"] == "dma":
            free["L"] = max(done[best], free["L"]) + ops[best]["bytes"] / DBW
            done[best] = free["L"] + DLAT
        seq.append(best)
        for u in users[best]:
            left[u] -= 1
            if not left[u]:
                offer(u)
    return seq, eng, start, done


KEPT = {}


def hand_on(g, core, home, T, topo):
    e = HANDS[helpers(home, T.cores, topo).index(core)]
    rid, pid, _se = topo.addr(home)
    g.wait_ge(T.sem.zeros, len(topo.engines(home, core)))
    mine = [j for j, x in fillers() if x == e]
    for n, j in enumerate(mine):
        g.remote_dma(T.tab[:, M + 1024 * j:M + 1024 * j + 1024], T.tab[:, ZEROS[1]:ZEROS[2]], T.sem["fill%s%d" % (e, n // LOT)], T.sem.sent,
                     pid, rid, topo.mask(core, home))
    g.wait_ge(T.sem.sent, len(mine) * len(topo.engines(core, home)))


def rank_program(g, core, T, topo):
    rank = T.rank_of(core)
    if rank is None:
        home = helped(core, T.cores, topo)
        if home is not None:
            hand_on(g, core, home, T, topo)
        return
    ops, groups = record(g, core, T, topo, rank)
    if "order" not in KEPT:
        KEPT["order"] = order(ops, groups)
    seq, eng, _start, _done = KEPT["order"]
    Q = {"v": g.vector, "s": g.scalar, "p": g.tensor, "g": g, "y": g.sync}
    count, mark, seen, sent = {e: 0 for e in "vspg"}, {}, {e: {} for e in Q}, 0
    gave = sum(o["val"] for o in ops if o["sem"] == "gave")
    for i in seq:
        o, e = ops[i], eng[i]
        if o["kind"] == "recv":
            mark[i] = (o["sem"], o["val"])
            continue
        need = {}
        for d, hard in o["deps"].items():
            if ops[d]["kind"] == "c" and eng[d] == e and not hard:
                continue
            sem, v = mark[d] if ops[d]["kind"] != "dma" else (ops[d]["sem"], 16 * len(groups[ops[d]["sem"]]))
            need[sem] = max(need.get(sem, 0), v)
        for sem, v in need.items():
            if seen[e].get(sem, 0) < v:
                Q[e].wait_ge(T.sem[sem], v)
                seen[e][sem] = v
        ins = o["fn"](e)
        if o["kind"] == "c":
            count[e] += 1
            ins.then_inc(T.sem["c" + e], 1)
            mark[i] = ("c" + e, count[e])
        elif o["kind"] == "dma":
            ins.then_inc(T.sem[o["sem"]], 16)
        elif o["sem"]:
            mark[i] = (o["sem"], gave)
        else:
            sent += o["val"]
    ends = {"c" + e: v for e, v in count.items()}
    ends.update({sem: 16 * len(m) for sem, m in groups.items()})
    ends.update({o["sem"]: o["val"] for o in ops if o["kind"] == "recv" and o["val"]})
    ends["sent"], ends["gave"] = sent, gave
    for sem, v in ends.items():
        if not any(seen[e].get(sem, 0) >= v for e in Q):
            g.wait_ge(T.sem[sem], v)
